import numpy as np
import ml_dtypes


def mxq(x, axis, fmt="e4m3"):
    dtype, down = {"e4m3": (ml_dtypes.float8_e4m3fn, 7), "e5m2": (ml_dtypes.float8_e5m2, 14)}[fmt]
    v = np.moveaxis(np.asarray(x, np.float32).astype(ml_dtypes.bfloat16).astype(np.float64), axis, -1)
    blocks = v.reshape(v.shape[:-1] + (-1, 32))
    amax = np.abs(blocks).max(-1, keepdims=True)
    byte = np.maximum(np.where(amax > 0, np.frexp(amax)[1] - 1 + 127, 0) - down, 1)
    scale = np.exp2(byte - 127.0)
    codes = (blocks / scale).astype(np.float32).astype(dtype).astype(np.float64)
    return np.moveaxis((codes * scale).reshape(v.shape), -1, axis)


WIDE = False


def mx_kscale(k, group=512):
    if not WIDE:
        return np.ones(k)
    levels = np.array([10, -10, 5, -5, 0])
    if group != 512:
        return np.exp2(np.random.permutation(np.resize(levels, k // group))).repeat(group)
    if k % 512:
        return np.exp2(np.random.permutation(np.resize(levels, k // 32))).repeat(32)
    a = np.empty((k // 512, 16))
    for p in range(k // 512):
        a[p, :8] = np.random.permutation(np.resize(levels, 8))
        for g in range(8):
            far = levels[np.abs(levels - a[p, g]) >= 10]
            a[p, g + 8] = far[np.random.randint(len(far))]
    return np.exp2(a.ravel()).repeat(32)


def f64(x):
    return np.asarray(x).astype(np.float64)


def bf(x):
    return np.asarray(x, np.float32).astype(ml_dtypes.bfloat16)


def planes(Y):
    r, m = Y.shape
    b = f64(bf(Y)).reshape(r // 32, 32, m)
    amax = np.abs(b).max(1)
    byte = np.clip(np.where(amax > 0, np.frexp(amax)[1] - 1 + 127 - 7, 1), 1, 254)
    codes = (b * np.exp2(127.0 - byte)[:, None, :]).reshape(r, m).astype(np.float32).astype(ml_dtypes.float8_e4m3fn).view(np.uint8)
    words = codes.reshape(r // 512, 128, 4, m).transpose(0, 1, 3, 2)
    return np.ascontiguousarray(words), np.ascontiguousarray(byte.astype(np.uint8).reshape(r // 512, 16, m))


G, D, M, N, K = 2, 256, 256, 512, 256


def sgn(shape):
    return np.random.uniform(0.5, 2.0, shape) * np.where(np.random.standard_normal(shape) < 0, -1.0, 1.0)


def setup_inputs():
    n = np.random.standard_normal
    s_d = mx_kscale(D, 0)
    s_m = mx_kscale(M, 0)
    return {
        "h": (n((G, D, N)) * s_d[:, None]).astype(np.float32),
        "w1": (n((G, D, M)) / np.sqrt(D) / s_d[:, None]).astype(np.float32),
        "x1": (n((G, M, N))).astype(np.float32),
        "a1": (sgn((G, M, 1)) * s_m[:, None]).astype(np.float32),
        "w2": (n((G, M, K)) / np.sqrt(M) / s_m[:, None]).astype(np.float32),
        "x2": (n((G, K, N))).astype(np.float32),
    }


def reference(h, w1, x1, a1, w2, x2):
    w1q = mxq(f64(w1), 1, "e4m3")
    hq = mxq(f64(h), 1, "e4m3")
    z1 = w1q.transpose(0, 2, 1) @ hq
    h1 = np.tanh(z1 + f64(x1)) * f64(a1)
    w2q = mxq(f64(w2), 1, "e4m3")
    h1q = mxq(h1, 1, "e4m3")
    z2 = w2q.transpose(0, 2, 1) @ h1q
    y = np.tanh(z2 + f64(x2))
    Y = y.reshape(G * K, N)
    words, scales = planes(Y)
    return Y, words, scales

@@ -1,0 +1,246 @@
+from contextlib import ExitStack
+
+import concourse.mybir as mybir
+
+G, D, N = 2, 256, 512
+FLOPS = 2 * 2 * G * D * D * N
+
+F32 = mybir.dt.float32
+BF16 = mybir.dt.bfloat16
+I32 = mybir.dt.int32
+U8 = mybir.dt.uint8
+FP8X4 = mybir.dt.float8_e4m3fn_x4
+TANH = mybir.ActivationFunctionType.Tanh
+ADD = mybir.AluOpType.add
+MULT = mybir.AluOpType.mult
+
+P = 128
+R = 64
+PACK = 4
+CH = 128
+HALF = 256
+SW = CH // 4
+
+
+def tile_rows_pl_steps_tanh_kernel(tc, h, w1, x1, a1, w2, x2, out_0, out_1, out_2):
+    nc = tc.nc
+    rows = [slice(0, R), slice(R, P)]
+    chunks = [(g, c) for c in range(2) for g in range(G)]
+
+    with ExitStack() as ctx:
+        sb = ctx.enter_context(tc.tile_pool(name="sb", bufs=1))
+        ps = ctx.enter_context(tc.psum_pool(name="ps", bufs=1))
+        ctx.enter_context(tc.manual_schedule())
+        queue = [nc.sync, nc.scalar]
+
+        def load_natural(name, src, width):
+            raw = sb.tile([P, PACK, width], F32, name=name)
+            view = src.rearrange("g (p j) w -> (g p) j w", j=PACK)
+            for s in range(2):
+                queue[s].dma_start(out=raw[:, 2 * s : 2 * s + 2, :], in_=view[:, 2 * s : 2 * s + 2, :])
+            return raw
+
+        def load_halves(name, src, g):
+            t = sb.tile([P, PACK, HALF], F32, name=name)
+            view = src[g].rearrange("(p j) n -> p j n", j=PACK)
+            for s in range(2):
+                queue[s].dma_start(out=t[rows[s], :, :], in_=view[:, :, s * HALF : (s + 1) * HALF])
+            return t
+
+        w1_raw = load_natural("w1_raw", w1, D)
+        h_raw = load_natural("h_raw", h, N)
+        x1_sb = [load_halves("x1_%d" % g, x1, g) for g in range(G)]
+
+        a_sb = sb.tile([P, G, 8], F32, name="a_sb")
+        for s in range(2):
+            queue[s].dma_start(out=a_sb[rows[s], :, 0:PACK], in_=a1.rearrange("g (p j) o -> p g (j o)", j=PACK))
+
+        warm = sb.tile([P, 8], F32, name="warm")
+        nc.vector.memset(warm[:], 0.0)
+        warm_out = sb.tile([P, 8], F32, name="warm_out")
+        nc.scalar.activation(out=warm_out[:], in_=warm[:], func=TANH)
+
+        w2_raw = load_natural("w2_raw", w2, D)
+
+        w_codes, w_scales = [], []
+        for i in range(2):
+            codes = sb.tile([P, 9 * R], I32, name="w_codes%d" % i, align_bytes=64)
+            scales = sb.tile([P, 9 * R], U8, name="w_scales%d" % i, align_bytes=64)
+            nc.vector.memset(codes[:], 0)
+            nc.vector.memset(scales[:].bitcast(I32), 0)
+            w_codes.append(codes)
+            w_scales.append(scales)
+        state = []
+        for q in range(4):
+            t = sb.tile([P, CH + SW], I32, name="state%d" % q, align_bytes=64)
+            nc.vector.memset(t[:, CH:], 0)
+            state.append(t)
+
+        def deal_weights(copy, name, raw):
+            wb = sb.tile([P, PACK, R, PACK], BF16, name=name, align_bytes=64)
+            copy(out=wb[:].rearrange("p x m j -> p m j x"), in_=raw[:].rearrange("p j (m x) -> p m j x", x=PACK))
+            return wb
+
+        def quantize_weights(i, wb):
+            for x in range(PACK):
+                cols = slice((2 * x + 1) * R, (2 * x + 2) * R)
+                nc.vector.quantize_mx(
+                    out=w_codes[i][:, cols].bitcast(FP8X4),
+                    scales=w_scales[i][:, cols],
+                    in_=wb[:, x, :, :].rearrange("p m j -> p (m j)"),
+                )
+
+        def interleave(copy, dst, src):
+            copy(out=dst.rearrange("p (c i) t -> p c t i", i=4), in_=src.rearrange("p t (c i) -> p c t i", i=4))
+
+        w1b = deal_weights(nc.vector.tensor_copy, "w1b", w1_raw)
+        quantize_weights(0, w1b)
+
+        x2_sb = [load_halves("x2_0", x2, 0)]
+
+        hb, h_q = {}, {}
+        for k, copy in ((0, nc.vector.tensor_copy), (1, nc.scalar.copy), (2, nc.vector.tensor_copy), (3, nc.scalar.copy)):
+            hb[k] = sb.tile([P, CH, PACK], BF16, name="hb%d" % k, align_bytes=64)
+            interleave(copy, hb[k][:], h_raw[:, :, k * CH : (k + 1) * CH])
+        x2_sb.append(load_halves("x2_1", x2, 1))
+
+        def quantize(t, src):
+            nc.vector.quantize_mx(
+                out=t[:, 0:CH].bitcast(FP8X4), scales=t[:, CH:].bitcast(U8), in_=src[:].rearrange("p n t -> p (n t)")
+            )
+
+        for k in (0, 2, 1, 3):
+            h_q[k] = sb.tile([P, CH + SW], I32, name="hq%d" % k, align_bytes=64)
+            quantize(h_q[k], hb[k])
+
+        def product(name, i, g, lower, upper):
+            bank = ps.tile([P, PACK, CH], F32, name=name)
+            for x in range(PACK):
+                for s, moving in enumerate((lower, upper)):
+                    first = (2 * x + 1 - s) * R
+                    cols = slice(first, first + P)
+                    nc.tensor.matmul_mx(
+                        out=bank[:, x, :],
+                        lhsT=w_codes[i][rows[g], cols].bitcast(FP8X4),
+                        lhsT_scale=w_scales[i][rows[g], cols],
+                        rhs=moving[rows[g], 0:CH].bitcast(FP8X4),
+                        rhs_scale=moving[rows[g], CH:].bitcast(U8),
+                        start=(s == 0),
+                        stop=(s == 1),
+                    )
+            return bank
+
+        z1 = [product("z1_%d" % q, 0, g, h_q[c], h_q[2 + c]) for q, (g, c) in enumerate(chunks)]
+
+        def add(name, bank, x_tile, c):
+            s = sb.tile([P, PACK, CH], F32, name=name)
+            nc.vector.tensor_tensor(out=s[:], in0=bank[:], in1=x_tile[:, :, c * CH : (c + 1) * CH], op=ADD)
+            return s
+
+        sum1, t1, h1b, moved = {}, {}, {}, {}
+
+        def add1(q):
+            g, c = chunks[q]
+            sum1[q] = add("sum1_%d" % q, z1[q], x1_sb[g], c)
+            t1[q] = sb.tile([P, CH, PACK], F32, name="t1_%d" % q)
+            nc.scalar.activation(
+                out=t1[q][:].rearrange("p (c i) t -> p c t i", i=2),
+                in_=sum1[q][:].rearrange("p t (c i) -> p c t i", i=2),
+                func=TANH,
+            )
+
+        def scale1(q):
+            g = chunks[q][0]
+            h1b[q] = sb.tile([P, CH, PACK], BF16, name="h1b%d" % q, align_bytes=64)
+            nc.vector.tensor_tensor(
+                out=h1b[q][:], in0=t1[q][:], in1=a_sb[:, g, 0:PACK].unsqueeze(1).to_broadcast([P, CH, PACK]), op=MULT
+            )
+
+        def quant1(q):
+            g = chunks[q][0]
+            quantize(state[q], h1b[q])
+            moved[q] = sb.tile([P, CH + SW], I32, name="moved%d" % q, align_bytes=64)
+            nc.sync.dma_start(out=moved[q][rows[g], :], in_=state[q][rows[1 - g], :])
+
+        add1(0)
+        add1(1)
+        scale1(0)
+        add1(2)
+        quant1(0)
+        scale1(1)
+        add1(3)
+        quant1(1)
+        w2b = deal_weights(nc.scalar.copy, "w2b", w2_raw)
+        scale1(2)
+        scale1(3)
+        quant1(2)
+        quant1(3)
+        quantize_weights(1, w2b)
+
+        z2 = []
+        for q, (g, c) in enumerate(chunks):
+            pair = (state[q], moved[q]) if g == 0 else (moved[q], state[q])
+            z2.append(product("z2_%d" % q, 1, g, pair[0], pair[1]))
+
+        y_view = out_0.rearrange("(g p u) n -> g p u n", g=G, u=PACK)
+        words_view = out_1[0].rearrange("p n t -> p (n t)").bitcast(I32)
+        scales_view = out_2[0].bitcast(I32).rearrange("(g q r) (s c) -> s q r g c", g=G, q=2, s=2)
+        words = [sb.tile([P, HALF], I32, name="words%d" % g, align_bytes=64) for g in range(G)]
+        y_scales = sb.tile([P, G * HALF], U8, name="y_scales", align_bytes=64)
+        y, yb = {}, {}
+
+        def add2(q):
+            g, c = chunks[q]
+            s = add("sum2_%d" % q, z2[q], x2_sb[g], c)
+            y[q] = sb.tile([P, PACK, CH], F32, name="y%d" % q)
+            nc.scalar.activation(out=y[q][:], in_=s[:], func=TANH)
+
+        def store_y(q, s):
+            g, c = chunks[q]
+            first = s * HALF + c * CH
+            queue[s].dma_start(out=y_view[g][:, :, first : first + CH], in_=y[q][rows[s], :, :])
+
+        def round2(q):
+            yb[q] = sb.tile([P, CH, PACK], BF16, name="yb%d" % q, align_bytes=64)
+            interleave(nc.vector.tensor_copy, yb[q][:], y[q][:])
+
+        def quant2(q):
+            g, c = chunks[q]
+            first = g * HALF + c * CH
+            nc.vector.quantize_mx(
+                out=words[g][:, c * CH : (c + 1) * CH].bitcast(FP8X4),
+                scales=y_scales[:, first : first + CH],
+                in_=yb[q][:].rearrange("p n t -> p (n t)"),
+            )
+
+        def store_words(g):
+            for s in range(2):
+                queue[s].dma_start(out=words_view[rows[g], s * HALF : (s + 1) * HALF], in_=words[g][rows[s], :])
+
+        add2(0)
+        store_y(0, 0)
+        add2(1)
+        store_y(0, 1)
+        store_y(1, 0)
+        round2(0)
+        add2(2)
+        store_y(1, 1)
+        store_y(2, 0)
+        quant2(0)
+        round2(1)
+        add2(3)
+        store_y(2, 1)
+        store_y(3, 0)
+        store_y(3, 1)
+        quant2(1)
+        round2(2)
+        round2(3)
+        quant2(2)
+        store_words(0)
+        quant2(3)
+        store_words(1)
+        scale_words = y_scales[:].bitcast(I32).rearrange("p (g c) -> p g c", g=G)
+        for q in range(2):
+            for s in range(2):
+                first = R * s + 32 * q
+                queue[s].dma_start(out=scales_view[s, q], in_=scale_words[first : first + 4, :, :])

@@ -33,154 +33,133 @@ def tile_rows_pl_steps_tanh_kernel(tc, h, w1, x1, a1, w2, x2, out_0, out_1, out_
         ctx.enter_context(tc.manual_schedule())
         queue = [nc.sync, nc.scalar]
 
-        def load_natural(name, src, width):
+        def load_rows(name, src, first, width):
             raw = sb.tile([P, PACK, width], F32, name=name)
             view = src.rearrange("g (p j) w -> (g p) j w", j=PACK)
-            for s in range(2):
-                queue[s].dma_start(out=raw[:, 2 * s : 2 * s + 2, :], in_=view[:, 2 * s : 2 * s + 2, :])
+            nc.sync.dma_start(out=raw[:], in_=view[:, :, first : first + width])
             return raw
 
-        def load_halves(name, src, g):
-            t = sb.tile([P, PACK, HALF], F32, name=name)
-            view = src[g].rearrange("(p j) n -> p j n", j=PACK)
-            for s in range(2):
-                queue[s].dma_start(out=t[rows[s], :, :], in_=view[:, :, s * HALF : (s + 1) * HALF])
-            return t
+        x2_sb = [sb.tile([P, PACK, HALF], F32, name="x2_%d" % g) for g in range(G)]
 
-        w1_raw = load_natural("w1_raw", w1, D)
-        h_raw = load_natural("h_raw", h, N)
-        x1_sb = [load_halves("x1_%d" % g, x1, g) for g in range(G)]
+        def load_x2(g, s):
+            view = x2[g].rearrange("(p j) n -> p j n", j=PACK)
+            queue[s].dma_start(out=x2_sb[g][rows[s], :, :], in_=view[:, :, s * HALF : (s + 1) * HALF])
 
-        a_sb = sb.tile([P, G, 8], F32, name="a_sb")
+        w1_raw = load_rows("w1_raw", w1, 0, D)
+        a_sb = sb.tile([P, PACK], F32, name="a_sb")
+        nc.scalar.dma_start(out=a_sb[:], in_=a1.rearrange("g (p j) o -> (g p) (j o)", j=PACK))
+        h_raw, x1_sb = [], []
         for s in range(2):
-            queue[s].dma_start(out=a_sb[rows[s], :, 0:PACK], in_=a1.rearrange("g (p j) o -> p g (j o)", j=PACK))
+            h_raw.append(load_rows("h_raw%d" % s, h, s * HALF, HALF))
+            x1_sb.append(load_rows("x1_%d" % s, x1, s * HALF, HALF))
+        w2_raw = load_rows("w2_raw", w2, 0, D)
+        load_x2(0, 0)
+        load_x2(1, 0)
 
         warm = sb.tile([P, 8], F32, name="warm")
         nc.vector.memset(warm[:], 0.0)
         warm_out = sb.tile([P, 8], F32, name="warm_out")
         nc.scalar.activation(out=warm_out[:], in_=warm[:], func=TANH)
 
-        w2_raw = load_natural("w2_raw", w2, D)
-
         w_codes, w_scales = [], []
-        for i in range(2):
-            codes = sb.tile([P, 9 * R], I32, name="w_codes%d" % i, align_bytes=64)
-            scales = sb.tile([P, 9 * R], U8, name="w_scales%d" % i, align_bytes=64)
+        for i, blocks in enumerate((6, 9)):
+            codes = sb.tile([P, blocks * R], I32, name="w_codes%d" % i, align_bytes=64)
+            scales = sb.tile([P, blocks * R], U8, name="w_scales%d" % i, align_bytes=64)
             nc.vector.memset(codes[:], 0)
             nc.vector.memset(scales[:].bitcast(I32), 0)
             w_codes.append(codes)
             w_scales.append(scales)
-        state = []
-        for q in range(4):
-            t = sb.tile([P, CH + SW], I32, name="state%d" % q, align_bytes=64)
-            nc.vector.memset(t[:, CH:], 0)
-            state.append(t)
 
         def deal_weights(copy, name, raw):
             wb = sb.tile([P, PACK, R, PACK], BF16, name=name, align_bytes=64)
             copy(out=wb[:].rearrange("p x m j -> p m j x"), in_=raw[:].rearrange("p j (m x) -> p m j x", x=PACK))
             return wb
 
-        def quantize_weights(i, wb):
+        def quantize_w2(wb):
             for x in range(PACK):
                 cols = slice((2 * x + 1) * R, (2 * x + 2) * R)
                 nc.vector.quantize_mx(
-                    out=w_codes[i][:, cols].bitcast(FP8X4),
-                    scales=w_scales[i][:, cols],
+                    out=w_codes[1][:, cols].bitcast(FP8X4),
+                    scales=w_scales[1][:, cols],
                     in_=wb[:, x, :, :].rearrange("p m j -> p (m j)"),
                 )
 
         def interleave(copy, dst, src):
             copy(out=dst.rearrange("p (c i) t -> p c t i", i=4), in_=src.rearrange("p t (c i) -> p c t i", i=4))
 
-        w1b = deal_weights(nc.vector.tensor_copy, "w1b", w1_raw)
-        quantize_weights(0, w1b)
-
-        x2_sb = [load_halves("x2_0", x2, 0)]
-
-        hb, h_q = {}, {}
-        for k, copy in ((0, nc.vector.tensor_copy), (1, nc.scalar.copy), (2, nc.vector.tensor_copy), (3, nc.scalar.copy)):
-            hb[k] = sb.tile([P, CH, PACK], BF16, name="hb%d" % k, align_bytes=64)
-            interleave(copy, hb[k][:], h_raw[:, :, k * CH : (k + 1) * CH])
-        x2_sb.append(load_halves("x2_1", x2, 1))
-
-        def quantize(t, src):
+        def quantize(name, src):
+            t = sb.tile([P, CH + SW], I32, name=name, align_bytes=64)
             nc.vector.quantize_mx(
                 out=t[:, 0:CH].bitcast(FP8X4), scales=t[:, CH:].bitcast(U8), in_=src[:].rearrange("p n t -> p (n t)")
             )
+            return t
 
-        for k in (0, 2, 1, 3):
-            h_q[k] = sb.tile([P, CH + SW], I32, name="hq%d" % k, align_bytes=64)
-            quantize(h_q[k], hb[k])
+        def matmul(bank, i, g, first, moving, start, stop):
+            cols = slice(first, first + P)
+            nc.tensor.matmul_mx(
+                out=bank,
+                lhsT=w_codes[i][rows[g], cols].bitcast(FP8X4),
+                lhsT_scale=w_scales[i][rows[g], cols],
+                rhs=moving[rows[g], 0:CH].bitcast(FP8X4),
+                rhs_scale=moving[rows[g], CH:].bitcast(U8),
+                start=start,
+                stop=stop,
+            )
 
-        def product(name, i, g, lower, upper):
-            bank = ps.tile([P, PACK, CH], F32, name=name)
+        hb, z1, sum1, t1, h1b, state = {}, {}, {}, {}, {}, {}
+
+        def round_h(k, copy):
+            hb[k] = sb.tile([P, CH, PACK], BF16, name="hb%d" % k, align_bytes=64)
+            interleave(copy, hb[k][:], h_raw[k // 2][:, :, (k % 2) * CH : (k % 2 + 1) * CH])
+
+        def product1(k):
+            hq = quantize("hq%d" % k, hb[k])
+            z1[k] = [ps.tile([P, PACK, CH], F32, name="z1_%d_%d" % (k, g), tag="bank%d_%d" % (g, k)) for g in range(G)]
             for x in range(PACK):
-                for s, moving in enumerate((lower, upper)):
-                    first = (2 * x + 1 - s) * R
-                    cols = slice(first, first + P)
-                    nc.tensor.matmul_mx(
-                        out=bank[:, x, :],
-                        lhsT=w_codes[i][rows[g], cols].bitcast(FP8X4),
-                        lhsT_scale=w_scales[i][rows[g], cols],
-                        rhs=moving[rows[g], 0:CH].bitcast(FP8X4),
-                        rhs_scale=moving[rows[g], CH:].bitcast(U8),
-                        start=(s == 0),
-                        stop=(s == 1),
-                    )
-            return bank
+                for g in range(G):
+                    matmul(z1[k][g][:, x, :], 0, g, (x + 1 - g) * R, hq, True, True)
 
-        z1 = [product("z1_%d" % q, 0, g, h_q[c], h_q[2 + c]) for q, (g, c) in enumerate(chunks)]
+        def add1(k):
+            sum1[k] = sb.tile([P, PACK, CH], F32, name="sum1_%d" % k)
+            for g in range(G):
+                nc.vector.tensor_tensor(
+                    out=sum1[k][rows[g], :, :],
+                    in0=z1[k][g][rows[g], :, :],
+                    in1=x1_sb[k // 2][rows[g], :, (k % 2) * CH : (k % 2 + 1) * CH],
+                    op=ADD,
+                )
+
+        def tanh1(k):
+            t1[k] = sb.tile([P, CH, PACK], F32, name="t1_%d" % k)
+            nc.scalar.activation(
+                out=t1[k][:].rearrange("p (c i) t -> p c t i", i=2),
+                in_=sum1[k][:].rearrange("p t (c i) -> p c t i", i=2),
+                func=TANH,
+            )
+
+        def scale1(k):
+            h1b[k] = sb.tile([P, CH, PACK], BF16, name="h1b%d" % k, align_bytes=64)
+            nc.vector.tensor_tensor(
+                out=h1b[k][:], in0=t1[k][:], in1=a_sb[:].unsqueeze(1).to_broadcast([P, CH, PACK]), op=MULT
+            )
+
+        def quant1(k):
+            state[k] = quantize("state%d" % k, h1b[k])
+
+        z2 = {}
+
+        def product2(c):
+            for g in range(G):
+                z2[2 * c + g] = ps.tile([P, PACK, CH], F32, name="z2_%d_%d" % (c, g), tag="bank%d_%d" % (g, c))
+            for x in range(PACK):
+                for s in range(2):
+                    for g in range(G):
+                        matmul(z2[2 * c + g][:, x, :], 1, g, (2 * x + 1 - s) * R, state[2 * s + c], s == 0, s == 1)
 
         def add(name, bank, x_tile, c):
             s = sb.tile([P, PACK, CH], F32, name=name)
             nc.vector.tensor_tensor(out=s[:], in0=bank[:], in1=x_tile[:, :, c * CH : (c + 1) * CH], op=ADD)
             return s
-
-        sum1, t1, h1b, moved = {}, {}, {}, {}
-
-        def add1(q):
-            g, c = chunks[q]
-            sum1[q] = add("sum1_%d" % q, z1[q], x1_sb[g], c)
-            t1[q] = sb.tile([P, CH, PACK], F32, name="t1_%d" % q)
-            nc.scalar.activation(
-                out=t1[q][:].rearrange("p (c i) t -> p c t i", i=2),
-                in_=sum1[q][:].rearrange("p t (c i) -> p c t i", i=2),
-                func=TANH,
-            )
-
-        def scale1(q):
-            g = chunks[q][0]
-            h1b[q] = sb.tile([P, CH, PACK], BF16, name="h1b%d" % q, align_bytes=64)
-            nc.vector.tensor_tensor(
-                out=h1b[q][:], in0=t1[q][:], in1=a_sb[:, g, 0:PACK].unsqueeze(1).to_broadcast([P, CH, PACK]), op=MULT
-            )
-
-        def quant1(q):
-            g = chunks[q][0]
-            quantize(state[q], h1b[q])
-            moved[q] = sb.tile([P, CH + SW], I32, name="moved%d" % q, align_bytes=64)
-            nc.sync.dma_start(out=moved[q][rows[g], :], in_=state[q][rows[1 - g], :])
-
-        add1(0)
-        add1(1)
-        scale1(0)
-        add1(2)
-        quant1(0)
-        scale1(1)
-        add1(3)
-        quant1(1)
-        w2b = deal_weights(nc.scalar.copy, "w2b", w2_raw)
-        scale1(2)
-        scale1(3)
-        quant1(2)
-        quant1(3)
-        quantize_weights(1, w2b)
-
-        z2 = []
-        for q, (g, c) in enumerate(chunks):
-            pair = (state[q], moved[q]) if g == 0 else (moved[q], state[q])
-            z2.append(product("z2_%d" % q, 1, g, pair[0], pair[1]))
 
         y_view = out_0.rearrange("(g p u) n -> g p u n", g=G, u=PACK)
         words_view = out_1[0].rearrange("p n t -> p (n t)").bitcast(I32)
@@ -217,22 +196,58 @@ def tile_rows_pl_steps_tanh_kernel(tc, h, w1, x1, a1, w2, x2, out_0, out_1, out_
             for s in range(2):
                 queue[s].dma_start(out=words_view[rows[g], s * HALF : (s + 1) * HALF], in_=words[g][rows[s], :])
 
+        w1b = deal_weights(nc.vector.tensor_copy, "w1b", w1_raw)
+        nc.vector.quantize_mx(
+            out=w_codes[0][:, R : 5 * R].bitcast(FP8X4),
+            scales=w_scales[0][:, R : 5 * R],
+            in_=w1b[:].rearrange("p x m j -> p (x m j)"),
+        )
+        round_h(0, nc.vector.tensor_copy)
+        round_h(1, nc.scalar.copy)
+        product1(0)
+        product1(1)
+        add1(0)
+        round_h(2, nc.scalar.copy)
+        tanh1(0)
+        add1(1)
+        round_h(3, nc.scalar.copy)
+        tanh1(1)
+        load_x2(0, 1)
+        load_x2(1, 1)
+        product1(2)
+        scale1(0)
+        product1(3)
+        quant1(0)
+        scale1(1)
+        add1(2)
+        w2b = deal_weights(nc.scalar.copy, "w2b", w2_raw)
+        tanh1(2)
+        quant1(1)
+        quantize_w2(w2b)
+        scale1(2)
+        quant1(2)
+        product2(0)
+        add1(3)
+        tanh1(3)
         add2(0)
         store_y(0, 0)
+        scale1(3)
         add2(1)
         store_y(0, 1)
         store_y(1, 0)
+        quant1(3)
+        product2(1)
         round2(0)
-        add2(2)
-        store_y(1, 1)
-        store_y(2, 0)
-        quant2(0)
         round2(1)
+        store_y(1, 1)
+        quant2(0)
+        quant2(1)
+        add2(2)
+        store_y(2, 0)
         add2(3)
         store_y(2, 1)
         store_y(3, 0)
         store_y(3, 1)
-        quant2(1)
         round2(2)
         round2(3)
         quant2(2)

@@ -25,13 +25,13 @@ SW = CH // 4
 def tile_rows_pl_steps_tanh_kernel(tc, h, w1, x1, a1, w2, x2, out_0, out_1, out_2):
     nc = tc.nc
     rows = [slice(0, R), slice(R, P)]
-    chunks = [(g, c) for c in range(2) for g in range(G)]
 
     with ExitStack() as ctx:
         sb = ctx.enter_context(tc.tile_pool(name="sb", bufs=1))
         ps = ctx.enter_context(tc.psum_pool(name="ps", bufs=1))
         ctx.enter_context(tc.manual_schedule())
         queue = [nc.sync, nc.scalar]
+        V, S, GP = nc.vector, nc.scalar, nc.gpsimd
 
         def load_rows(name, src, first, width):
             raw = sb.tile([P, PACK, width], F32, name=name)
@@ -39,22 +39,18 @@ def tile_rows_pl_steps_tanh_kernel(tc, h, w1, x1, a1, w2, x2, out_0, out_1, out_
             nc.sync.dma_start(out=raw[:], in_=view[:, :, first : first + width])
             return raw
 
-        x2_sb = [sb.tile([P, PACK, HALF], F32, name="x2_%d" % g) for g in range(G)]
-
-        def load_x2(g, s):
-            view = x2[g].rearrange("(p j) n -> p j n", j=PACK)
-            queue[s].dma_start(out=x2_sb[g][rows[s], :, :], in_=view[:, :, s * HALF : (s + 1) * HALF])
-
         w1_raw = load_rows("w1_raw", w1, 0, D)
         a_sb = sb.tile([P, PACK], F32, name="a_sb")
         nc.scalar.dma_start(out=a_sb[:], in_=a1.rearrange("g (p j) o -> (g p) (j o)", j=PACK))
-        h_raw, x1_sb = [], []
+        h_raw, x_sb = [], [[], []]
         for s in range(2):
-            h_raw.append(load_rows("h_raw%d" % s, h, s * HALF, HALF))
-            x1_sb.append(load_rows("x1_%d" % s, x1, s * HALF, HALF))
+            for dst, src, name in ((h_raw, h, "h_%d" % s), (x_sb[0], x1, "x1_%d" % s)):
+                half = load_rows(name, src, s * HALF, HALF)
+                dst.extend([half[:, :, 0:CH], half[:, :, CH:]])
         w2_raw = load_rows("w2_raw", w2, 0, D)
-        load_x2(0, 0)
-        load_x2(1, 0)
+        for s in range(2):
+            half = load_rows("x2_%d" % s, x2, s * HALF, HALF)
+            x_sb[1].extend([half[:, :, 0:CH], half[:, :, CH:]])
 
         warm = sb.tile([P, 8], F32, name="warm")
         nc.vector.memset(warm[:], 0.0)
@@ -62,200 +58,205 @@ def tile_rows_pl_steps_tanh_kernel(tc, h, w1, x1, a1, w2, x2, out_0, out_1, out_
         nc.scalar.activation(out=warm_out[:], in_=warm[:], func=TANH)
 
         w_codes, w_scales = [], []
-        for i, blocks in enumerate((6, 9)):
-            codes = sb.tile([P, blocks * R], I32, name="w_codes%d" % i, align_bytes=64)
-            scales = sb.tile([P, blocks * R], U8, name="w_scales%d" % i, align_bytes=64)
+        for i in range(2):
+            codes = sb.tile([P, 6 * R], I32, name="w_codes%d" % i, align_bytes=64)
+            scales = sb.tile([P, 6 * R], U8, name="w_scales%d" % i, align_bytes=64)
             nc.vector.memset(codes[:], 0)
             nc.vector.memset(scales[:].bitcast(I32), 0)
             w_codes.append(codes)
             w_scales.append(scales)
 
-        def deal_weights(copy, name, raw):
-            wb = sb.tile([P, PACK, R, PACK], BF16, name=name, align_bytes=64)
-            copy(out=wb[:].rearrange("p x m j -> p m j x"), in_=raw[:].rearrange("p j (m x) -> p m j x", x=PACK))
-            return wb
+        def copy(eng, out, in_):
+            if eng is S:
+                nc.scalar.copy(out=out, in_=in_)
+            elif eng is V:
+                nc.vector.tensor_copy(out=out, in_=in_)
+            else:
+                nc.gpsimd.tensor_scalar(out=out, in0=in_, scalar1=1.0, scalar2=0.0, op0=MULT, op1=ADD)
 
-        def quantize_w2(wb):
-            for x in range(PACK):
-                cols = slice((2 * x + 1) * R, (2 * x + 2) * R)
-                nc.vector.quantize_mx(
-                    out=w_codes[1][:, cols].bitcast(FP8X4),
-                    scales=w_scales[1][:, cols],
-                    in_=wb[:, x, :, :].rearrange("p m j -> p (m j)"),
-                )
+        wb = {}
 
-        def interleave(copy, dst, src):
-            copy(out=dst.rearrange("p (c i) t -> p c t i", i=4), in_=src.rearrange("p t (c i) -> p c t i", i=4))
+        for i in range(2):
+            wb[i] = sb.tile([P, PACK, R, PACK], BF16, name="wb%d" % i, align_bytes=64)
 
-        def quantize(name, src):
-            t = sb.tile([P, CH + SW], I32, name=name, align_bytes=64)
+        def deal(i, eng, first=0, last=R):
+            raw = (w1_raw, w2_raw)[i]
+            copy(
+                eng,
+                wb[i][:, :, first:last, :].rearrange("p x m j -> p m j x"),
+                raw[:, :, PACK * first : PACK * last].rearrange("p j (m x) -> p m j x", x=PACK),
+            )
+
+        def quant_w(i):
             nc.vector.quantize_mx(
-                out=t[:, 0:CH].bitcast(FP8X4), scales=t[:, CH:].bitcast(U8), in_=src[:].rearrange("p n t -> p (n t)")
-            )
-            return t
-
-        def matmul(bank, i, g, first, moving, start, stop):
-            cols = slice(first, first + P)
-            nc.tensor.matmul_mx(
-                out=bank,
-                lhsT=w_codes[i][rows[g], cols].bitcast(FP8X4),
-                lhsT_scale=w_scales[i][rows[g], cols],
-                rhs=moving[rows[g], 0:CH].bitcast(FP8X4),
-                rhs_scale=moving[rows[g], CH:].bitcast(U8),
-                start=start,
-                stop=stop,
+                out=w_codes[i][:, R : 5 * R].bitcast(FP8X4),
+                scales=w_scales[i][:, R : 5 * R],
+                in_=wb[i][:].rearrange("p x m j -> p (x m j)"),
             )
 
-        hb, z1, sum1, t1, h1b, state = {}, {}, {}, {}, {}, {}
+        def interleave(eng, dst, src):
+            copy(eng, dst.rearrange("p (c i) t -> p c t i", i=4), src.rearrange("p t (c i) -> p c t i", i=4))
 
-        def round_h(k, copy):
-            hb[k] = sb.tile([P, CH, PACK], BF16, name="hb%d" % k, align_bytes=64)
-            interleave(copy, hb[k][:], h_raw[k // 2][:, :, (k % 2) * CH : (k % 2 + 1) * CH])
+        rounded, z, total, t1, y = {}, {}, {}, {}, {}
 
-        def product1(k):
-            hq = quantize("hq%d" % k, hb[k])
-            z1[k] = [ps.tile([P, PACK, CH], F32, name="z1_%d_%d" % (k, g), tag="bank%d_%d" % (g, k)) for g in range(G)]
+        def round_h(k, eng):
+            rounded[0, k] = sb.tile([P, CH, PACK], BF16, name="hb%d" % k, align_bytes=64)
+            interleave(eng, rounded[0, k][:], h_raw[k][:, :, :])
+
+        mov = {}
+
+        def quant(i, k):
+            t = sb.tile([P, CH + SW], I32, name="mov%d_%d" % (i, k), align_bytes=64)
+            nc.vector.quantize_mx(
+                out=t[:, 0:CH].bitcast(FP8X4),
+                scales=t[:, CH:].bitcast(U8),
+                in_=rounded[i, k][:].rearrange("p n t -> p (n t)"),
+            )
+            mov[i, k] = t
+
+        def product(i, k):
+            t = mov[i, k]
+            for g in range(G):
+                z[i, k, g] = ps.tile([P, PACK, CH], F32, name="z%d_%d_%d" % (i, k, g), tag="bank%d_%d_%d" % (g, i, k % 2))
             for x in range(PACK):
                 for g in range(G):
-                    matmul(z1[k][g][:, x, :], 0, g, (x + 1 - g) * R, hq, True, True)
+                    cols = slice((x + 1 - g) * R, (x + 3 - g) * R)
+                    nc.tensor.matmul_mx(
+                        out=z[i, k, g][:, x, :],
+                        lhsT=w_codes[i][rows[g], cols].bitcast(FP8X4),
+                        lhsT_scale=w_scales[i][rows[g], cols],
+                        rhs=t[rows[g], 0:CH].bitcast(FP8X4),
+                        rhs_scale=t[rows[g], CH:].bitcast(U8),
+                        start=True,
+                        stop=True,
+                    )
 
-        def add1(k):
-            sum1[k] = sb.tile([P, PACK, CH], F32, name="sum1_%d" % k)
+        def add(i, k, lo=0, hi=CH):
+            if lo == 0:
+                total[i, k] = sb.tile([P, PACK, CH], F32, name="sum%d_%d" % (i, k))
             for g in range(G):
                 nc.vector.tensor_tensor(
-                    out=sum1[k][rows[g], :, :],
-                    in0=z1[k][g][rows[g], :, :],
-                    in1=x1_sb[k // 2][rows[g], :, (k % 2) * CH : (k % 2 + 1) * CH],
+                    out=total[i, k][rows[g], :, lo:hi],
+                    in0=z[i, k, g][rows[g], :, lo:hi],
+                    in1=x_sb[i][k][rows[g], :, lo:hi],
                     op=ADD,
                 )
+
+        moved = {}
+
+        def evac(i, k):
+            moved[i, k] = sb.tile([P, PACK, CH], F32, name="ev%d_%d" % (i, k))
+            for g in range(G):
+                nc.scalar.copy(out=moved[i, k][rows[g], :, :], in_=z[i, k, g][rows[g], :, :])
+
+        def add_sb(i, k, eng):
+            total[i, k] = sb.tile([P, PACK, CH], F32, name="sum%d_%d" % (i, k))
+            eng.tensor_tensor(
+                out=total[i, k][:], in0=moved[i, k][:], in1=x_sb[i][k][:, :, :], op=ADD
+            )
 
         def tanh1(k):
             t1[k] = sb.tile([P, CH, PACK], F32, name="t1_%d" % k)
             nc.scalar.activation(
                 out=t1[k][:].rearrange("p (c i) t -> p c t i", i=2),
-                in_=sum1[k][:].rearrange("p t (c i) -> p c t i", i=2),
+                in_=total[0, k][:].rearrange("p t (c i) -> p c t i", i=2),
                 func=TANH,
             )
 
-        def scale1(k):
-            h1b[k] = sb.tile([P, CH, PACK], BF16, name="h1b%d" % k, align_bytes=64)
-            nc.vector.tensor_tensor(
-                out=h1b[k][:], in0=t1[k][:], in1=a_sb[:].unsqueeze(1).to_broadcast([P, CH, PACK]), op=MULT
+        def scale1(k, eng):
+            rounded[1, k] = sb.tile([P, CH, PACK], BF16, name="h1b%d" % k, align_bytes=64)
+            eng.tensor_tensor(
+                out=rounded[1, k][:], in0=t1[k][:], in1=a_sb[:].unsqueeze(1).to_broadcast([P, CH, PACK]), op=MULT
             )
 
-        def quant1(k):
-            state[k] = quantize("state%d" % k, h1b[k])
-
-        z2 = {}
-
-        def product2(c):
-            for g in range(G):
-                z2[2 * c + g] = ps.tile([P, PACK, CH], F32, name="z2_%d_%d" % (c, g), tag="bank%d_%d" % (g, c))
-            for x in range(PACK):
-                for s in range(2):
-                    for g in range(G):
-                        matmul(z2[2 * c + g][:, x, :], 1, g, (2 * x + 1 - s) * R, state[2 * s + c], s == 0, s == 1)
-
-        def add(name, bank, x_tile, c):
-            s = sb.tile([P, PACK, CH], F32, name=name)
-            nc.vector.tensor_tensor(out=s[:], in0=bank[:], in1=x_tile[:, :, c * CH : (c + 1) * CH], op=ADD)
-            return s
-
-        y_view = out_0.rearrange("(g p u) n -> g p u n", g=G, u=PACK)
+        y_view = out_0.rearrange("(p u) n -> p u n", u=PACK)
         words_view = out_1[0].rearrange("p n t -> p (n t)").bitcast(I32)
-        scales_view = out_2[0].bitcast(I32).rearrange("(g q r) (s c) -> s q r g c", g=G, q=2, s=2)
-        words = [sb.tile([P, HALF], I32, name="words%d" % g, align_bytes=64) for g in range(G)]
-        y_scales = sb.tile([P, G * HALF], U8, name="y_scales", align_bytes=64)
-        y, yb = {}, {}
+        scales_view = out_2[0].bitcast(I32)
+        words = sb.tile([P, N], I32, name="words", align_bytes=64)
+        y_scales = sb.tile([P, N], U8, name="y_scales", align_bytes=64)
 
-        def add2(q):
-            g, c = chunks[q]
-            s = add("sum2_%d" % q, z2[q], x2_sb[g], c)
-            y[q] = sb.tile([P, PACK, CH], F32, name="y%d" % q)
-            nc.scalar.activation(out=y[q][:], in_=s[:], func=TANH)
+        def tanh2(k, lo=0, hi=CH):
+            if lo == 0:
+                y[k] = sb.tile([P, PACK, CH], F32, name="y%d" % k)
+            nc.scalar.activation(out=y[k][:, :, lo:hi], in_=total[1, k][:, :, lo:hi], func=TANH)
+            if hi == CH:
+                nc.sync.dma_start(out=y_view[:, :, k * CH : (k + 1) * CH], in_=y[k][:])
 
-        def store_y(q, s):
-            g, c = chunks[q]
-            first = s * HALF + c * CH
-            queue[s].dma_start(out=y_view[g][:, :, first : first + CH], in_=y[q][rows[s], :, :])
+        def round2(k, eng, lo=0, hi=CH):
+            if lo == 0:
+                rounded[2, k] = sb.tile([P, CH, PACK], BF16, name="yb%d" % k, align_bytes=64)
+            interleave(eng, rounded[2, k][:, lo:hi, :], y[k][:, :, lo:hi])
 
-        def round2(q):
-            yb[q] = sb.tile([P, CH, PACK], BF16, name="yb%d" % q, align_bytes=64)
-            interleave(nc.vector.tensor_copy, yb[q][:], y[q][:])
-
-        def quant2(q):
-            g, c = chunks[q]
-            first = g * HALF + c * CH
+        def quant2(k, lo=0, hi=CH):
             nc.vector.quantize_mx(
-                out=words[g][:, c * CH : (c + 1) * CH].bitcast(FP8X4),
-                scales=y_scales[:, first : first + CH],
-                in_=yb[q][:].rearrange("p n t -> p (n t)"),
+                out=words[:, k * CH + lo : k * CH + hi].bitcast(FP8X4),
+                scales=y_scales[:, k * CH + lo : k * CH + hi],
+                in_=rounded[2, k][:, lo:hi, :].rearrange("p n t -> p (n t)"),
             )
 
-        def store_words(g):
-            for s in range(2):
-                queue[s].dma_start(out=words_view[rows[g], s * HALF : (s + 1) * HALF], in_=words[g][rows[s], :])
+        def store_words(first, last):
+            nc.sync.dma_start(out=words_view[:, first * CH : last * CH], in_=words[:, first * CH : last * CH])
 
-        w1b = deal_weights(nc.vector.tensor_copy, "w1b", w1_raw)
-        nc.vector.quantize_mx(
-            out=w_codes[0][:, R : 5 * R].bitcast(FP8X4),
-            scales=w_scales[0][:, R : 5 * R],
-            in_=w1b[:].rearrange("p x m j -> p (x m j)"),
-        )
-        round_h(0, nc.vector.tensor_copy)
-        round_h(1, nc.scalar.copy)
-        product1(0)
-        product1(1)
-        add1(0)
-        round_h(2, nc.scalar.copy)
+        def store_scales():
+            for q in range(4):
+                queue[q % 2].dma_start(
+                    out=scales_view[4 * q : 4 * q + 4, :], in_=y_scales[32 * q : 32 * q + 4, :].bitcast(I32)
+                )
+
+        deal(0,V)
+        quant_w(0)
+        round_h(0,V)
+        round_h(1,S)
+        quant(0,0)
+        product(0,0)
+        quant(0,1)
+        product(0,1)
+        add(0,0)
+        round_h(2,S)
         tanh1(0)
-        add1(1)
-        round_h(3, nc.scalar.copy)
+        add(0,1)
+        quant(0,2)
+        product(0,2)
+        round_h(3,S)
         tanh1(1)
-        load_x2(0, 1)
-        load_x2(1, 1)
-        product1(2)
-        scale1(0)
-        product1(3)
-        quant1(0)
-        scale1(1)
-        add1(2)
-        w2b = deal_weights(nc.scalar.copy, "w2b", w2_raw)
+        scale1(0,V)
+        quant(0,3)
+        product(0,3)
+        quant(1,0)
+        scale1(1,V)
+        deal(1,S)
+        add(0,2)
+        evac(0,3)
         tanh1(2)
-        quant1(1)
-        quantize_w2(w2b)
-        scale1(2)
-        quant1(2)
-        product2(0)
-        add1(3)
+        quant(1,1)
+        quant_w(1)
+        product(1,0)
+        product(1,1)
+        add_sb(0,3,V)
         tanh1(3)
-        add2(0)
-        store_y(0, 0)
-        scale1(3)
-        add2(1)
-        store_y(0, 1)
-        store_y(1, 0)
-        quant1(3)
-        product2(1)
-        round2(0)
-        round2(1)
-        store_y(1, 1)
+        scale1(2,V)
+        evac(1,1)
+        add(1,0)
+        quant(1,2)
+        product(1,2)
+        scale1(3,V)
+        tanh2(0)
+        add_sb(1,1,V)
+        quant(1,3)
+        product(1,3)
+        tanh2(1)
+        round2(0,S)
+        add(1,2)
+        round2(1,S)
+        tanh2(2)
         quant2(0)
+        add(1,3)
         quant2(1)
-        add2(2)
-        store_y(2, 0)
-        add2(3)
-        store_y(2, 1)
-        store_y(3, 0)
-        store_y(3, 1)
-        round2(2)
-        round2(3)
+        store_words(0,2)
+        tanh2(3)
+        round2(2,V)
         quant2(2)
-        store_words(0)
+        round2(3,V)
         quant2(3)
-        store_words(1)
-        scale_words = y_scales[:].bitcast(I32).rearrange("p (g c) -> p g c", g=G)
-        for q in range(2):
-            for s in range(2):
-                first = R * s + 32 * q
-                queue[s].dma_start(out=scales_view[s, q], in_=scale_words[first : first + 4, :, :])
+        store_words(2,4)
+        store_scales()

@@ -52,11 +52,6 @@ def tile_rows_pl_steps_tanh_kernel(tc, h, w1, x1, a1, w2, x2, out_0, out_1, out_
             half = load_rows("x2_%d" % s, x2, s * HALF, HALF)
             x_sb[1].extend([half[:, :, 0:CH], half[:, :, CH:]])
 
-        warm = sb.tile([P, 8], F32, name="warm")
-        nc.vector.memset(warm[:], 0.0)
-        warm_out = sb.tile([P, 8], F32, name="warm_out")
-        nc.scalar.activation(out=warm_out[:], in_=warm[:], func=TANH)
-
         w_codes, w_scales = [], []
         for i in range(2):
             codes = sb.tile([P, 6 * R], I32, name="w_codes%d" % i, align_bytes=64)
@@ -83,8 +78,8 @@ def tile_rows_pl_steps_tanh_kernel(tc, h, w1, x1, a1, w2, x2, out_0, out_1, out_
             raw = (w1_raw, w2_raw)[i]
             copy(
                 eng,
-                wb[i][:, :, first:last, :].rearrange("p x m j -> p m j x"),
-                raw[:, :, PACK * first : PACK * last].rearrange("p j (m x) -> p m j x", x=PACK),
+                wb[i][:, :, first:last, :].rearrange("p x m j -> p m x j"),
+                raw[:, :, PACK * first : PACK * last].rearrange("p j (m x) -> p m x j", x=PACK),
             )
 
         def quant_w(i):
@@ -114,40 +109,38 @@ def tile_rows_pl_steps_tanh_kernel(tc, h, w1, x1, a1, w2, x2, out_0, out_1, out_
             )
             mov[i, k] = t
 
-        def product(i, k):
+        def product(i, k, g):
             t = mov[i, k]
-            for g in range(G):
-                z[i, k, g] = ps.tile([P, PACK, CH], F32, name="z%d_%d_%d" % (i, k, g), tag="bank%d_%d_%d" % (g, i, k % 2))
+            z[i, k, g] = ps.tile([P, PACK, CH], F32, name="z%d_%d_%d" % (i, k, g), tag="bank%d_%d_%d" % (g, i, k % 2))
             for x in range(PACK):
-                for g in range(G):
-                    cols = slice((x + 1 - g) * R, (x + 3 - g) * R)
-                    nc.tensor.matmul_mx(
-                        out=z[i, k, g][:, x, :],
-                        lhsT=w_codes[i][rows[g], cols].bitcast(FP8X4),
-                        lhsT_scale=w_scales[i][rows[g], cols],
-                        rhs=t[rows[g], 0:CH].bitcast(FP8X4),
-                        rhs_scale=t[rows[g], CH:].bitcast(U8),
-                        start=True,
-                        stop=True,
-                    )
-
-        def add(i, k, lo=0, hi=CH):
-            if lo == 0:
-                total[i, k] = sb.tile([P, PACK, CH], F32, name="sum%d_%d" % (i, k))
-            for g in range(G):
-                nc.vector.tensor_tensor(
-                    out=total[i, k][rows[g], :, lo:hi],
-                    in0=z[i, k, g][rows[g], :, lo:hi],
-                    in1=x_sb[i][k][rows[g], :, lo:hi],
-                    op=ADD,
+                cols = slice((x + 1 - g) * R, (x + 3 - g) * R)
+                nc.tensor.matmul_mx(
+                    out=z[i, k, g][:, x, :],
+                    lhsT=w_codes[i][rows[g], cols].bitcast(FP8X4),
+                    lhsT_scale=w_scales[i][rows[g], cols],
+                    rhs=t[rows[g], 0:CH].bitcast(FP8X4),
+                    rhs_scale=t[rows[g], CH:].bitcast(U8),
+                    start=True,
+                    stop=True,
                 )
+
+        def add_u(i, k):
+            total[i, k] = sb.tile([P, PACK, CH], F32, name="sum%d_%d" % (i, k))
+            nc.vector.tensor_tensor(out=total[i, k][:], in0=z[i, k, 1][:], in1=x_sb[i][k], op=ADD)
+
+        def add_l(i, k):
+            nc.vector.tensor_tensor(
+                out=total[i, k][0:R, :, :], in0=z[i, k, 0][0:R, :, :], in1=x_sb[i][k][0:R, :, :], op=ADD
+            )
 
         moved = {}
 
-        def evac(i, k):
+        def evac_u(i, k):
             moved[i, k] = sb.tile([P, PACK, CH], F32, name="ev%d_%d" % (i, k))
-            for g in range(G):
-                nc.scalar.copy(out=moved[i, k][rows[g], :, :], in_=z[i, k, g][rows[g], :, :])
+            nc.scalar.copy(out=moved[i, k][:], in_=z[i, k, 1][:])
+
+        def evac_l(i, k):
+            nc.scalar.copy(out=moved[i, k][0:R, :, :], in_=z[i, k, 0][0:R, :, :])
 
         def add_sb(i, k, eng):
             total[i, k] = sb.tile([P, PACK, CH], F32, name="sum%d_%d" % (i, k))
@@ -158,8 +151,8 @@ def tile_rows_pl_steps_tanh_kernel(tc, h, w1, x1, a1, w2, x2, out_0, out_1, out_
         def tanh1(k):
             t1[k] = sb.tile([P, CH, PACK], F32, name="t1_%d" % k)
             nc.scalar.activation(
-                out=t1[k][:].rearrange("p (c i) t -> p c t i", i=2),
-                in_=total[0, k][:].rearrange("p t (c i) -> p c t i", i=2),
+                out=t1[k][:].rearrange("p (c i) t -> p c t i", i=4),
+                in_=total[0, k][:].rearrange("p t (c i) -> p c t i", i=4),
                 func=TANH,
             )
 
@@ -208,55 +201,70 @@ def tile_rows_pl_steps_tanh_kernel(tc, h, w1, x1, a1, w2, x2, out_0, out_1, out_
         round_h(0,V)
         round_h(1,S)
         quant(0,0)
-        product(0,0)
+        product(0,0,1)
         quant(0,1)
-        product(0,1)
-        add(0,0)
+        product(0,1,1)
+        product(0,0,0)
+        product(0,1,0)
+        add_u(0,0)
+        add_u(0,1)
         round_h(2,S)
-        tanh1(0)
-        add(0,1)
-        quant(0,2)
-        product(0,2)
+        add_l(0,0)
         round_h(3,S)
-        tanh1(1)
-        scale1(0,V)
+        quant(0,2)
+        product(0,2,1)
+        tanh1(0)
+        add_l(0,1)
         quant(0,3)
-        product(0,3)
-        quant(1,0)
-        scale1(1,V)
+        product(0,3,1)
+        product(0,2,0)
+        product(0,3,0)
+        scale1(0,GP)
+        tanh1(1)
+        scale1(1,GP)
         deal(1,S)
-        add(0,2)
-        evac(0,3)
+        add_u(0,2)
+        add_u(0,3)
+        add_l(0,2)
         tanh1(2)
-        quant(1,1)
-        quant_w(1)
-        product(1,0)
-        product(1,1)
-        add_sb(0,3,V)
+        add_l(0,3)
         tanh1(3)
+        quant_w(1)
+        quant(1,0)
+        product(1,0,1)
+        product(1,0,0)
+        quant(1,1)
+        product(1,1,1)
+        product(1,1,0)
         scale1(2,V)
-        evac(1,1)
-        add(1,0)
-        quant(1,2)
-        product(1,2)
         scale1(3,V)
-        tanh2(0)
-        add_sb(1,1,V)
+        quant(1,2)
+        product(1,2,1)
+        product(1,2,0)
+        add_u(1,0)
         quant(1,3)
-        product(1,3)
+        product(1,3,1)
+        product(1,3,0)
+        evac_u(1,1)
+        add_l(1,0)
+        evac_l(1,1)
+        tanh2(0)
+        add_u(1,2)
+        add_sb(1,1,V)
         tanh2(1)
+        add_l(1,2)
         round2(0,S)
-        add(1,2)
-        round2(1,S)
+        add_u(1,3)
         tanh2(2)
+        round2(1,V)
+        add_l(1,3)
+        tanh2(3)
         quant2(0)
-        add(1,3)
         quant2(1)
         store_words(0,2)
-        tanh2(3)
         round2(2,V)
-        quant2(2)
         round2(3,V)
+        quant2(2)
         quant2(3)
         store_words(2,4)
         store_scales()

@@ -11,6 +11,7 @@ I32 = mybir.dt.int32
 U8 = mybir.dt.uint8
 FP8X4 = mybir.dt.float8_e4m3fn_x4
 TANH = mybir.ActivationFunctionType.Tanh
+COPY = mybir.ActivationFunctionType.Copy
 ADD = mybir.AluOpType.add
 MULT = mybir.AluOpType.mult
 
@@ -18,7 +19,6 @@ P = 128
 R = 64
 PACK = 4
 CH = 128
-HALF = 256
 SW = CH // 4
 
 
@@ -33,33 +33,36 @@ def tile_rows_pl_steps_tanh_kernel(tc, h, w1, x1, a1, w2, x2, out_0, out_1, out_
         queue = [nc.sync, nc.scalar]
         V, S, GP = nc.vector, nc.scalar, nc.gpsimd
 
-        def load_rows(name, src, first, width):
+        h_raw, x_sb, w_raw = {}, [{}, {}], {}
+
+        def load_rows(name, src, first, width, q):
             raw = sb.tile([P, PACK, width], F32, name=name)
             view = src.rearrange("g (p j) w -> (g p) j w", j=PACK)
-            nc.sync.dma_start(out=raw[:], in_=view[:, :, first : first + width])
+            q.dma_start(out=raw[:], in_=view[:, :, first : first + width])
             return raw
 
-        w1_raw = load_rows("w1_raw", w1, 0, D)
-        a_sb = sb.tile([P, PACK], F32, name="a_sb")
-        nc.scalar.dma_start(out=a_sb[:], in_=a1.rearrange("g (p j) o -> (g p) (j o)", j=PACK))
-        h_raw, x_sb = [], [[], []]
-        for s in range(2):
-            for dst, src, name in ((h_raw, h, "h_%d" % s), (x_sb[0], x1, "x1_%d" % s)):
-                half = load_rows(name, src, s * HALF, HALF)
-                dst.extend([half[:, :, 0:CH], half[:, :, CH:]])
-        w2_raw = load_rows("w2_raw", w2, 0, D)
-        for s in range(2):
-            half = load_rows("x2_%d" % s, x2, s * HALF, HALF)
-            x_sb[1].extend([half[:, :, 0:CH], half[:, :, CH:]])
+        def load_cols(dst, src, name, first, last, q=nc.sync):
+            raw = load_rows("%s_%d" % (name, first), src, first * CH, (last - first) * CH, q)
+            for k in range(first, last):
+                dst[k] = raw[:, :, (k - first) * CH : (k - first + 1) * CH]
 
-        w_codes, w_scales = [], []
+        def load_w(i, q=nc.sync):
+            w_raw[i] = load_rows("w_raw%d" % i, (w1, w2)[i], 0, D, q)
+
+        a_sb = sb.tile([P, PACK], F32, name="a_sb")
+
+        def load_a(q):
+            q.dma_start(out=a_sb[:], in_=a1.rearrange("g (p j) o -> (g p) (j o)", j=PACK))
+
+        w_codes, w_scales, wb = [], [], []
         for i in range(2):
-            codes = sb.tile([P, 6 * R], I32, name="w_codes%d" % i, align_bytes=64)
-            scales = sb.tile([P, 6 * R], U8, name="w_scales%d" % i, align_bytes=64)
-            nc.vector.memset(codes[:], 0)
-            nc.vector.memset(scales[:].bitcast(I32), 0)
-            w_codes.append(codes)
-            w_scales.append(scales)
+            w_codes.append(sb.tile([P, 6 * R], I32, name="w_codes%d" % i, align_bytes=64))
+            w_scales.append(sb.tile([P, 6 * R], U8, name="w_scales%d" % i, align_bytes=64))
+            wb.append(sb.tile([P, PACK, R, PACK], BF16, name="wb%d" % i, align_bytes=64))
+
+        def zero_w(i):
+            nc.vector.memset(w_codes[i][:], 0)
+            nc.vector.memset(w_scales[i][:].bitcast(I32), 0)
 
         def copy(eng, out, in_):
             if eng is S:
@@ -69,17 +72,11 @@ def tile_rows_pl_steps_tanh_kernel(tc, h, w1, x1, a1, w2, x2, out_0, out_1, out_
             else:
                 nc.gpsimd.tensor_scalar(out=out, in0=in_, scalar1=1.0, scalar2=0.0, op0=MULT, op1=ADD)
 
-        wb = {}
-
-        for i in range(2):
-            wb[i] = sb.tile([P, PACK, R, PACK], BF16, name="wb%d" % i, align_bytes=64)
-
         def deal(i, eng, first=0, last=R):
-            raw = (w1_raw, w2_raw)[i]
             copy(
                 eng,
-                wb[i][:, :, first:last, :].rearrange("p x m j -> p m x j"),
-                raw[:, :, PACK * first : PACK * last].rearrange("p j (m x) -> p m x j", x=PACK),
+                wb[i][:, :, first:last, :].rearrange("p x m j -> p m j x"),
+                w_raw[i][:, :, PACK * first : PACK * last].rearrange("p j (m x) -> p m j x", x=PACK),
             )
 
         def quant_w(i):
@@ -89,16 +86,17 @@ def tile_rows_pl_steps_tanh_kernel(tc, h, w1, x1, a1, w2, x2, out_0, out_1, out_
                 in_=wb[i][:].rearrange("p x m j -> p (x m j)"),
             )
 
-        def interleave(eng, dst, src):
-            copy(eng, dst.rearrange("p (c i) t -> p c t i", i=4), src.rearrange("p t (c i) -> p c t i", i=4))
+        def walk_out(dst):
+            return dst.rearrange("p (c i) t -> p c t i", i=4)
 
-        rounded, z, total, t1, y = {}, {}, {}, {}, {}
+        def walk_in(src):
+            return src.rearrange("p t (c i) -> p c t i", i=4)
+
+        rounded, z, total, t1, y, mov, moved = {}, {}, {}, {}, {}, {}, {}
 
         def round_h(k, eng):
             rounded[0, k] = sb.tile([P, CH, PACK], BF16, name="hb%d" % k, align_bytes=64)
-            interleave(eng, rounded[0, k][:], h_raw[k][:, :, :])
-
-        mov = {}
+            copy(eng, walk_out(rounded[0, k][:]), walk_in(h_raw[k]))
 
         def quant(i, k):
             t = sb.tile([P, CH + SW], I32, name="mov%d_%d" % (i, k), align_bytes=64)
@@ -109,31 +107,122 @@ def tile_rows_pl_steps_tanh_kernel(tc, h, w1, x1, a1, w2, x2, out_0, out_1, out_
             )
             mov[i, k] = t
 
-        def product(i, k, g):
+        def bank(i, k, g):
+            z[i, k, g] = ps.tile([P, PACK, CH], F32, name="z%d_%d_%d" % (i, k, g), tag="bank%d_%d" % (g, k))
+
+        def one_pass(i, k, g, x):
             t = mov[i, k]
-            z[i, k, g] = ps.tile([P, PACK, CH], F32, name="z%d_%d_%d" % (i, k, g), tag="bank%d_%d_%d" % (g, i, k % 2))
+            cols = slice((x + 1 - g) * R, (x + 3 - g) * R)
+            nc.tensor.matmul_mx(
+                out=z[i, k, g][:, x, :],
+                lhsT=w_codes[i][rows[g], cols].bitcast(FP8X4),
+                lhsT_scale=w_scales[i][rows[g], cols],
+                rhs=t[rows[g], 0:CH].bitcast(FP8X4),
+                rhs_scale=t[rows[g], CH:].bitcast(U8),
+                start=True,
+                stop=True,
+            )
+
+        def product(i, k, g):
+            bank(i, k, g)
             for x in range(PACK):
-                cols = slice((x + 1 - g) * R, (x + 3 - g) * R)
+                one_pass(i, k, g, x)
+
+        def product_both(i, k):
+            bank(i, k, 1)
+            bank(i, k, 0)
+            for x in range(PACK):
+                one_pass(i, k, 1, x)
+                one_pass(i, k, 0, x)
+
+        def add_u(i, k):
+            total[i, k] = sb.tile([P, PACK, CH], F32, name="sum%d_%d" % (i, k))
+            nc.vector.tensor_tensor(out=total[i, k][:], in0=z[i, k, 1][:], in1=x_sb[i][k], op=ADD)
+
+        def add_l(i, k, lo=0, hi=PACK):
+            nc.vector.tensor_tensor(
+                out=total[i, k][0:R, lo:hi, :], in0=z[i, k, 0][0:R, lo:hi, :], in1=x_sb[i][k][0:R, lo:hi, :], op=ADD
+            )
+
+        def add_lc(i, k, lo, hi):
+            nc.vector.tensor_tensor(
+                out=total[i, k][0:R, :, lo:hi], in0=z[i, k, 0][0:R, :, lo:hi], in1=x_sb[i][k][0:R, :, lo:hi], op=ADD
+            )
+
+        def tanh2c(k, lo, hi):
+            nc.scalar.activation(out=y[k][:, :, lo:hi], in_=total[1, k][:, :, lo:hi], func=TANH)
+
+        zs, ts, xs, ys, evs, tsum = {}, {}, {}, {}, {}, {}
+        HALF = 2 * CH
+
+        def load_x2(sp, q=nc.sync):
+            raw = sb.tile([P, 2, N], F32, name="x2s%d" % sp)
+            view = x2.rearrange("g (p j) w -> (g p) j w", j=PACK)
+            q.dma_start(out=raw[:], in_=view[:, 2 * sp : 2 * sp + 2, :])
+            for hf in range(2):
+                xs[hf, sp] = raw[:, :, hf * HALF : (hf + 1) * HALF]
+
+        def product2(hf, sp, g, c):
+            if c == 0:
+                zs[hf, sp, g] = ps.tile(
+                    [P, 2, HALF], F32, name="zs%d_%d_%d" % (hf, sp, g), tag="bank%d_%d" % (g, 2 * hf + sp)
+                )
+            t = mov[1, 2 * hf + c]
+            for x in range(2):
+                first = 2 * sp + x + 1 - g
+                cols = slice(first * R, (first + 2) * R)
                 nc.tensor.matmul_mx(
-                    out=z[i, k, g][:, x, :],
-                    lhsT=w_codes[i][rows[g], cols].bitcast(FP8X4),
-                    lhsT_scale=w_scales[i][rows[g], cols],
+                    out=zs[hf, sp, g][:, x, c * CH : (c + 1) * CH],
+                    lhsT=w_codes[1][rows[g], cols].bitcast(FP8X4),
+                    lhsT_scale=w_scales[1][rows[g], cols],
                     rhs=t[rows[g], 0:CH].bitcast(FP8X4),
                     rhs_scale=t[rows[g], CH:].bitcast(U8),
                     start=True,
                     stop=True,
                 )
 
-        def add_u(i, k):
-            total[i, k] = sb.tile([P, PACK, CH], F32, name="sum%d_%d" % (i, k))
-            nc.vector.tensor_tensor(out=total[i, k][:], in0=z[i, k, 1][:], in1=x_sb[i][k], op=ADD)
+        def prod2(hf, sp, g):
+            product2(hf, sp, g, 0)
+            product2(hf, sp, g, 1)
 
-        def add_l(i, k):
+        def sum_tile(hf, sp):
+            if hf not in tsum:
+                tsum[hf] = sb.tile([P, PACK, HALF], F32, name="ts%d" % hf)
+                for c in range(2):
+                    total[1, 2 * hf + c] = tsum[hf][:, :, c * CH : (c + 1) * CH]
+            ts[hf, sp] = tsum[hf][:, 2 * sp : 2 * sp + 2, :]
+
+        def add2_u(hf, sp):
+            sum_tile(hf, sp)
+            nc.vector.tensor_tensor(out=ts[hf, sp], in0=zs[hf, sp, 1][:], in1=xs[hf, sp], op=ADD)
+
+        def add2_l(hf, sp, lo=0, hi=HALF):
             nc.vector.tensor_tensor(
-                out=total[i, k][0:R, :, :], in0=z[i, k, 0][0:R, :, :], in1=x_sb[i][k][0:R, :, :], op=ADD
+                out=ts[hf, sp][0:R, :, lo:hi], in0=zs[hf, sp, 0][0:R, :, lo:hi], in1=xs[hf, sp][0:R, :, lo:hi], op=ADD
             )
 
-        moved = {}
+        def evac2_u(hf, sp):
+            evs[hf, sp] = sb.tile([P, 2, HALF], F32, name="evs%d_%d" % (hf, sp))
+            nc.scalar.copy(out=evs[hf, sp][:], in_=zs[hf, sp, 1][:])
+
+        def evac2_l(hf, sp):
+            nc.scalar.copy(out=evs[hf, sp][0:R], in_=zs[hf, sp, 0][0:R])
+
+        def add2_sb(hf, sp, eng):
+            sum_tile(hf, sp)
+            eng.tensor_tensor(out=ts[hf, sp], in0=evs[hf, sp][:], in1=xs[hf, sp], op=ADD)
+
+        def tanh2s(hf, sp, lo=0, hi=HALF):
+            if hf not in ys:
+                ys[hf] = sb.tile([P, PACK, HALF], F32, name="ys%d" % hf)
+                for c in range(2):
+                    y[2 * hf + c] = ys[hf][:, :, c * CH : (c + 1) * CH]
+            nc.scalar.activation(out=ys[hf][:, 2 * sp : 2 * sp + 2, lo:hi], in_=ts[hf, sp][:, :, lo:hi], func=TANH)
+
+        def store_ys(hf, sp, q=nc.sync):
+            q.dma_start(
+                out=y_view[:, 2 * sp : 2 * sp + 2, hf * HALF : (hf + 1) * HALF], in_=ys[hf][:, 2 * sp : 2 * sp + 2, :]
+            )
 
         def evac_u(i, k):
             moved[i, k] = sb.tile([P, PACK, CH], F32, name="ev%d_%d" % (i, k))
@@ -144,41 +233,66 @@ def tile_rows_pl_steps_tanh_kernel(tc, h, w1, x1, a1, w2, x2, out_0, out_1, out_
 
         def add_sb(i, k, eng):
             total[i, k] = sb.tile([P, PACK, CH], F32, name="sum%d_%d" % (i, k))
-            eng.tensor_tensor(
-                out=total[i, k][:], in0=moved[i, k][:], in1=x_sb[i][k][:, :, :], op=ADD
-            )
+            eng.tensor_tensor(out=total[i, k][:], in0=moved[i, k][:], in1=x_sb[i][k], op=ADD)
 
         def tanh1(k):
             t1[k] = sb.tile([P, CH, PACK], F32, name="t1_%d" % k)
-            nc.scalar.activation(
-                out=t1[k][:].rearrange("p (c i) t -> p c t i", i=4),
-                in_=total[0, k][:].rearrange("p t (c i) -> p c t i", i=4),
-                func=TANH,
+            nc.scalar.activation(out=walk_out(t1[k][:]), in_=walk_in(total[0, k][:]), func=TANH)
+
+        def scale1(k, eng, lo=0, hi=CH):
+            if lo == 0:
+                rounded[1, k] = sb.tile([P, CH, PACK], BF16, name="h1b%d" % k, align_bytes=64)
+            eng.tensor_tensor(
+                out=rounded[1, k][:, lo:hi, :],
+                in0=t1[k][:, lo:hi, :],
+                in1=a_sb[:].unsqueeze(1).to_broadcast([P, hi - lo, PACK]),
+                op=MULT,
             )
 
-        def scale1(k, eng):
+        def tanh1_flat(k):
+            t1[k] = sb.tile([P, PACK, CH], F32, name="t1_%d" % k)
+            nc.scalar.activation(out=t1[k][:], in_=total[0, k][:], func=TANH)
+
+        scaled = {}
+
+        def scale1_slots(k):
+            scaled[k] = sb.tile([P, PACK, CH], F32, name="scaled%d" % k)
+            for j in range(PACK):
+                nc.scalar.activation(out=scaled[k][:, j, :], in_=t1[k][:, j, :], func=COPY, scale=a_sb[:, j : j + 1])
+
+        def round1(k, eng):
             rounded[1, k] = sb.tile([P, CH, PACK], BF16, name="h1b%d" % k, align_bytes=64)
-            eng.tensor_tensor(
-                out=rounded[1, k][:], in0=t1[k][:], in1=a_sb[:].unsqueeze(1).to_broadcast([P, CH, PACK]), op=MULT
-            )
+            copy(eng, walk_out(rounded[1, k][:]), walk_in(scaled[k][:]))
 
         y_view = out_0.rearrange("(p u) n -> p u n", u=PACK)
         words_view = out_1[0].rearrange("p n t -> p (n t)").bitcast(I32)
         scales_view = out_2[0].bitcast(I32)
         words = sb.tile([P, N], I32, name="words", align_bytes=64)
         y_scales = sb.tile([P, N], U8, name="y_scales", align_bytes=64)
+        y_tiles = {}
 
-        def tanh2(k, lo=0, hi=CH):
-            if lo == 0:
-                y[k] = sb.tile([P, PACK, CH], F32, name="y%d" % k)
-            nc.scalar.activation(out=y[k][:, :, lo:hi], in_=total[1, k][:, :, lo:hi], func=TANH)
-            if hi == CH:
-                nc.sync.dma_start(out=y_view[:, :, k * CH : (k + 1) * CH], in_=y[k][:])
+        def y_tile(first, last):
+            t = sb.tile([P, PACK, (last - first) * CH], F32, name="y%d" % first)
+            y_tiles[first] = t
+            for k in range(first, last):
+                y[k] = t[:, :, (k - first) * CH : (k - first + 1) * CH]
+
+        def tanh2(k, lo=0, hi=PACK):
+            nc.scalar.activation(out=y[k][:, lo:hi, :], in_=total[1, k][:, lo:hi, :], func=TANH)
+
+        def store_y(first, last, lo=0, hi=PACK, q=nc.sync):
+            q.dma_start(out=y_view[:, lo:hi, first * CH : last * CH], in_=y_tiles[first][:, lo:hi, :])
+
+        def yb(k, lo):
+            if (2, k) not in rounded:
+                rounded[2, k] = sb.tile([P, CH, PACK], BF16, name="yb%d" % k, align_bytes=64)
+            return rounded[2, k]
 
         def round2(k, eng, lo=0, hi=CH):
-            if lo == 0:
-                rounded[2, k] = sb.tile([P, CH, PACK], BF16, name="yb%d" % k, align_bytes=64)
-            interleave(eng, rounded[2, k][:, lo:hi, :], y[k][:, :, lo:hi])
+            copy(eng, walk_out(yb(k, lo)[:, lo:hi, :]), walk_in(y[k][:, :, lo:hi]))
+
+        def tanh2b(k, lo=0, hi=CH):
+            nc.scalar.activation(out=walk_out(yb(k, lo)[:, lo:hi, :]), in_=walk_in(total[1, k][:, :, lo:hi]), func=TANH)
 
         def quant2(k, lo=0, hi=CH):
             nc.vector.quantize_mx(
@@ -187,15 +301,26 @@ def tile_rows_pl_steps_tanh_kernel(tc, h, w1, x1, a1, w2, x2, out_0, out_1, out_
                 in_=rounded[2, k][:, lo:hi, :].rearrange("p n t -> p (n t)"),
             )
 
-        def store_words(first, last):
-            nc.sync.dma_start(out=words_view[:, first * CH : last * CH], in_=words[:, first * CH : last * CH])
+        def store_words(first, last, q=nc.sync):
+            q.dma_start(out=words_view[:, first * CH : last * CH], in_=words[:, first * CH : last * CH])
 
-        def store_scales():
+        def store_scales(queues=(0, 1, 0, 1)):
             for q in range(4):
-                queue[q % 2].dma_start(
+                queue[queues[q]].dma_start(
                     out=scales_view[4 * q : 4 * q + 4, :], in_=y_scales[32 * q : 32 * q + 4, :].bitcast(I32)
                 )
 
+        load_w(0)
+        load_a(nc.scalar)
+        load_cols(h_raw, h, "h", 0, 2)
+        load_cols(x_sb[0], x1, "x1", 0, 2)
+        load_cols(h_raw, h, "h", 2, 4)
+        load_cols(x_sb[0], x1, "x1", 2, 4)
+        load_w(1)
+        load_x2(0)
+        load_x2(1)
+        zero_w(0)
+        zero_w(1)
         deal(0,V)
         quant_w(0)
         round_h(0,V)
@@ -209,16 +334,16 @@ def tile_rows_pl_steps_tanh_kernel(tc, h, w1, x1, a1, w2, x2, out_0, out_1, out_
         add_u(0,0)
         add_u(0,1)
         round_h(2,S)
+        round_h(3,GP)
         add_l(0,0)
-        round_h(3,S)
+        tanh1(0)
         quant(0,2)
         product(0,2,1)
-        tanh1(0)
-        add_l(0,1)
         quant(0,3)
         product(0,3,1)
         product(0,2,0)
         product(0,3,0)
+        add_l(0,1)
         scale1(0,GP)
         tanh1(1)
         scale1(1,GP)
@@ -231,40 +356,47 @@ def tile_rows_pl_steps_tanh_kernel(tc, h, w1, x1, a1, w2, x2, out_0, out_1, out_
         tanh1(3)
         quant_w(1)
         quant(1,0)
-        product(1,0,1)
-        product(1,0,0)
+        product2(0,0,1,0)
         quant(1,1)
-        product(1,1,1)
-        product(1,1,0)
+        product2(0,0,1,1)
+        prod2(0,0,0)
+        prod2(0,1,1)
+        prod2(0,1,0)
         scale1(2,V)
         scale1(3,V)
         quant(1,2)
-        product(1,2,1)
-        product(1,2,0)
-        add_u(1,0)
+        add2_u(0,0)
         quant(1,3)
-        product(1,3,1)
-        product(1,3,0)
-        evac_u(1,1)
-        add_l(1,0)
-        evac_l(1,1)
-        tanh2(0)
-        add_u(1,2)
-        add_sb(1,1,V)
-        tanh2(1)
-        add_l(1,2)
-        round2(0,S)
-        add_u(1,3)
-        tanh2(2)
-        round2(1,V)
-        add_l(1,3)
-        tanh2(3)
+        prod2(1,0,1)
+        prod2(1,0,0)
+        prod2(1,1,1)
+        prod2(1,1,0)
+        evac2_u(0,1)
+        add2_l(0,0)
+        evac2_l(0,1)
+        tanh2s(0,0)
+        store_ys(0,0)
+        add2_u(1,0)
+        add2_sb(0,1,V)
+        add2_l(1,0)
+        tanh2s(0,1)
+        store_ys(0,1)
+        add2_u(1,1)
+        tanh2s(1,0)
+        store_ys(1,0)
+        round2(0,V)
+        add2_l(1,1,0,128)
+        add2_l(1,1,128,256)
+        tanh2b(1)
         quant2(0)
+        tanh2s(1,1,0,128)
+        tanh2s(1,1,128,256)
         quant2(1)
         store_words(0,2)
+        store_ys(1,1)
         round2(2,V)
         round2(3,V)
         quant2(2)
         quant2(3)
-        store_words(2,4)
-        store_scales()
+        store_words(2,4,nc.scalar)
+        store_scales((0,0,1,0))

@@ -94,9 +94,10 @@ def tile_rows_pl_steps_tanh_kernel(tc, h, w1, x1, a1, w2, x2, out_0, out_1, out_
 
         rounded, z, total, t1, y, mov, moved = {}, {}, {}, {}, {}, {}, {}
 
-        def round_h(k, eng):
-            rounded[0, k] = sb.tile([P, CH, PACK], BF16, name="hb%d" % k, align_bytes=64)
-            copy(eng, walk_out(rounded[0, k][:]), walk_in(h_raw[k]))
+        def round_h(k, eng, lo=0, hi=CH):
+            if lo == 0:
+                rounded[0, k] = sb.tile([P, CH, PACK], BF16, name="hb%d" % k, align_bytes=64)
+            copy(eng, walk_out(rounded[0, k][:, lo:hi, :]), walk_in(h_raw[k][:, :, lo:hi]))
 
         def quant(i, k):
             t = sb.tile([P, CH + SW], I32, name="mov%d_%d" % (i, k), align_bytes=64)
@@ -334,8 +335,9 @@ def tile_rows_pl_steps_tanh_kernel(tc, h, w1, x1, a1, w2, x2, out_0, out_1, out_
         add_u(0,0)
         add_u(0,1)
         round_h(2,S)
-        round_h(3,GP)
+        round_h(3,S,0,64)
         add_l(0,0)
+        round_h(3,V,64,128)
         tanh1(0)
         quant(0,2)
         product(0,2,1)
@@ -346,7 +348,7 @@ def tile_rows_pl_steps_tanh_kernel(tc, h, w1, x1, a1, w2, x2, out_0, out_1, out_
         add_l(0,1)
         scale1(0,GP)
         tanh1(1)
-        scale1(1,GP)
+        scale1(1,GP,0,48)
         deal(1,S)
         add_u(0,2)
         add_u(0,3)
@@ -354,6 +356,7 @@ def tile_rows_pl_steps_tanh_kernel(tc, h, w1, x1, a1, w2, x2, out_0, out_1, out_
         tanh1(2)
         add_l(0,3)
         tanh1(3)
+        scale1(1,V,48,128)
         quant_w(1)
         quant(1,0)
         product2(0,0,1,0)

@@ -156,10 +156,14 @@ def tile_rows_pl_steps_tanh_kernel(tc, h, w1, x1, a1, w2, x2, out_0, out_1, out_
         zs, ts, xs, ys, evs, tsum = {}, {}, {}, {}, {}, {}
         HALF = 2 * CH
 
+        x2_all = sb.tile([P, PACK, N], F32, name="x2_all")
+        for k in range(4):
+            x_sb[1][k] = x2_all[:, :, k * CH : (k + 1) * CH]
+
         def load_x2(sp, q=nc.sync):
-            raw = sb.tile([P, 2, N], F32, name="x2s%d" % sp)
+            raw = x2_all[:, 2 * sp : 2 * sp + 2, :]
             view = x2.rearrange("g (p j) w -> (g p) j w", j=PACK)
-            q.dma_start(out=raw[:], in_=view[:, 2 * sp : 2 * sp + 2, :])
+            q.dma_start(out=raw, in_=view[:, 2 * sp : 2 * sp + 2, :])
             for hf in range(2):
                 xs[hf, sp] = raw[:, :, hf * HALF : (hf + 1) * HALF]
 
@@ -240,13 +244,23 @@ def tile_rows_pl_steps_tanh_kernel(tc, h, w1, x1, a1, w2, x2, out_0, out_1, out_
             t1[k] = sb.tile([P, CH, PACK], F32, name="t1_%d" % k)
             nc.scalar.activation(out=walk_out(t1[k][:]), in_=walk_in(total[0, k][:]), func=TANH)
 
-        def scale1(k, eng, lo=0, hi=CH):
+        def scale1(k, eng, lo=0, hi=CH, tag=None):
             if lo == 0:
-                rounded[1, k] = sb.tile([P, CH, PACK], BF16, name="h1b%d" % k, align_bytes=64)
+                rounded[1, k] = sb.tile([P, CH, PACK], BF16, name="h1b%d" % k, tag=tag or "h1b%d" % k, align_bytes=64)
             eng.tensor_tensor(
                 out=rounded[1, k][:, lo:hi, :],
                 in0=t1[k][:, lo:hi, :],
                 in1=a_sb[:].unsqueeze(1).to_broadcast([P, hi - lo, PACK]),
+                op=MULT,
+            )
+
+        def scale1_walk(k, eng, lo=0, hi=CH):
+            if lo == 0:
+                rounded[1, k] = sb.tile([P, CH, PACK], BF16, name="h1b%d" % k, align_bytes=64)
+            eng.tensor_tensor(
+                out=walk_out(rounded[1, k][:, lo:hi, :]),
+                in0=walk_in(t1[k][:, :, lo:hi]),
+                in1=a_sb[:].unsqueeze(1).unsqueeze(3).to_broadcast([P, (hi - lo) // 4, PACK, 4]),
                 op=MULT,
             )
 
@@ -322,9 +336,11 @@ def tile_rows_pl_steps_tanh_kernel(tc, h, w1, x1, a1, w2, x2, out_0, out_1, out_
         load_x2(1)
         zero_w(0)
         zero_w(1)
-        deal(0,V)
+        deal(0,V,0,40)
+        deal(0,S,40,64)
         quant_w(0)
-        round_h(0,V)
+        round_h(0,V,0,88)
+        round_h(0,S,88,128)
         round_h(1,S)
         quant(0,0)
         product(0,0,1)
@@ -338,7 +354,7 @@ def tile_rows_pl_steps_tanh_kernel(tc, h, w1, x1, a1, w2, x2, out_0, out_1, out_
         round_h(3,S,0,64)
         add_l(0,0)
         round_h(3,V,64,128)
-        tanh1(0)
+        tanh1_flat(0)
         quant(0,2)
         product(0,2,1)
         quant(0,3)
@@ -346,17 +362,17 @@ def tile_rows_pl_steps_tanh_kernel(tc, h, w1, x1, a1, w2, x2, out_0, out_1, out_
         product(0,2,0)
         product(0,3,0)
         add_l(0,1)
-        scale1(0,GP)
-        tanh1(1)
-        scale1(1,GP,0,48)
+        scale1_walk(0,GP)
+        tanh1_flat(1)
+        scale1_walk(1,GP,0,64)
         deal(1,S)
         add_u(0,2)
         add_u(0,3)
         add_l(0,2)
-        tanh1(2)
+        tanh1_flat(2)
         add_l(0,3)
-        tanh1(3)
-        scale1(1,V,48,128)
+        tanh1_flat(3)
+        scale1_walk(1,V,64,128)
         quant_w(1)
         quant(1,0)
         product2(0,0,1,0)
@@ -365,8 +381,8 @@ def tile_rows_pl_steps_tanh_kernel(tc, h, w1, x1, a1, w2, x2, out_0, out_1, out_
         prod2(0,0,0)
         prod2(0,1,1)
         prod2(0,1,0)
-        scale1(2,V)
-        scale1(3,V)
+        scale1_walk(2,V)
+        scale1_walk(3,V)
         quant(1,2)
         add2_u(0,0)
         quant(1,3)

@@ -11,71 +11,84 @@ I32 = mybir.dt.int32
 U8 = mybir.dt.uint8
 FP8X4 = mybir.dt.float8_e4m3fn_x4
 TANH = mybir.ActivationFunctionType.Tanh
-COPY = mybir.ActivationFunctionType.Copy
 ADD = mybir.AluOpType.add
 MULT = mybir.AluOpType.mult
 
 P = 128
 R = 64
 PACK = 4
-CH = 128
-SW = CH // 4
+QUARTER = 128
+HALF = 2 * QUARTER
+PLANE_WORDS = QUARTER // 4
+RUN = 4
+
+W1_ON_VECTOR = 40
+H0_ON_VECTOR = 88
+H3_ON_SCALAR = 64
+H1_ON_GPSIMD = 64
 
 
 def tile_rows_pl_steps_tanh_kernel(tc, h, w1, x1, a1, w2, x2, out_0, out_1, out_2):
     nc = tc.nc
     rows = [slice(0, R), slice(R, P)]
+    read = [slice(0, R), slice(0, P)]
+    upper, lower = 1, 0
 
     with ExitStack() as ctx:
         sb = ctx.enter_context(tc.tile_pool(name="sb", bufs=1))
         ps = ctx.enter_context(tc.psum_pool(name="ps", bufs=1))
         ctx.enter_context(tc.manual_schedule())
-        queue = [nc.sync, nc.scalar]
-        V, S, GP = nc.vector, nc.scalar, nc.gpsimd
 
-        h_raw, x_sb, w_raw = {}, [{}, {}], {}
+        def by_slot(src):
+            return src.rearrange("g (p j) w -> (g p) j w", j=PACK)
 
-        def load_rows(name, src, first, width, q):
-            raw = sb.tile([P, PACK, width], F32, name=name)
-            view = src.rearrange("g (p j) w -> (g p) j w", j=PACK)
-            q.dma_start(out=raw[:], in_=view[:, :, first : first + width])
+        def quarter(k):
+            return slice(k * QUARTER, (k + 1) * QUARTER)
+
+        def half(hf):
+            return slice(hf * HALF, (hf + 1) * HALF)
+
+        def pair(sp):
+            return slice(2 * sp, 2 * sp + 2)
+
+        def load(name, src, cols):
+            raw = sb.tile([P, PACK, cols.stop - cols.start], F32, name=name)
+            nc.sync.dma_start(out=raw[:], in_=by_slot(src)[:, :, cols])
             return raw
 
-        def load_cols(dst, src, name, first, last, q=nc.sync):
-            raw = load_rows("%s_%d" % (name, first), src, first * CH, (last - first) * CH, q)
-            for k in range(first, last):
-                dst[k] = raw[:, :, (k - first) * CH : (k - first + 1) * CH]
-
-        def load_w(i, q=nc.sync):
-            w_raw[i] = load_rows("w_raw%d" % i, (w1, w2)[i], 0, D, q)
-
+        w_raw = [load("w1_raw", w1, slice(0, D))]
         a_sb = sb.tile([P, PACK], F32, name="a_sb")
+        nc.scalar.dma_start(out=a_sb[:], in_=a1.rearrange("g (p j) o -> (g p) (j o)", j=PACK))
+        h_raw, x1_sb = [], []
+        for hf in range(2):
+            for dst, src, name in ((h_raw, h, "h_raw%d" % hf), (x1_sb, x1, "x1_sb%d" % hf)):
+                raw = load(name, src, half(hf))
+                dst.extend([raw[:, :, quarter(0)], raw[:, :, quarter(1)]])
+        w_raw.append(load("w2_raw", w2, slice(0, D)))
+        x2_sb = sb.tile([P, PACK, N], F32, name="x2_sb")
+        for sp in range(2):
+            nc.sync.dma_start(out=x2_sb[:, pair(sp), :], in_=by_slot(x2)[:, pair(sp), :])
 
-        def load_a(q):
-            q.dma_start(out=a_sb[:], in_=a1.rearrange("g (p j) o -> (g p) (j o)", j=PACK))
-
-        w_codes, w_scales, wb = [], [], []
+        w_codes, w_scales, w_dealt = [], [], []
         for i in range(2):
-            w_codes.append(sb.tile([P, 6 * R], I32, name="w_codes%d" % i, align_bytes=64))
-            w_scales.append(sb.tile([P, 6 * R], U8, name="w_scales%d" % i, align_bytes=64))
-            wb.append(sb.tile([P, PACK, R, PACK], BF16, name="wb%d" % i, align_bytes=64))
-
-        def zero_w(i):
-            nc.vector.memset(w_codes[i][:], 0)
-            nc.vector.memset(w_scales[i][:].bitcast(I32), 0)
+            codes = sb.tile([P, 6 * R], I32, name="w_codes%d" % i, align_bytes=64)
+            scales = sb.tile([P, 6 * R], U8, name="w_scales%d" % i, align_bytes=64)
+            nc.vector.memset(codes[:].rearrange("p (b m) -> p b m", m=R)[:, 0:6:5, :], 0)
+            nc.vector.memset(scales[:].bitcast(I32).rearrange("p (b m) -> p b m", b=6)[:, 0:6:5, :], 0)
+            w_codes.append(codes)
+            w_scales.append(scales)
+            w_dealt.append(sb.tile([P, PACK, R, PACK], BF16, name="w_dealt%d" % i, align_bytes=64))
 
         def copy(eng, out, in_):
-            if eng is S:
+            if eng is nc.scalar:
                 nc.scalar.copy(out=out, in_=in_)
-            elif eng is V:
-                nc.vector.tensor_copy(out=out, in_=in_)
             else:
-                nc.gpsimd.tensor_scalar(out=out, in0=in_, scalar1=1.0, scalar2=0.0, op0=MULT, op1=ADD)
+                nc.vector.tensor_copy(out=out, in_=in_)
 
-        def deal(i, eng, first=0, last=R):
+        def deal_w(i, eng, first, last):
             copy(
                 eng,
-                wb[i][:, :, first:last, :].rearrange("p x m j -> p m j x"),
+                w_dealt[i][:, :, first:last, :].rearrange("p x m j -> p m j x"),
                 w_raw[i][:, :, PACK * first : PACK * last].rearrange("p j (m x) -> p m j x", x=PACK),
             )
 
@@ -83,339 +96,211 @@ def tile_rows_pl_steps_tanh_kernel(tc, h, w1, x1, a1, w2, x2, out_0, out_1, out_
             nc.vector.quantize_mx(
                 out=w_codes[i][:, R : 5 * R].bitcast(FP8X4),
                 scales=w_scales[i][:, R : 5 * R],
-                in_=wb[i][:].rearrange("p x m j -> p (x m j)"),
+                in_=w_dealt[i][:].rearrange("p x m j -> p (x m j)"),
             )
 
-        def walk_out(dst):
-            return dst.rearrange("p (c i) t -> p c t i", i=4)
+        def packed_walk(dst):
+            return dst.rearrange("p (c i) j -> p c j i", i=RUN)
 
-        def walk_in(src):
-            return src.rearrange("p t (c i) -> p c t i", i=4)
+        def flat_walk(src):
+            return src.rearrange("p j (c i) -> p c j i", i=RUN)
 
-        rounded, z, total, t1, y, mov, moved = {}, {}, {}, {}, {}, {}, {}
+        def packed_tiles(name):
+            return [sb.tile([P, QUARTER, PACK], BF16, name="%s%d" % (name, k), align_bytes=64) for k in range(4)]
 
-        def round_h(k, eng, lo=0, hi=CH):
-            if lo == 0:
-                rounded[0, k] = sb.tile([P, CH, PACK], BF16, name="hb%d" % k, align_bytes=64)
-            copy(eng, walk_out(rounded[0, k][:, lo:hi, :]), walk_in(h_raw[k][:, :, lo:hi]))
+        h_packed, h1_packed, y_packed = packed_tiles("h_packed"), packed_tiles("h1_packed"), packed_tiles("y_packed")
+        moving = {}
 
-        def quant(i, k):
-            t = sb.tile([P, CH + SW], I32, name="mov%d_%d" % (i, k), align_bytes=64)
+        def round_h(k, eng, first=0, last=QUARTER):
+            copy(eng, packed_walk(h_packed[k][:, first:last, :]), flat_walk(h_raw[k][:, :, first:last]))
+
+        def quant_moving(step, k):
+            t = sb.tile([P, QUARTER + PLANE_WORDS], I32, name="moving%d_%d" % (step, k), align_bytes=64)
             nc.vector.quantize_mx(
-                out=t[:, 0:CH].bitcast(FP8X4),
-                scales=t[:, CH:].bitcast(U8),
-                in_=rounded[i, k][:].rearrange("p n t -> p (n t)"),
+                out=t[:, 0:QUARTER].bitcast(FP8X4),
+                scales=t[:, QUARTER:].bitcast(U8),
+                in_=(h_packed, h1_packed)[step][k][:].rearrange("p n j -> p (n j)"),
             )
-            mov[i, k] = t
+            moving[step, k] = t
 
-        def bank(i, k, g):
-            z[i, k, g] = ps.tile([P, PACK, CH], F32, name="z%d_%d_%d" % (i, k, g), tag="bank%d_%d" % (g, k))
-
-        def one_pass(i, k, g, x):
-            t = mov[i, k]
-            cols = slice((x + 1 - g) * R, (x + 3 - g) * R)
+        def one_pass(out, step, k, g, x):
+            t = moving[step, k]
+            window = slice((x + 1 - g) * R, (x + 3 - g) * R)
             nc.tensor.matmul_mx(
-                out=z[i, k, g][:, x, :],
-                lhsT=w_codes[i][rows[g], cols].bitcast(FP8X4),
-                lhsT_scale=w_scales[i][rows[g], cols],
-                rhs=t[rows[g], 0:CH].bitcast(FP8X4),
-                rhs_scale=t[rows[g], CH:].bitcast(U8),
+                out=out,
+                lhsT=w_codes[step][rows[g], window].bitcast(FP8X4),
+                lhsT_scale=w_scales[step][rows[g], window],
+                rhs=t[rows[g], 0:QUARTER].bitcast(FP8X4),
+                rhs_scale=t[rows[g], QUARTER:].bitcast(U8),
                 start=True,
                 stop=True,
             )
 
-        def product(i, k, g):
-            bank(i, k, g)
+        z1 = {}
+        sum1 = [sb.tile([P, PACK, QUARTER], F32, name="sum1_%d" % k) for k in range(4)]
+        tanh1 = [sb.tile([P, PACK, QUARTER], F32, name="tanh1_%d" % k) for k in range(4)]
+
+        def product1(k, g):
+            z1[k, g] = ps.tile([P, PACK, QUARTER], F32, name="z1_%d_%d" % (k, g), tag="bank%d_%d" % (g, k))
             for x in range(PACK):
-                one_pass(i, k, g, x)
+                one_pass(z1[k, g][:, x, :], 0, k, g, x)
 
-        def product_both(i, k):
-            bank(i, k, 1)
-            bank(i, k, 0)
-            for x in range(PACK):
-                one_pass(i, k, 1, x)
-                one_pass(i, k, 0, x)
+        def add1(k, g):
+            part = read[g]
+            nc.vector.tensor_tensor(out=sum1[k][part], in0=z1[k, g][part], in1=x1_sb[k][part], op=ADD)
 
-        def add_u(i, k):
-            total[i, k] = sb.tile([P, PACK, CH], F32, name="sum%d_%d" % (i, k))
-            nc.vector.tensor_tensor(out=total[i, k][:], in0=z[i, k, 1][:], in1=x_sb[i][k], op=ADD)
+        def act1(k):
+            nc.scalar.activation(out=tanh1[k][:], in_=sum1[k][:], func=TANH)
 
-        def add_l(i, k, lo=0, hi=PACK):
-            nc.vector.tensor_tensor(
-                out=total[i, k][0:R, lo:hi, :], in0=z[i, k, 0][0:R, lo:hi, :], in1=x_sb[i][k][0:R, lo:hi, :], op=ADD
-            )
-
-        def add_lc(i, k, lo, hi):
-            nc.vector.tensor_tensor(
-                out=total[i, k][0:R, :, lo:hi], in0=z[i, k, 0][0:R, :, lo:hi], in1=x_sb[i][k][0:R, :, lo:hi], op=ADD
-            )
-
-        def tanh2c(k, lo, hi):
-            nc.scalar.activation(out=y[k][:, :, lo:hi], in_=total[1, k][:, :, lo:hi], func=TANH)
-
-        zs, ts, xs, ys, evs, tsum = {}, {}, {}, {}, {}, {}
-        HALF = 2 * CH
-
-        x2_all = sb.tile([P, PACK, N], F32, name="x2_all")
-        for k in range(4):
-            x_sb[1][k] = x2_all[:, :, k * CH : (k + 1) * CH]
-
-        def load_x2(sp, q=nc.sync):
-            raw = x2_all[:, 2 * sp : 2 * sp + 2, :]
-            view = x2.rearrange("g (p j) w -> (g p) j w", j=PACK)
-            q.dma_start(out=raw, in_=view[:, 2 * sp : 2 * sp + 2, :])
-            for hf in range(2):
-                xs[hf, sp] = raw[:, :, hf * HALF : (hf + 1) * HALF]
-
-        def product2(hf, sp, g, c):
-            if c == 0:
-                zs[hf, sp, g] = ps.tile(
-                    [P, 2, HALF], F32, name="zs%d_%d_%d" % (hf, sp, g), tag="bank%d_%d" % (g, 2 * hf + sp)
-                )
-            t = mov[1, 2 * hf + c]
-            for x in range(2):
-                first = 2 * sp + x + 1 - g
-                cols = slice(first * R, (first + 2) * R)
-                nc.tensor.matmul_mx(
-                    out=zs[hf, sp, g][:, x, c * CH : (c + 1) * CH],
-                    lhsT=w_codes[1][rows[g], cols].bitcast(FP8X4),
-                    lhsT_scale=w_scales[1][rows[g], cols],
-                    rhs=t[rows[g], 0:CH].bitcast(FP8X4),
-                    rhs_scale=t[rows[g], CH:].bitcast(U8),
-                    start=True,
-                    stop=True,
-                )
-
-        def prod2(hf, sp, g):
-            product2(hf, sp, g, 0)
-            product2(hf, sp, g, 1)
-
-        def sum_tile(hf, sp):
-            if hf not in tsum:
-                tsum[hf] = sb.tile([P, PACK, HALF], F32, name="ts%d" % hf)
-                for c in range(2):
-                    total[1, 2 * hf + c] = tsum[hf][:, :, c * CH : (c + 1) * CH]
-            ts[hf, sp] = tsum[hf][:, 2 * sp : 2 * sp + 2, :]
-
-        def add2_u(hf, sp):
-            sum_tile(hf, sp)
-            nc.vector.tensor_tensor(out=ts[hf, sp], in0=zs[hf, sp, 1][:], in1=xs[hf, sp], op=ADD)
-
-        def add2_l(hf, sp, lo=0, hi=HALF):
-            nc.vector.tensor_tensor(
-                out=ts[hf, sp][0:R, :, lo:hi], in0=zs[hf, sp, 0][0:R, :, lo:hi], in1=xs[hf, sp][0:R, :, lo:hi], op=ADD
-            )
-
-        def evac2_u(hf, sp):
-            evs[hf, sp] = sb.tile([P, 2, HALF], F32, name="evs%d_%d" % (hf, sp))
-            nc.scalar.copy(out=evs[hf, sp][:], in_=zs[hf, sp, 1][:])
-
-        def evac2_l(hf, sp):
-            nc.scalar.copy(out=evs[hf, sp][0:R], in_=zs[hf, sp, 0][0:R])
-
-        def add2_sb(hf, sp, eng):
-            sum_tile(hf, sp)
-            eng.tensor_tensor(out=ts[hf, sp], in0=evs[hf, sp][:], in1=xs[hf, sp], op=ADD)
-
-        def tanh2s(hf, sp, lo=0, hi=HALF):
-            if hf not in ys:
-                ys[hf] = sb.tile([P, PACK, HALF], F32, name="ys%d" % hf)
-                for c in range(2):
-                    y[2 * hf + c] = ys[hf][:, :, c * CH : (c + 1) * CH]
-            nc.scalar.activation(out=ys[hf][:, 2 * sp : 2 * sp + 2, lo:hi], in_=ts[hf, sp][:, :, lo:hi], func=TANH)
-
-        def store_ys(hf, sp, q=nc.sync):
-            q.dma_start(
-                out=y_view[:, 2 * sp : 2 * sp + 2, hf * HALF : (hf + 1) * HALF], in_=ys[hf][:, 2 * sp : 2 * sp + 2, :]
-            )
-
-        def evac_u(i, k):
-            moved[i, k] = sb.tile([P, PACK, CH], F32, name="ev%d_%d" % (i, k))
-            nc.scalar.copy(out=moved[i, k][:], in_=z[i, k, 1][:])
-
-        def evac_l(i, k):
-            nc.scalar.copy(out=moved[i, k][0:R, :, :], in_=z[i, k, 0][0:R, :, :])
-
-        def add_sb(i, k, eng):
-            total[i, k] = sb.tile([P, PACK, CH], F32, name="sum%d_%d" % (i, k))
-            eng.tensor_tensor(out=total[i, k][:], in0=moved[i, k][:], in1=x_sb[i][k], op=ADD)
-
-        def tanh1(k):
-            t1[k] = sb.tile([P, CH, PACK], F32, name="t1_%d" % k)
-            nc.scalar.activation(out=walk_out(t1[k][:]), in_=walk_in(total[0, k][:]), func=TANH)
-
-        def scale1(k, eng, lo=0, hi=CH, tag=None):
-            if lo == 0:
-                rounded[1, k] = sb.tile([P, CH, PACK], BF16, name="h1b%d" % k, tag=tag or "h1b%d" % k, align_bytes=64)
+        def scale1(k, eng, first=0, last=QUARTER):
             eng.tensor_tensor(
-                out=rounded[1, k][:, lo:hi, :],
-                in0=t1[k][:, lo:hi, :],
-                in1=a_sb[:].unsqueeze(1).to_broadcast([P, hi - lo, PACK]),
+                out=packed_walk(h1_packed[k][:, first:last, :]),
+                in0=flat_walk(tanh1[k][:, :, first:last]),
+                in1=a_sb[:].unsqueeze(1).unsqueeze(3).to_broadcast([P, (last - first) // RUN, PACK, RUN]),
                 op=MULT,
             )
 
-        def scale1_walk(k, eng, lo=0, hi=CH):
-            if lo == 0:
-                rounded[1, k] = sb.tile([P, CH, PACK], BF16, name="h1b%d" % k, align_bytes=64)
-            eng.tensor_tensor(
-                out=walk_out(rounded[1, k][:, lo:hi, :]),
-                in0=walk_in(t1[k][:, :, lo:hi]),
-                in1=a_sb[:].unsqueeze(1).unsqueeze(3).to_broadcast([P, (hi - lo) // 4, PACK, 4]),
-                op=MULT,
-            )
-
-        def tanh1_flat(k):
-            t1[k] = sb.tile([P, PACK, CH], F32, name="t1_%d" % k)
-            nc.scalar.activation(out=t1[k][:], in_=total[0, k][:], func=TANH)
-
-        scaled = {}
-
-        def scale1_slots(k):
-            scaled[k] = sb.tile([P, PACK, CH], F32, name="scaled%d" % k)
-            for j in range(PACK):
-                nc.scalar.activation(out=scaled[k][:, j, :], in_=t1[k][:, j, :], func=COPY, scale=a_sb[:, j : j + 1])
-
-        def round1(k, eng):
-            rounded[1, k] = sb.tile([P, CH, PACK], BF16, name="h1b%d" % k, align_bytes=64)
-            copy(eng, walk_out(rounded[1, k][:]), walk_in(scaled[k][:]))
-
-        y_view = out_0.rearrange("(p u) n -> p u n", u=PACK)
-        words_view = out_1[0].rearrange("p n t -> p (n t)").bitcast(I32)
-        scales_view = out_2[0].bitcast(I32)
+        z2 = {}
+        sum2 = [sb.tile([P, PACK, HALF], F32, name="sum2_%d" % hf) for hf in range(2)]
+        copied = [sb.tile([P, 2, HALF], F32, name="copied%d" % hf) for hf in range(2)]
+        y = sb.tile([P, PACK, N], F32, name="y")
         words = sb.tile([P, N], I32, name="words", align_bytes=64)
         y_scales = sb.tile([P, N], U8, name="y_scales", align_bytes=64)
-        y_tiles = {}
+        y_view = out_0.rearrange("(p j) n -> p j n", j=PACK)
+        words_view = out_1[0].rearrange("p n j -> p (n j)").bitcast(I32)
+        scales_view = out_2[0].bitcast(I32)
 
-        def y_tile(first, last):
-            t = sb.tile([P, PACK, (last - first) * CH], F32, name="y%d" % first)
-            y_tiles[first] = t
-            for k in range(first, last):
-                y[k] = t[:, :, (k - first) * CH : (k - first + 1) * CH]
+        def product2(hf, sp, g, quarters=(0, 1)):
+            if (hf, sp, g) not in z2:
+                z2[hf, sp, g] = ps.tile(
+                    [P, 2, HALF], F32, name="z2_%d_%d_%d" % (hf, sp, g), tag="bank%d_%d" % (g, 2 * hf + sp)
+                )
+            for c in quarters:
+                for x in range(2):
+                    one_pass(z2[hf, sp, g][:, x, quarter(c)], 1, 2 * hf + c, g, 2 * sp + x)
 
-        def tanh2(k, lo=0, hi=PACK):
-            nc.scalar.activation(out=y[k][:, lo:hi, :], in_=total[1, k][:, lo:hi, :], func=TANH)
-
-        def store_y(first, last, lo=0, hi=PACK, q=nc.sync):
-            q.dma_start(out=y_view[:, lo:hi, first * CH : last * CH], in_=y_tiles[first][:, lo:hi, :])
-
-        def yb(k, lo):
-            if (2, k) not in rounded:
-                rounded[2, k] = sb.tile([P, CH, PACK], BF16, name="yb%d" % k, align_bytes=64)
-            return rounded[2, k]
-
-        def round2(k, eng, lo=0, hi=CH):
-            copy(eng, walk_out(yb(k, lo)[:, lo:hi, :]), walk_in(y[k][:, :, lo:hi]))
-
-        def tanh2b(k, lo=0, hi=CH):
-            nc.scalar.activation(out=walk_out(yb(k, lo)[:, lo:hi, :]), in_=walk_in(total[1, k][:, :, lo:hi]), func=TANH)
-
-        def quant2(k, lo=0, hi=CH):
-            nc.vector.quantize_mx(
-                out=words[:, k * CH + lo : k * CH + hi].bitcast(FP8X4),
-                scales=y_scales[:, k * CH + lo : k * CH + hi],
-                in_=rounded[2, k][:, lo:hi, :].rearrange("p n t -> p (n t)"),
+        def add2(hf, sp, g, first=0, last=HALF):
+            part = read[g]
+            nc.vector.tensor_tensor(
+                out=sum2[hf][part, pair(sp), first:last],
+                in0=z2[hf, sp, g][part, :, first:last],
+                in1=x2_sb[part, pair(sp), hf * HALF + first : hf * HALF + last],
+                op=ADD,
             )
 
-        def store_words(first, last, q=nc.sync):
-            q.dma_start(out=words_view[:, first * CH : last * CH], in_=words[:, first * CH : last * CH])
+        def copy_banks(hf, sp):
+            for g in (upper, lower):
+                nc.scalar.copy(out=copied[hf][rows[g]], in_=z2[hf, sp, g][rows[g]])
 
-        def store_scales(queues=(0, 1, 0, 1)):
-            for q in range(4):
-                queue[queues[q]].dma_start(
-                    out=scales_view[4 * q : 4 * q + 4, :], in_=y_scales[32 * q : 32 * q + 4, :].bitcast(I32)
-                )
+        def add_copied(hf, sp):
+            nc.vector.tensor_tensor(
+                out=sum2[hf][:, pair(sp), :], in0=copied[hf][:], in1=x2_sb[:, pair(sp), half(hf)], op=ADD
+            )
 
-        load_w(0)
-        load_a(nc.scalar)
-        load_cols(h_raw, h, "h", 0, 2)
-        load_cols(x_sb[0], x1, "x1", 0, 2)
-        load_cols(h_raw, h, "h", 2, 4)
-        load_cols(x_sb[0], x1, "x1", 2, 4)
-        load_w(1)
-        load_x2(0)
-        load_x2(1)
-        zero_w(0)
-        zero_w(1)
-        deal(0,V,0,40)
-        deal(0,S,40,64)
+        def act2(hf, sp, first=0, last=HALF):
+            nc.scalar.activation(
+                out=y[:, pair(sp), hf * HALF + first : hf * HALF + last],
+                in_=sum2[hf][:, pair(sp), first:last],
+                func=TANH,
+            )
+
+        def round_y(k):
+            nc.vector.tensor_copy(out=packed_walk(y_packed[k][:]), in_=flat_walk(y[:, :, quarter(k)]))
+
+        def act2_packed(k):
+            nc.scalar.activation(
+                out=packed_walk(y_packed[k][:]), in_=flat_walk(sum2[k // 2][:, :, quarter(k % 2)]), func=TANH
+            )
+
+        def quant_y(k):
+            nc.vector.quantize_mx(
+                out=words[:, quarter(k)].bitcast(FP8X4),
+                scales=y_scales[:, quarter(k)],
+                in_=y_packed[k][:].rearrange("p n j -> p (n j)"),
+            )
+
+        def store_y(hf, sp):
+            nc.sync.dma_start(out=y_view[:, pair(sp), half(hf)], in_=y[:, pair(sp), half(hf)])
+
+        vector, scalar, gpsimd = nc.vector, nc.scalar, nc.gpsimd
+
+        deal_w(0, vector, 0, W1_ON_VECTOR)
+        deal_w(0, scalar, W1_ON_VECTOR, R)
         quant_w(0)
-        round_h(0,V,0,88)
-        round_h(0,S,88,128)
-        round_h(1,S)
-        quant(0,0)
-        product(0,0,1)
-        quant(0,1)
-        product(0,1,1)
-        product(0,0,0)
-        product(0,1,0)
-        add_u(0,0)
-        add_u(0,1)
-        round_h(2,S)
-        round_h(3,S,0,64)
-        add_l(0,0)
-        round_h(3,V,64,128)
-        tanh1_flat(0)
-        quant(0,2)
-        product(0,2,1)
-        quant(0,3)
-        product(0,3,1)
-        product(0,2,0)
-        product(0,3,0)
-        add_l(0,1)
-        scale1_walk(0,GP)
-        tanh1_flat(1)
-        scale1_walk(1,GP,0,64)
-        deal(1,S)
-        add_u(0,2)
-        add_u(0,3)
-        add_l(0,2)
-        tanh1_flat(2)
-        add_l(0,3)
-        tanh1_flat(3)
-        scale1_walk(1,V,64,128)
+        round_h(0, vector, 0, H0_ON_VECTOR)
+        round_h(0, scalar, H0_ON_VECTOR, QUARTER)
+        round_h(1, scalar)
+        for k in (0, 1):
+            quant_moving(0, k)
+            product1(k, upper)
+        for k in (0, 1):
+            product1(k, lower)
+        for k in (0, 1):
+            add1(k, upper)
+        round_h(2, scalar)
+        round_h(3, scalar, 0, H3_ON_SCALAR)
+        add1(0, lower)
+        round_h(3, vector, H3_ON_SCALAR, QUARTER)
+        act1(0)
+
+        for k in (2, 3):
+            quant_moving(0, k)
+            product1(k, upper)
+        for k in (2, 3):
+            product1(k, lower)
+        add1(1, lower)
+        scale1(0, gpsimd)
+        act1(1)
+        scale1(1, gpsimd, 0, H1_ON_GPSIMD)
+        deal_w(1, scalar, 0, R)
+        for k in (2, 3):
+            add1(k, upper)
+        for k in (2, 3):
+            add1(k, lower)
+            act1(k)
+
+        scale1(1, vector, H1_ON_GPSIMD, QUARTER)
         quant_w(1)
-        quant(1,0)
-        product2(0,0,1,0)
-        quant(1,1)
-        product2(0,0,1,1)
-        prod2(0,0,0)
-        prod2(0,1,1)
-        prod2(0,1,0)
-        scale1_walk(2,V)
-        scale1_walk(3,V)
-        quant(1,2)
-        add2_u(0,0)
-        quant(1,3)
-        prod2(1,0,1)
-        prod2(1,0,0)
-        prod2(1,1,1)
-        prod2(1,1,0)
-        evac2_u(0,1)
-        add2_l(0,0)
-        evac2_l(0,1)
-        tanh2s(0,0)
-        store_ys(0,0)
-        add2_u(1,0)
-        add2_sb(0,1,V)
-        add2_l(1,0)
-        tanh2s(0,1)
-        store_ys(0,1)
-        add2_u(1,1)
-        tanh2s(1,0)
-        store_ys(1,0)
-        round2(0,V)
-        add2_l(1,1,0,128)
-        add2_l(1,1,128,256)
-        tanh2b(1)
-        quant2(0)
-        tanh2s(1,1,0,128)
-        tanh2s(1,1,128,256)
-        quant2(1)
-        store_words(0,2)
-        store_ys(1,1)
-        round2(2,V)
-        round2(3,V)
-        quant2(2)
-        quant2(3)
-        store_words(2,4,nc.scalar)
-        store_scales((0,0,1,0))
+        for c in (0, 1):
+            quant_moving(1, c)
+            product2(0, 1, upper, (c,))
+        product2(0, 1, lower)
+        product2(0, 0, upper)
+        product2(0, 0, lower)
+        for k in (2, 3):
+            scale1(k, vector)
+        copy_banks(0, 1)
+        for k in (2, 3):
+            quant_moving(1, k)
+        for sp in (0, 1):
+            product2(1, sp, upper)
+            product2(1, sp, lower)
+        add2(0, 0, upper)
+        add_copied(0, 1)
+
+        copy_banks(1, 0)
+        act2(0, 1)
+        store_y(0, 1)
+        add2(0, 0, lower)
+        act2(0, 0)
+        store_y(0, 0)
+        add2(1, 1, upper)
+        add_copied(1, 0)
+        act2(1, 0)
+        store_y(1, 0)
+
+        for c in (0, 1):
+            add2(1, 1, lower, c * QUARTER, (c + 1) * QUARTER)
+        for k in (0, 1):
+            round_y(k)
+        for c in (0, 1):
+            act2(1, 1, c * QUARTER, (c + 1) * QUARTER)
+        act2_packed(3)
+        store_y(1, 1)
+        round_y(2)
+        for k in range(4):
+            quant_y(k)
+        nc.scalar.dma_start(out=words_view, in_=words[:])
+
+        for q, queue in enumerate((nc.sync, nc.sync, nc.scalar, nc.sync)):
+            queue.dma_start(out=scales_view[4 * q : 4 * q + 4, :], in_=y_scales[32 * q : 32 * q + 4, :].bitcast(I32))

@@ -17,6 +17,7 @@ MULT = mybir.AluOpType.mult
 P = 128
 R = 64
 PACK = 4
+ROWS = 2
 QUARTER = 128
 HALF = 2 * QUARTER
 PLANE_WORDS = QUARTER // 4
@@ -33,6 +34,7 @@ def tile_rows_pl_steps_tanh_kernel(tc, h, w1, x1, a1, w2, x2, out_0, out_1, out_
     rows = [slice(0, R), slice(R, P)]
     read = [slice(0, R), slice(0, P)]
     upper, lower = 1, 0
+    heads = (upper, lower)
 
     with ExitStack() as ctx:
         sb = ctx.enter_context(tc.tile_pool(name="sb", bufs=1))
@@ -42,42 +44,39 @@ def tile_rows_pl_steps_tanh_kernel(tc, h, w1, x1, a1, w2, x2, out_0, out_1, out_
         def by_slot(src):
             return src.rearrange("g (p j) w -> (g p) j w", j=PACK)
 
+        def by_row(src):
+            return src.rearrange("(q s) n -> q s n", s=ROWS)
+
         def quarter(k):
             return slice(k * QUARTER, (k + 1) * QUARTER)
 
         def half(hf):
             return slice(hf * HALF, (hf + 1) * HALF)
 
-        def pair(sp):
-            return slice(2 * sp, 2 * sp + 2)
-
-        def load(name, src, cols):
-            raw = sb.tile([P, PACK, cols.stop - cols.start], F32, name=name)
-            nc.sync.dma_start(out=raw[:], in_=by_slot(src)[:, :, cols])
+        def load(name, src):
+            raw = sb.tile(list(src.shape), F32, name=name)
+            nc.sync.dma_start(out=raw[:], in_=src)
             return raw
 
-        w_raw = [load("w1_raw", w1, slice(0, D))]
+        w1_raw = load("w1_raw", by_slot(w1))
         a_sb = sb.tile([P, PACK], F32, name="a_sb")
         nc.scalar.dma_start(out=a_sb[:], in_=a1.rearrange("g (p j) o -> (g p) (j o)", j=PACK))
         h_raw, x1_sb = [], []
         for hf in range(2):
             for dst, src, name in ((h_raw, h, "h_raw%d" % hf), (x1_sb, x1, "x1_sb%d" % hf)):
-                raw = load(name, src, half(hf))
+                raw = load(name, by_slot(src)[:, :, half(hf)])
                 dst.extend([raw[:, :, quarter(0)], raw[:, :, quarter(1)]])
-        w_raw.append(load("w2_raw", w2, slice(0, D)))
-        x2_sb = sb.tile([P, PACK, N], F32, name="x2_sb")
-        for sp in range(2):
-            nc.sync.dma_start(out=x2_sb[:, pair(sp), :], in_=by_slot(x2)[:, pair(sp), :])
+        w2_raw = load("w2_raw", by_slot(w2))
+        x2_sb = {g: load("x2_sb%d" % g, by_row(x2[g])) for g in heads}
 
-        w_codes, w_scales, w_dealt = [], [], []
-        for i in range(2):
-            codes = sb.tile([P, 6 * R], I32, name="w_codes%d" % i, align_bytes=64)
-            scales = sb.tile([P, 6 * R], U8, name="w_scales%d" % i, align_bytes=64)
-            nc.vector.memset(codes[:].rearrange("p (b m) -> p b m", m=R)[:, 0:6:5, :], 0)
-            nc.vector.memset(scales[:].bitcast(I32).rearrange("p (b m) -> p b m", b=6)[:, 0:6:5, :], 0)
-            w_codes.append(codes)
-            w_scales.append(scales)
-            w_dealt.append(sb.tile([P, PACK, R, PACK], BF16, name="w_dealt%d" % i, align_bytes=64))
+        w1_codes = sb.tile([P, 6 * R], I32, name="w1_codes", align_bytes=64)
+        w1_scales = sb.tile([P, 6 * R], U8, name="w1_scales", align_bytes=64)
+        nc.vector.memset(w1_codes[:].rearrange("p (b m) -> p b m", m=R)[:, 0:6:5, :], 0)
+        nc.vector.memset(w1_scales[:].bitcast(I32).rearrange("p (b m) -> p b m", b=6)[:, 0:6:5, :], 0)
+        w2_codes = sb.tile([P, D], I32, name="w2_codes", align_bytes=64)
+        w2_scales = sb.tile([P, D], U8, name="w2_scales", align_bytes=64)
+        w1_dealt = sb.tile([P, PACK, R, PACK], BF16, name="w1_dealt", align_bytes=64)
+        w2_dealt = sb.tile([P, ROWS, P, PACK], BF16, name="w2_dealt", align_bytes=64)
 
         def copy(eng, out, in_):
             if eng is nc.scalar:
@@ -85,19 +84,21 @@ def tile_rows_pl_steps_tanh_kernel(tc, h, w1, x1, a1, w2, x2, out_0, out_1, out_
             else:
                 nc.vector.tensor_copy(out=out, in_=in_)
 
-        def deal_w(i, eng, first, last):
+        def deal_w1(eng, first, last):
             copy(
                 eng,
-                w_dealt[i][:, :, first:last, :].rearrange("p x m j -> p m j x"),
-                w_raw[i][:, :, PACK * first : PACK * last].rearrange("p j (m x) -> p m j x", x=PACK),
+                w1_dealt[:, :, first:last, :].rearrange("p x m j -> p m j x"),
+                w1_raw[:, :, PACK * first : PACK * last].rearrange("p j (m x) -> p m j x", x=PACK),
             )
 
-        def quant_w(i):
-            nc.vector.quantize_mx(
-                out=w_codes[i][:, R : 5 * R].bitcast(FP8X4),
-                scales=w_scales[i][:, R : 5 * R],
-                in_=w_dealt[i][:].rearrange("p x m j -> p (x m j)"),
+        def deal_w2():
+            nc.scalar.copy(
+                out=w2_dealt[:].rearrange("p s (c i) j -> p c j i s", i=2),
+                in_=w2_raw[:].rearrange("p j (c i s) -> p c j i s", i=2, s=ROWS),
             )
+
+        def quantise(codes, scales, packed):
+            nc.vector.quantize_mx(out=codes.bitcast(FP8X4), scales=scales, in_=packed)
 
         def packed_walk(dst):
             return dst.rearrange("p (c i) j -> p c j i", i=RUN)
@@ -116,34 +117,33 @@ def tile_rows_pl_steps_tanh_kernel(tc, h, w1, x1, a1, w2, x2, out_0, out_1, out_
 
         def quant_moving(step, k):
             t = sb.tile([P, QUARTER + PLANE_WORDS], I32, name="moving%d_%d" % (step, k), align_bytes=64)
-            nc.vector.quantize_mx(
-                out=t[:, 0:QUARTER].bitcast(FP8X4),
-                scales=t[:, QUARTER:].bitcast(U8),
-                in_=(h_packed, h1_packed)[step][k][:].rearrange("p n j -> p (n j)"),
-            )
+            packed = (h_packed, h1_packed)[step][k]
+            quantise(t[:, 0:QUARTER], t[:, QUARTER:].bitcast(U8), packed[:].rearrange("p n j -> p (n j)"))
             moving[step, k] = t
 
-        def one_pass(out, step, k, g, x):
-            t = moving[step, k]
-            window = slice((x + 1 - g) * R, (x + 3 - g) * R)
+        def one_pass(out, codes, scales, window, t, g):
             nc.tensor.matmul_mx(
                 out=out,
-                lhsT=w_codes[step][rows[g], window].bitcast(FP8X4),
-                lhsT_scale=w_scales[step][rows[g], window],
+                lhsT=codes[rows[g], window].bitcast(FP8X4),
+                lhsT_scale=scales[rows[g], window],
                 rhs=t[rows[g], 0:QUARTER].bitcast(FP8X4),
                 rhs_scale=t[rows[g], QUARTER:].bitcast(U8),
                 start=True,
                 stop=True,
             )
 
+        def bank(name, shape, k, g):
+            return ps.tile(shape, F32, name="%s_%d_%d" % (name, k, g), tag="bank%d_%d" % (g, k))
+
         z1 = {}
         sum1 = [sb.tile([P, PACK, QUARTER], F32, name="sum1_%d" % k) for k in range(4)]
         tanh1 = [sb.tile([P, PACK, QUARTER], F32, name="tanh1_%d" % k) for k in range(4)]
 
         def product1(k, g):
-            z1[k, g] = ps.tile([P, PACK, QUARTER], F32, name="z1_%d_%d" % (k, g), tag="bank%d_%d" % (g, k))
+            z1[k, g] = bank("z1", [P, PACK, QUARTER], k, g)
             for x in range(PACK):
-                one_pass(z1[k, g][:, x, :], 0, k, g, x)
+                window = slice((x + 1 - g) * R, (x + 3 - g) * R)
+                one_pass(z1[k, g][:, x, :], w1_codes, w1_scales, window, moving[0, k], g)
 
         def add1(k, g):
             part = read[g]
@@ -160,73 +160,62 @@ def tile_rows_pl_steps_tanh_kernel(tc, h, w1, x1, a1, w2, x2, out_0, out_1, out_
                 op=MULT,
             )
 
-        z2 = {}
-        sum2 = [sb.tile([P, PACK, HALF], F32, name="sum2_%d" % hf) for hf in range(2)]
-        copied = [sb.tile([P, 2, HALF], F32, name="copied%d" % hf) for hf in range(2)]
-        y = sb.tile([P, PACK, N], F32, name="y")
+        def scale1_by_slot(k):
+            for j in range(PACK):
+                nc.scalar.mul(out=tanh1[k][:, j, :], in_=tanh1[k][:, j, :], mul=a_sb[:, j : j + 1])
+
+        def round_h1(k):
+            nc.vector.tensor_copy(out=packed_walk(h1_packed[k][:]), in_=flat_walk(tanh1[k][:]))
+
+        z2, sum2 = {}, {}
+        y = {g: sb.tile([P, ROWS, N], F32, name="y%d" % g) for g in heads}
+        moved = [sb.tile([P, 2, QUARTER], I32, name="moved%d" % k) for k in range(4)]
         words = sb.tile([P, N], I32, name="words", align_bytes=64)
         y_scales = sb.tile([P, N], U8, name="y_scales", align_bytes=64)
-        y_view = out_0.rearrange("(p j) n -> p j n", j=PACK)
         words_view = out_1[0].rearrange("p n j -> p (n j)").bitcast(I32)
         scales_view = out_2[0].bitcast(I32)
 
-        def product2(hf, sp, g, quarters=(0, 1)):
-            if (hf, sp, g) not in z2:
-                z2[hf, sp, g] = ps.tile(
-                    [P, 2, HALF], F32, name="z2_%d_%d_%d" % (hf, sp, g), tag="bank%d_%d" % (g, 2 * hf + sp)
-                )
-            for c in quarters:
-                for x in range(2):
-                    one_pass(z2[hf, sp, g][:, x, quarter(c)], 1, 2 * hf + c, g, 2 * sp + x)
+        def product2(k):
+            quant_moving(1, k)
+            for g in heads:
+                z2[k, g] = bank("z2", [P, ROWS, QUARTER], k, g)
+                for s in range(ROWS):
+                    one_pass(z2[k, g][:, s, :], w2_codes, w2_scales, slice(s * P, (s + 1) * P), moving[1, k], g)
 
-        def add2(hf, sp, g, first=0, last=HALF):
-            part = read[g]
-            nc.vector.tensor_tensor(
-                out=sum2[hf][part, pair(sp), first:last],
-                in0=z2[hf, sp, g][part, :, first:last],
-                in1=x2_sb[part, pair(sp), hf * HALF + first : hf * HALF + last],
-                op=ADD,
-            )
+        def add2(k, g):
+            sum2[k, g] = sb.tile([P, ROWS, QUARTER], F32, name="sum2_%d_%d" % (k, g))
+            nc.vector.tensor_tensor(out=sum2[k, g][:], in0=z2[k, g][:], in1=x2_sb[g][:, :, quarter(k)], op=ADD)
 
-        def copy_banks(hf, sp):
-            for g in (upper, lower):
-                nc.scalar.copy(out=copied[hf][rows[g]], in_=z2[hf, sp, g][rows[g]])
+        def act2(k, g):
+            nc.scalar.activation(out=y[g][:, :, quarter(k)], in_=sum2[k, g][:], func=TANH)
 
-        def add_copied(hf, sp):
-            nc.vector.tensor_tensor(
-                out=sum2[hf][:, pair(sp), :], in0=copied[hf][:], in1=x2_sb[:, pair(sp), half(hf)], op=ADD
-            )
+        def send_pairs(k, g):
+            pairs = sb.tile([P, QUARTER, ROWS], BF16, name="pairs%d_%d" % (k, g))
+            nc.scalar.activation(out=packed_walk(pairs[:]), in_=flat_walk(sum2[k, g][:]), func=TANH)
+            nc.sync.dma_start(out=moved[k][rows[g]], in_=pairs[:].rearrange("p n s -> p (n s)").bitcast(I32))
 
-        def act2(hf, sp, first=0, last=HALF):
-            nc.scalar.activation(
-                out=y[:, pair(sp), hf * HALF + first : hf * HALF + last],
-                in_=sum2[hf][:, pair(sp), first:last],
-                func=TANH,
-            )
-
-        def round_y(k):
-            nc.vector.tensor_copy(out=packed_walk(y_packed[k][:]), in_=flat_walk(y[:, :, quarter(k)]))
-
-        def act2_packed(k):
-            nc.scalar.activation(
-                out=packed_walk(y_packed[k][:]), in_=flat_walk(sum2[k // 2][:, :, quarter(k % 2)]), func=TANH
+        def join_pairs(k):
+            nc.vector.tensor_copy(
+                out=y_packed[k][:].rearrange("p n j -> p (n j)").bitcast(I32).rearrange("p (n u) -> p n u", u=2),
+                in_=moved[k][:].rearrange("p u n -> p n u"),
             )
 
         def quant_y(k):
-            nc.vector.quantize_mx(
-                out=words[:, quarter(k)].bitcast(FP8X4),
-                scales=y_scales[:, quarter(k)],
-                in_=y_packed[k][:].rearrange("p n j -> p (n j)"),
-            )
+            quantise(words[:, quarter(k)], y_scales[:, quarter(k)], y_packed[k][:].rearrange("p n j -> p (n j)"))
 
-        def store_y(hf, sp):
-            nc.sync.dma_start(out=y_view[:, pair(sp), half(hf)], in_=y[:, pair(sp), half(hf)])
+        def store_y(g, first, last):
+            cols = slice(first * QUARTER, last * QUARTER)
+            nc.sync.dma_start(out=by_row(out_0[g * D : (g + 1) * D, :])[:, :, cols], in_=y[g][:, :, cols])
+
+        def store_words(first, last):
+            cols = slice(first * QUARTER, last * QUARTER)
+            nc.scalar.dma_start(out=words_view[:, cols], in_=words[:, cols])
 
         vector, scalar, gpsimd = nc.vector, nc.scalar, nc.gpsimd
 
-        deal_w(0, vector, 0, W1_ON_VECTOR)
-        deal_w(0, scalar, W1_ON_VECTOR, R)
-        quant_w(0)
+        deal_w1(vector, 0, W1_ON_VECTOR)
+        deal_w1(scalar, W1_ON_VECTOR, R)
+        quantise(w1_codes[:, R : 5 * R], w1_scales[:, R : 5 * R], w1_dealt[:].rearrange("p x m j -> p (x m j)"))
         round_h(0, vector, 0, H0_ON_VECTOR)
         round_h(0, scalar, H0_ON_VECTOR, QUARTER)
         round_h(1, scalar)
@@ -252,55 +241,49 @@ def tile_rows_pl_steps_tanh_kernel(tc, h, w1, x1, a1, w2, x2, out_0, out_1, out_
         scale1(0, gpsimd)
         act1(1)
         scale1(1, gpsimd, 0, H1_ON_GPSIMD)
-        deal_w(1, scalar, 0, R)
+        deal_w2()
         for k in (2, 3):
             add1(k, upper)
         for k in (2, 3):
             add1(k, lower)
             act1(k)
 
+        scale1_by_slot(3)
+        quantise(w2_codes[:], w2_scales[:], w2_dealt[:].rearrange("p s q j -> p (s q j)"))
+        product2(0)
         scale1(1, vector, H1_ON_GPSIMD, QUARTER)
-        quant_w(1)
-        for c in (0, 1):
-            quant_moving(1, c)
-            product2(0, 1, upper, (c,))
-        product2(0, 1, lower)
-        product2(0, 0, upper)
-        product2(0, 0, lower)
+        scale1(2, vector)
+        product2(1)
+        for g in heads:
+            add2(0, g)
+        product2(2)
+        round_h1(3)
+        add2(1, upper)
+        product2(3)
+        add2(1, lower)
         for k in (2, 3):
-            scale1(k, vector)
-        copy_banks(0, 1)
-        for k in (2, 3):
-            quant_moving(1, k)
-        for sp in (0, 1):
-            product2(1, sp, upper)
-            product2(1, sp, lower)
-        add2(0, 0, upper)
-        add_copied(0, 1)
+            for g in heads:
+                add2(k, g)
 
-        copy_banks(1, 0)
-        act2(0, 1)
-        store_y(0, 1)
-        add2(0, 0, lower)
-        act2(0, 0)
-        store_y(0, 0)
-        add2(1, 1, upper)
-        add_copied(1, 0)
-        act2(1, 0)
-        store_y(1, 0)
-
-        for c in (0, 1):
-            add2(1, 1, lower, c * QUARTER, (c + 1) * QUARTER)
-        for k in (0, 1):
-            round_y(k)
-        for c in (0, 1):
-            act2(1, 1, c * QUARTER, (c + 1) * QUARTER)
-        act2_packed(3)
-        store_y(1, 1)
-        round_y(2)
         for k in range(4):
+            for g in heads:
+                send_pairs(k, g)
+            if k == 0:
+                for g in heads:
+                    act2(k, g)
+                    store_y(g, 0, 1)
+        for g in heads:
+            for k in (1, 2, 3):
+                act2(k, g)
+            store_y(g, 1, 4)
+
+        join_pairs(0)
+        for k in range(3):
+            join_pairs(k + 1)
             quant_y(k)
-        nc.scalar.dma_start(out=words_view, in_=words[:])
+        store_words(0, 3)
+        quant_y(3)
+        store_words(3, 4)
 
         for q, queue in enumerate((nc.sync, nc.sync, nc.scalar, nc.sync)):
             queue.dma_start(out=scales_view[4 * q : 4 * q + 4, :], in_=y_scales[32 * q : 32 * q + 4, :].bitcast(I32))

@@ -8,6 +8,7 @@ FLOPS = 2 * 2 * G * D * D * N
 F32 = mybir.dt.float32
 BF16 = mybir.dt.bfloat16
 I32 = mybir.dt.int32
+U32 = mybir.dt.uint32
 U8 = mybir.dt.uint8
 FP8X4 = mybir.dt.float8_e4m3fn_x4
 TANH = mybir.ActivationFunctionType.Tanh
@@ -21,6 +22,7 @@ ROWS = 2
 QUARTER = 128
 HALF = 2 * QUARTER
 PLANE_WORDS = QUARTER // 4
+WIDE = 2
 RUN = 4
 
 W1_ON_VECTOR = 40
@@ -67,7 +69,8 @@ def tile_rows_pl_steps_tanh_kernel(tc, h, w1, x1, a1, w2, x2, out_0, out_1, out_
                 raw = load(name, by_slot(src)[:, :, half(hf)])
                 dst.extend([raw[:, :, quarter(0)], raw[:, :, quarter(1)]])
         w2_raw = load("w2_raw", by_slot(w2))
-        x2_sb = {g: load("x2_sb%d" % g, by_row(x2[g])) for g in heads}
+        x2_sb = {g: load("x2_sb%d" % g, by_row(x2[g])[:, :, 0 : WIDE * QUARTER]) for g in heads}
+        x2_late = load("x2_late", by_slot(x2)[:, :, WIDE * QUARTER : N])
 
         w1_codes = sb.tile([P, 6 * R], I32, name="w1_codes", align_bytes=64)
         w1_scales = sb.tile([P, 6 * R], U8, name="w1_scales", align_bytes=64)
@@ -75,6 +78,11 @@ def tile_rows_pl_steps_tanh_kernel(tc, h, w1, x1, a1, w2, x2, out_0, out_1, out_
         nc.vector.memset(w1_scales[:].bitcast(I32).rearrange("p (b m) -> p b m", b=6)[:, 0:6:5, :], 0)
         w2_codes = sb.tile([P, D], I32, name="w2_codes", align_bytes=64)
         w2_scales = sb.tile([P, D], U8, name="w2_scales", align_bytes=64)
+        w2p_codes = sb.tile([P, 6 * R], I32, name="w2p_codes", align_bytes=64)
+        w2p_scales = sb.tile([P, 6 * R], U8, name="w2p_scales", align_bytes=64)
+        nc.vector.memset(w2p_codes[:].rearrange("p (b m) -> p b m", m=R)[:, 0:6:5, :], 0)
+        nc.vector.memset(w2p_scales[:].bitcast(I32).rearrange("p (b m) -> p b m", b=6)[:, 0:6:5, :], 0)
+        nc.vector.memset(w2_scales[:].bitcast(I32), 0)
         w1_dealt = sb.tile([P, PACK, R, PACK], BF16, name="w1_dealt", align_bytes=64)
         w2_dealt = sb.tile([P, ROWS, P, PACK], BF16, name="w2_dealt", align_bytes=64)
 
@@ -95,6 +103,18 @@ def tile_rows_pl_steps_tanh_kernel(tc, h, w1, x1, a1, w2, x2, out_0, out_1, out_
             nc.scalar.copy(
                 out=w2_dealt[:].rearrange("p s (c i) j -> p c j i s", i=2),
                 in_=w2_raw[:].rearrange("p j (c i s) -> p c j i s", i=2, s=ROWS),
+            )
+
+        def regroup_codes():
+            nc.scalar.copy(
+                out=w2p_codes[:, R : 5 * R].bitcast(U32).rearrange("p (u s m) -> p s m u", u=2, s=ROWS),
+                in_=w2_codes[:].bitcast(U32).rearrange("p (s m u) -> p s m u", s=ROWS, u=2),
+            )
+
+        def regroup_scales():
+            nc.vector.tensor_copy(
+                out=w2p_scales[:, R : 5 * R].rearrange("p (u s m) -> p s m u", u=2, s=ROWS),
+                in_=w2_scales[:].rearrange("p (s m u) -> p s m u", s=ROWS, u=2),
             )
 
         def quantise(codes, scales, packed):
@@ -168,8 +188,10 @@ def tile_rows_pl_steps_tanh_kernel(tc, h, w1, x1, a1, w2, x2, out_0, out_1, out_
             nc.vector.tensor_copy(out=packed_walk(h1_packed[k][:]), in_=flat_walk(tanh1[k][:]))
 
         z2, sum2 = {}, {}
-        y = {g: sb.tile([P, ROWS, N], F32, name="y%d" % g) for g in heads}
-        moved = [sb.tile([P, 2, QUARTER], I32, name="moved%d" % k) for k in range(4)]
+        y = {g: sb.tile([P, ROWS, WIDE * QUARTER], F32, name="y%d" % g) for g in heads}
+        y_late = sb.tile([P, PACK, N - WIDE * QUARTER], F32, name="y_late")
+        sum_late = sb.tile([P, PACK, N - WIDE * QUARTER], F32, name="sum_late")
+        moved = [sb.tile([P, 2, QUARTER], I32, name="moved%d" % k) for k in range(WIDE)]
         words = sb.tile([P, N], I32, name="words", align_bytes=64)
         y_scales = sb.tile([P, N], U8, name="y_scales", align_bytes=64)
         words_view = out_1[0].rearrange("p n j -> p (n j)").bitcast(I32)
@@ -193,6 +215,35 @@ def tile_rows_pl_steps_tanh_kernel(tc, h, w1, x1, a1, w2, x2, out_0, out_1, out_
             pairs = sb.tile([P, QUARTER, ROWS], BF16, name="pairs%d_%d" % (k, g))
             nc.scalar.activation(out=packed_walk(pairs[:]), in_=flat_walk(sum2[k, g][:]), func=TANH)
             nc.sync.dma_start(out=moved[k][rows[g]], in_=pairs[:].rearrange("p n s -> p (n s)").bitcast(I32))
+
+        def product2p(k, g):
+            z2[k, g] = bank("z2", [P, PACK, QUARTER], k, g)
+            for x in range(PACK):
+                window = slice((x + 1 - g) * R, (x + 3 - g) * R)
+                one_pass(z2[k, g][:, x, :], w2p_codes, w2p_scales, window, moving[1, k], g)
+
+        def add2p(k, g, s0=0, s1=PACK):
+            part = read[g]
+            nc.vector.tensor_tensor(
+                out=sum_late[part, s0:s1, quarter(k - WIDE)],
+                in0=z2[k, g][part, s0:s1, :],
+                in1=x2_late[part, s0:s1, quarter(k - WIDE)],
+                op=ADD,
+            )
+
+        def act2p(k, s0=0, s1=PACK):
+            nc.scalar.activation(
+                out=y_late[:, s0:s1, quarter(k - WIDE)], in_=sum_late[:, s0:s1, quarter(k - WIDE)], func=TANH
+            )
+
+        def round_y(k):
+            nc.vector.tensor_copy(out=packed_walk(y_packed[k][:]), in_=flat_walk(y_late[:, :, quarter(k - WIDE)]))
+
+        def store_late(first, last, s0=0, s1=PACK):
+            nc.sync.dma_start(
+                out=out_0.rearrange("(p j) n -> p j n", j=PACK)[:, s0:s1, first * QUARTER : last * QUARTER],
+                in_=y_late[:, s0:s1, (first - WIDE) * QUARTER : (last - WIDE) * QUARTER],
+            )
 
         def join_pairs(k):
             nc.vector.tensor_copy(
@@ -253,37 +304,50 @@ def tile_rows_pl_steps_tanh_kernel(tc, h, w1, x1, a1, w2, x2, out_0, out_1, out_
         product2(0)
         scale1(1, vector, H1_ON_GPSIMD, QUARTER)
         scale1(2, vector)
+        regroup_codes()
         product2(1)
+        regroup_scales()
+        quant_moving(1, 2)
         for g in heads:
-            add2(0, g)
-        product2(2)
+            product2p(2, g)
+        add2(0, upper)
         round_h1(3)
-        add2(1, upper)
-        product2(3)
-        add2(1, lower)
-        for k in (2, 3):
-            for g in heads:
-                add2(k, g)
-
-        for k in range(4):
-            for g in heads:
-                send_pairs(k, g)
-            if k == 0:
-                for g in heads:
-                    act2(k, g)
-                    store_y(g, 0, 1)
+        add2(0, lower)
+        quant_moving(1, 3)
         for g in heads:
-            for k in (1, 2, 3):
-                act2(k, g)
-            store_y(g, 1, 4)
+            product2p(3, g)
+        for g in heads:
+            add2(1, g)
+        for k in (2, 3):
+            add2p(k, upper)
+        add2p(2, lower)
+        for s0 in (0, 2):
+            add2p(3, lower, s0, s0 + 2)
+
+        send_pairs(0, upper)
+        act2(0, upper)
+        send_pairs(0, lower)
+        for g in heads:
+            send_pairs(1, g)
+        act2(1, upper)
+        store_y(upper, 0, 2)
+        for k in (0, 1):
+            act2(k, lower)
+        store_y(lower, 0, 2)
+        act2p(2)
+        for s0 in (0, 2):
+            act2p(3, s0, s0 + 2)
+            store_late(2, 4, s0, s0 + 2)
 
         join_pairs(0)
-        for k in range(3):
-            join_pairs(k + 1)
+        quant_y(0)
+        join_pairs(1)
+        round_y(2)
+        quant_y(1)
+        round_y(3)
+        for k in (2, 3):
             quant_y(k)
-        store_words(0, 3)
-        quant_y(3)
-        store_words(3, 4)
+        store_words(0, 4)
 
         for q, queue in enumerate((nc.sync, nc.sync, nc.scalar, nc.sync)):
             queue.dma_start(out=scales_view[4 * q : 4 * q + 4, :], in_=y_scales[32 * q : 32 * q + 4, :].bitcast(I32))

@@ -63,14 +63,25 @@ def tile_rows_pl_steps_tanh_kernel(tc, h, w1, x1, a1, w2, x2, out_0, out_1, out_
         w1_raw = load("w1_raw", by_slot(w1))
         a_sb = sb.tile([P, PACK], F32, name="a_sb")
         nc.scalar.dma_start(out=a_sb[:], in_=a1.rearrange("g (p j) o -> (g p) (j o)", j=PACK))
-        h_raw, x1_sb = [], []
-        for hf in range(2):
-            for dst, src, name in ((h_raw, h, "h_raw%d" % hf), (x1_sb, x1, "x1_sb%d" % hf)):
-                raw = load(name, by_slot(src)[:, :, half(hf)])
-                dst.extend([raw[:, :, quarter(0)], raw[:, :, quarter(1)]])
+        a_wide = sb.tile([P, G, ROWS], F32, name="a_wide")
+        nc.scalar.dma_start(out=a_wide[:], in_=a1.rearrange("g (q s) o -> q g (s o)", s=ROWS))
+        h_raw, x1_sb = {}, {}
+        raw = load("h_raw0", by_slot(h)[:, :, half(0)])
+        h_raw[0], h_raw[1] = raw[:, :, quarter(0)], raw[:, :, quarter(1)]
+        raw = load("h_raw1", by_slot(h)[:, :, half(1)])
+        h_raw[2], h_raw[3] = raw[:, :, quarter(0)], raw[:, :, quarter(1)]
+        x1_wide = {g: load("x1_wide%d" % g, by_row(x1[g])[:, :, half(0)]) for g in heads}
+        raw = load("x1_sb1", by_slot(x1)[:, :, half(1)])
+        x1_sb[2], x1_sb[3] = raw[:, :, quarter(0)], raw[:, :, quarter(1)]
         w2_raw = load("w2_raw", by_slot(w2))
-        x2_sb = {g: load("x2_sb%d" % g, by_row(x2[g])[:, :, 0 : WIDE * QUARTER]) for g in heads}
-        x2_late = load("x2_late", by_slot(x2)[:, :, WIDE * QUARTER : N])
+        x2_sb, late = {}, {}
+
+        def load_x2(g):
+            x2_sb[g] = load("x2_sb%d" % g, by_row(x2[g])[:, :, 0 : WIDE * QUARTER])
+
+        def load_x2_late():
+            late["x2"] = load("x2_late", by_slot(x2)[:, :, WIDE * QUARTER : N])
+
 
         w1_codes = sb.tile([P, 6 * R], I32, name="w1_codes", align_bytes=64)
         w1_scales = sb.tile([P, 6 * R], U8, name="w1_scales", align_bytes=64)
@@ -83,7 +94,10 @@ def tile_rows_pl_steps_tanh_kernel(tc, h, w1, x1, a1, w2, x2, out_0, out_1, out_
         nc.vector.memset(w2p_codes[:].rearrange("p (b m) -> p b m", m=R)[:, 0:6:5, :], 0)
         nc.vector.memset(w2p_scales[:].bitcast(I32).rearrange("p (b m) -> p b m", b=6)[:, 0:6:5, :], 0)
         nc.vector.memset(w2_scales[:].bitcast(I32), 0)
-        w1_dealt = sb.tile([P, PACK, R, PACK], BF16, name="w1_dealt", align_bytes=64)
+        w1w_codes = sb.tile([P, D], I32, name="w1w_codes", align_bytes=64)
+        w1w_scales = sb.tile([P, D], U8, name="w1w_scales", align_bytes=64)
+        nc.vector.memset(w1w_scales[:].bitcast(I32), 0)
+        w1_dealt = sb.tile([P, ROWS, P, PACK], BF16, name="w1_dealt", align_bytes=64)
         w2_dealt = sb.tile([P, ROWS, P, PACK], BF16, name="w2_dealt", align_bytes=64)
 
         def copy(eng, out, in_):
@@ -92,29 +106,24 @@ def tile_rows_pl_steps_tanh_kernel(tc, h, w1, x1, a1, w2, x2, out_0, out_1, out_
             else:
                 nc.vector.tensor_copy(out=out, in_=in_)
 
-        def deal_w1(eng, first, last):
-            copy(
-                eng,
-                w1_dealt[:, :, first:last, :].rearrange("p x m j -> p m j x"),
-                w1_raw[:, :, PACK * first : PACK * last].rearrange("p j (m x) -> p m j x", x=PACK),
-            )
+        def deal(i, eng, first, last, s0=0, s1=ROWS):
+            out = (w1_dealt, w2_dealt)[i][:].rearrange("p s (c i) j -> p c j i s", i=2)[:, first:last, :, :, s0:s1]
+            in_ = (w1_raw, w2_raw)[i][:].rearrange("p j (c i s) -> p c j i s", i=2, s=ROWS)[:, first:last, :, :, s0:s1]
+            copy(eng, out, in_)
 
-        def deal_w2():
+        def quant_w(i):
+            quantise((w1w_codes, w2_codes)[i][:], (w1w_scales, w2_scales)[i][:], (w1_dealt, w2_dealt)[i][:].rearrange("p s q j -> p (s q j)"))
+
+        def regroup_codes(i):
             nc.scalar.copy(
-                out=w2_dealt[:].rearrange("p s (c i) j -> p c j i s", i=2),
-                in_=w2_raw[:].rearrange("p j (c i s) -> p c j i s", i=2, s=ROWS),
+                out=(w1_codes, w2p_codes)[i][:, R : 5 * R].bitcast(U32).rearrange("p (u s m) -> p s m u", u=2, s=ROWS),
+                in_=(w1w_codes, w2_codes)[i][:].bitcast(U32).rearrange("p (s m u) -> p s m u", s=ROWS, u=2),
             )
 
-        def regroup_codes():
-            nc.scalar.copy(
-                out=w2p_codes[:, R : 5 * R].bitcast(U32).rearrange("p (u s m) -> p s m u", u=2, s=ROWS),
-                in_=w2_codes[:].bitcast(U32).rearrange("p (s m u) -> p s m u", s=ROWS, u=2),
-            )
-
-        def regroup_scales():
+        def regroup_scales(i):
             nc.vector.tensor_copy(
-                out=w2p_scales[:, R : 5 * R].rearrange("p (u s m) -> p s m u", u=2, s=ROWS),
-                in_=w2_scales[:].rearrange("p (s m u) -> p s m u", s=ROWS, u=2),
+                out=(w1_scales, w2p_scales)[i][:, R : 5 * R].rearrange("p (u s m) -> p s m u", u=2, s=ROWS),
+                in_=(w1w_scales, w2_scales)[i][:].rearrange("p (s m u) -> p s m u", s=ROWS, u=2),
             )
 
         def quantise(codes, scales, packed):
@@ -187,6 +196,45 @@ def tile_rows_pl_steps_tanh_kernel(tc, h, w1, x1, a1, w2, x2, out_0, out_1, out_
         def round_h1(k):
             nc.vector.tensor_copy(out=packed_walk(h1_packed[k][:]), in_=flat_walk(tanh1[k][:]))
 
+        sum1w, tanh1w = {}, {}
+        moved1 = [sb.tile([P, 2, QUARTER], I32, name="moved1_%d" % k) for k in range(2)]
+
+        def product1w(k):
+            for g in heads:
+                z1[k, g] = bank("z1", [P, ROWS, QUARTER], k, g)
+                for s in range(ROWS):
+                    one_pass(z1[k, g][:, s, :], w1w_codes, w1w_scales, slice(s * P, (s + 1) * P), moving[0, k], g)
+
+        def add1w(k, g):
+            sum1w[k, g] = sb.tile([P, ROWS, QUARTER], F32, name="sum1w_%d_%d" % (k, g))
+            nc.vector.tensor_tensor(out=sum1w[k, g][:], in0=z1[k, g][:], in1=x1_wide[g][:, :, quarter(k)], op=ADD)
+
+        def act1w(k, g):
+            tanh1w[k, g] = sb.tile([P, ROWS, QUARTER], F32, name="tanh1w_%d_%d" % (k, g))
+            nc.scalar.activation(out=tanh1w[k, g][:], in_=sum1w[k, g][:], func=TANH)
+
+        pairs1 = {}
+
+        def scale1w(k, g, eng):
+            pairs = pairs1[k, g] = sb.tile([P, QUARTER, ROWS], BF16, name="pairs1_%d_%d" % (k, g))
+            eng.tensor_tensor(
+                out=packed_walk(pairs[:]),
+                in0=flat_walk(tanh1w[k, g][:]),
+                in1=a_wide[:, g, :].unsqueeze(1).unsqueeze(3).to_broadcast([P, QUARTER // RUN, ROWS, RUN]),
+                op=MULT,
+            )
+
+        def move1(k, g):
+            nc.sync.dma_start(out=moved1[k][rows[g]], in_=pairs1[k, g][:].rearrange("p n s -> p (n s)").bitcast(I32))
+
+        def join1(k, eng):
+            word = U32 if eng is nc.scalar else I32
+            copy(
+                eng,
+                h1_packed[k][:].rearrange("p n j -> p (n j)").bitcast(word).rearrange("p (n u) -> p n u", u=2),
+                moved1[k][:].bitcast(word).rearrange("p u n -> p n u"),
+            )
+
         z2, sum2 = {}, {}
         y = {g: sb.tile([P, ROWS, WIDE * QUARTER], F32, name="y%d" % g) for g in heads}
         y_late = sb.tile([P, PACK, N - WIDE * QUARTER], F32, name="y_late")
@@ -198,7 +246,6 @@ def tile_rows_pl_steps_tanh_kernel(tc, h, w1, x1, a1, w2, x2, out_0, out_1, out_
         scales_view = out_2[0].bitcast(I32)
 
         def product2(k):
-            quant_moving(1, k)
             for g in heads:
                 z2[k, g] = bank("z2", [P, ROWS, QUARTER], k, g)
                 for s in range(ROWS):
@@ -227,7 +274,7 @@ def tile_rows_pl_steps_tanh_kernel(tc, h, w1, x1, a1, w2, x2, out_0, out_1, out_
             nc.vector.tensor_tensor(
                 out=sum_late[part, s0:s1, quarter(k - WIDE)],
                 in0=z2[k, g][part, s0:s1, :],
-                in1=x2_late[part, s0:s1, quarter(k - WIDE)],
+                in1=late["x2"][part, s0:s1, quarter(k - WIDE)],
                 op=ADD,
             )
 
@@ -236,8 +283,9 @@ def tile_rows_pl_steps_tanh_kernel(tc, h, w1, x1, a1, w2, x2, out_0, out_1, out_
                 out=y_late[:, s0:s1, quarter(k - WIDE)], in_=sum_late[:, s0:s1, quarter(k - WIDE)], func=TANH
             )
 
-        def round_y(k):
-            nc.vector.tensor_copy(out=packed_walk(y_packed[k][:]), in_=flat_walk(y_late[:, :, quarter(k - WIDE)]))
+        def round_y(k, eng=nc.vector, first=0, last=QUARTER):
+            o = (k - WIDE) * QUARTER
+            copy(eng, packed_walk(y_packed[k][:, first:last, :]), flat_walk(y_late[:, :, o + first : o + last]))
 
         def store_late(first, last, s0=0, s1=PACK):
             nc.sync.dma_start(
@@ -245,10 +293,12 @@ def tile_rows_pl_steps_tanh_kernel(tc, h, w1, x1, a1, w2, x2, out_0, out_1, out_
                 in_=y_late[:, s0:s1, (first - WIDE) * QUARTER : (last - WIDE) * QUARTER],
             )
 
-        def join_pairs(k):
-            nc.vector.tensor_copy(
-                out=y_packed[k][:].rearrange("p n j -> p (n j)").bitcast(I32).rearrange("p (n u) -> p n u", u=2),
-                in_=moved[k][:].rearrange("p u n -> p n u"),
+        def join_pairs(k, eng=nc.vector):
+            word = U32 if eng is nc.scalar else I32
+            copy(
+                eng,
+                y_packed[k][:].rearrange("p n j -> p (n j)").bitcast(word).rearrange("p (n u) -> p n u", u=2),
+                moved[k][:].bitcast(word).rearrange("p u n -> p n u"),
             )
 
         def quant_y(k):
@@ -264,90 +314,103 @@ def tile_rows_pl_steps_tanh_kernel(tc, h, w1, x1, a1, w2, x2, out_0, out_1, out_
 
         vector, scalar, gpsimd = nc.vector, nc.scalar, nc.gpsimd
 
-        deal_w1(vector, 0, W1_ON_VECTOR)
-        deal_w1(scalar, W1_ON_VECTOR, R)
-        quantise(w1_codes[:, R : 5 * R], w1_scales[:, R : 5 * R], w1_dealt[:].rearrange("p x m j -> p (x m j)"))
+        deal(0, vector, 0, 40)
+        deal(0, scalar, 40, R)
+        quant_w(0)
         round_h(0, vector, 0, H0_ON_VECTOR)
         round_h(0, scalar, H0_ON_VECTOR, QUARTER)
         round_h(1, scalar)
-        for k in (0, 1):
-            quant_moving(0, k)
-            product1(k, upper)
-        for k in (0, 1):
-            product1(k, lower)
-        for k in (0, 1):
-            add1(k, upper)
-        round_h(2, scalar)
-        round_h(3, scalar, 0, H3_ON_SCALAR)
-        add1(0, lower)
-        round_h(3, vector, H3_ON_SCALAR, QUARTER)
-        act1(0)
-
+        quant_moving(0, 0)
+        product1w(0)
+        regroup_scales(0)
+        regroup_codes(0)
+        quant_moving(0, 1)
+        product1w(1)
+        round_h(2, vector)
+        round_h(3, scalar)
+        quant_moving(0, 2)
+        add1w(0, upper)
+        quant_moving(0, 3)
+        add1w(1, upper)
         for k in (2, 3):
-            quant_moving(0, k)
             product1(k, upper)
         for k in (2, 3):
             product1(k, lower)
-        add1(1, lower)
-        scale1(0, gpsimd)
-        act1(1)
-        scale1(1, gpsimd, 0, H1_ON_GPSIMD)
-        deal_w2()
+        add1w(0, lower)
+        add1w(1, lower)
+        for g in heads:
+            for k in (0, 1):
+                act1w(k, g)
+        load_x2(upper)
+        scale1w(0, upper, vector)
+        scale1w(1, upper, vector)
+        scale1w(0, lower, vector)
+        scale1w(1, lower, gpsimd)
+        for k in (0, 1):
+            for g in heads:
+                move1(k, g)
+        load_x2(lower)
+        load_x2_late()
+        deal(1, scalar, 0, R)
         for k in (2, 3):
             add1(k, upper)
         for k in (2, 3):
             add1(k, lower)
             act1(k)
-
+        quant_w(1)
+        join1(0, vector)
+        regroup_codes(1)
         scale1_by_slot(3)
-        quantise(w2_codes[:], w2_scales[:], w2_dealt[:].rearrange("p s q j -> p (s q j)"))
+        regroup_scales(1)
+        quant_moving(1, 0)
         product2(0)
-        scale1(1, vector, H1_ON_GPSIMD, QUARTER)
         scale1(2, vector)
-        regroup_codes()
-        product2(1)
-        regroup_scales()
+        join1(1, vector)
         quant_moving(1, 2)
-        for g in heads:
-            product2p(2, g)
+        quant_moving(1, 1)
+        product2(1)
+        product2p(2, upper)
         add2(0, upper)
         round_h1(3)
         add2(0, lower)
         quant_moving(1, 3)
-        for g in heads:
-            product2p(3, g)
-        for g in heads:
-            add2(1, g)
+        product2p(3, upper)
+        product2p(2, lower)
+        product2p(3, lower)
+        add2(1, upper)
+        add2(1, lower)
         for k in (2, 3):
             add2p(k, upper)
-        add2p(2, lower)
-        for s0 in (0, 2):
-            add2p(3, lower, s0, s0 + 2)
-
+        add2p(2, lower, 0, 2)
+        add2p(2, lower, 2, 4)
+        add2p(3, lower, 0, 2)
+        add2p(3, lower, 2, 4)
         send_pairs(0, upper)
         act2(0, upper)
         send_pairs(0, lower)
-        for g in heads:
-            send_pairs(1, g)
+        send_pairs(1, upper)
+        send_pairs(1, lower)
         act2(1, upper)
         store_y(upper, 0, 2)
-        for k in (0, 1):
-            act2(k, lower)
+        act2(0, lower)
+        act2(1, lower)
         store_y(lower, 0, 2)
-        act2p(2)
-        for s0 in (0, 2):
-            act2p(3, s0, s0 + 2)
-            store_late(2, 4, s0, s0 + 2)
-
+        act2p(2, 0, 2)
+        act2p(2, 2, 4)
+        act2p(3, 0, 2)
+        store_late(2, 4, 0, 2)
+        act2p(3, 2, 4)
+        store_late(2, 4, 2, 4)
         join_pairs(0)
-        quant_y(0)
-        join_pairs(1)
         round_y(2)
-        quant_y(1)
+        join_pairs(1)
+        quant_y(0)
         round_y(3)
-        for k in (2, 3):
-            quant_y(k)
-        store_words(0, 4)
+        quant_y(1)
+        quant_y(2)
+        store_words(0, 3)
+        quant_y(3)
+        store_words(3, 4)
 
         for q, queue in enumerate((nc.sync, nc.sync, nc.scalar, nc.sync)):
             queue.dma_start(out=scales_view[4 * q : 4 * q + 4, :], in_=y_scales[32 * q : 32 * q + 4, :].bitcast(I32))

@@ -22,17 +22,16 @@ ROWS = 2
 QUARTER = 128
 HALF = 2 * QUARTER
 PLANE_WORDS = QUARTER // 4
-WIDE = 2
 RUN = 4
+WIDE, PACKED = (0, 1), (2, 3)
 
 W1_ON_VECTOR = 40
 H0_ON_VECTOR = 88
-H3_ON_SCALAR = 64
-H1_ON_GPSIMD = 64
 
 
 def tile_rows_pl_steps_tanh_kernel(tc, h, w1, x1, a1, w2, x2, out_0, out_1, out_2):
     nc = tc.nc
+    vector, scalar, gpsimd = nc.vector, nc.scalar, nc.gpsimd
     rows = [slice(0, R), slice(R, P)]
     read = [slice(0, R), slice(0, P)]
     upper, lower = 1, 0
@@ -55,79 +54,72 @@ def tile_rows_pl_steps_tanh_kernel(tc, h, w1, x1, a1, w2, x2, out_0, out_1, out_
         def half(hf):
             return slice(hf * HALF, (hf + 1) * HALF)
 
+        def copy(eng, out, in_):
+            if eng is scalar:
+                scalar.copy(out=out, in_=in_)
+            else:
+                vector.tensor_copy(out=out, in_=in_)
+
         def load(name, src):
             raw = sb.tile(list(src.shape), F32, name=name)
             nc.sync.dma_start(out=raw[:], in_=src)
             return raw
 
-        w1_raw = load("w1_raw", by_slot(w1))
-        a_sb = sb.tile([P, PACK], F32, name="a_sb")
-        nc.scalar.dma_start(out=a_sb[:], in_=a1.rearrange("g (p j) o -> (g p) (j o)", j=PACK))
+        x = {}
+
+        def load_wide(step, g):
+            x[step, g] = load("x%d_wide%d" % (step, g), by_row((x1, x2)[step][g])[:, :, half(0)])
+
+        def load_packed(step):
+            x[step] = load("x%d_packed" % step, by_slot((x1, x2)[step])[:, :, half(1)])
+
+        w_raw = [load("w1_raw", by_slot(w1))]
+        a_packed = sb.tile([P, PACK], F32, name="a_packed")
+        scalar.dma_start(out=a_packed[:], in_=a1.rearrange("g (p j) o -> (g p) (j o)", j=PACK))
         a_wide = sb.tile([P, G, ROWS], F32, name="a_wide")
-        nc.scalar.dma_start(out=a_wide[:], in_=a1.rearrange("g (q s) o -> q g (s o)", s=ROWS))
-        h_raw, x1_sb = {}, {}
-        raw = load("h_raw0", by_slot(h)[:, :, half(0)])
-        h_raw[0], h_raw[1] = raw[:, :, quarter(0)], raw[:, :, quarter(1)]
-        raw = load("h_raw1", by_slot(h)[:, :, half(1)])
-        h_raw[2], h_raw[3] = raw[:, :, quarter(0)], raw[:, :, quarter(1)]
-        x1_wide = {g: load("x1_wide%d" % g, by_row(x1[g])[:, :, half(0)]) for g in heads}
-        raw = load("x1_sb1", by_slot(x1)[:, :, half(1)])
-        x1_sb[2], x1_sb[3] = raw[:, :, quarter(0)], raw[:, :, quarter(1)]
-        w2_raw = load("w2_raw", by_slot(w2))
-        x2_sb, late = {}, {}
+        scalar.dma_start(out=a_wide[:], in_=a1.rearrange("g (q s) o -> q g (s o)", s=ROWS))
+        h_raw = [load("h_raw%d" % hf, by_slot(h)[:, :, half(hf)]) for hf in range(2)]
+        for g in heads:
+            load_wide(0, g)
+        load_packed(0)
+        w_raw.append(load("w2_raw", by_slot(w2)))
 
-        def load_x2(g):
-            x2_sb[g] = load("x2_sb%d" % g, by_row(x2[g])[:, :, 0 : WIDE * QUARTER])
-
-        def load_x2_late():
-            late["x2"] = load("x2_late", by_slot(x2)[:, :, WIDE * QUARTER : N])
-
-
-        w1_codes = sb.tile([P, 6 * R], I32, name="w1_codes", align_bytes=64)
-        w1_scales = sb.tile([P, 6 * R], U8, name="w1_scales", align_bytes=64)
-        nc.vector.memset(w1_codes[:].rearrange("p (b m) -> p b m", m=R)[:, 0:6:5, :], 0)
-        nc.vector.memset(w1_scales[:].bitcast(I32).rearrange("p (b m) -> p b m", b=6)[:, 0:6:5, :], 0)
-        w2_codes = sb.tile([P, D], I32, name="w2_codes", align_bytes=64)
-        w2_scales = sb.tile([P, D], U8, name="w2_scales", align_bytes=64)
-        w2p_codes = sb.tile([P, 6 * R], I32, name="w2p_codes", align_bytes=64)
-        w2p_scales = sb.tile([P, 6 * R], U8, name="w2p_scales", align_bytes=64)
-        nc.vector.memset(w2p_codes[:].rearrange("p (b m) -> p b m", m=R)[:, 0:6:5, :], 0)
-        nc.vector.memset(w2p_scales[:].bitcast(I32).rearrange("p (b m) -> p b m", b=6)[:, 0:6:5, :], 0)
-        nc.vector.memset(w2_scales[:].bitcast(I32), 0)
-        w1w_codes = sb.tile([P, D], I32, name="w1w_codes", align_bytes=64)
-        w1w_scales = sb.tile([P, D], U8, name="w1w_scales", align_bytes=64)
-        nc.vector.memset(w1w_scales[:].bitcast(I32), 0)
-        w1_dealt = sb.tile([P, ROWS, P, PACK], BF16, name="w1_dealt", align_bytes=64)
-        w2_dealt = sb.tile([P, ROWS, P, PACK], BF16, name="w2_dealt", align_bytes=64)
-
-        def copy(eng, out, in_):
-            if eng is nc.scalar:
-                nc.scalar.copy(out=out, in_=in_)
-            else:
-                nc.vector.tensor_copy(out=out, in_=in_)
-
-        def deal(i, eng, first, last, s0=0, s1=ROWS):
-            out = (w1_dealt, w2_dealt)[i][:].rearrange("p s (c i) j -> p c j i s", i=2)[:, first:last, :, :, s0:s1]
-            in_ = (w1_raw, w2_raw)[i][:].rearrange("p j (c i s) -> p c j i s", i=2, s=ROWS)[:, first:last, :, :, s0:s1]
-            copy(eng, out, in_)
-
-        def quant_w(i):
-            quantise((w1w_codes, w2_codes)[i][:], (w1w_scales, w2_scales)[i][:], (w1_dealt, w2_dealt)[i][:].rearrange("p s q j -> p (s q j)"))
-
-        def regroup_codes(i):
-            nc.scalar.copy(
-                out=(w1_codes, w2p_codes)[i][:, R : 5 * R].bitcast(U32).rearrange("p (u s m) -> p s m u", u=2, s=ROWS),
-                in_=(w1w_codes, w2_codes)[i][:].bitcast(U32).rearrange("p (s m u) -> p s m u", s=ROWS, u=2),
-            )
-
-        def regroup_scales(i):
-            nc.vector.tensor_copy(
-                out=(w1_scales, w2p_scales)[i][:, R : 5 * R].rearrange("p (u s m) -> p s m u", u=2, s=ROWS),
-                in_=(w1w_scales, w2_scales)[i][:].rearrange("p (s m u) -> p s m u", s=ROWS, u=2),
-            )
+        dealt, wide_codes, wide_scales, packed_codes, packed_scales = [], [], [], [], []
+        for i in range(2):
+            dealt.append(sb.tile([P, ROWS, P, PACK], BF16, name="dealt%d" % i, align_bytes=64))
+            wide_codes.append(sb.tile([P, D], I32, name="wide_codes%d" % i, align_bytes=64))
+            wide_scales.append(sb.tile([P, D], U8, name="wide_scales%d" % i, align_bytes=64))
+            packed_codes.append(sb.tile([P, 6 * R], I32, name="packed_codes%d" % i, align_bytes=64))
+            packed_scales.append(sb.tile([P, 6 * R], U8, name="packed_scales%d" % i, align_bytes=64))
+            vector.memset(packed_codes[i][:].rearrange("p (b m) -> p b m", m=R)[:, 0:6:5, :], 0)
+            vector.memset(packed_scales[i][:].bitcast(I32).rearrange("p (b m) -> p b m", b=6)[:, 0:6:5, :], 0)
+            vector.memset(wide_scales[i][:].bitcast(I32), 0)
 
         def quantise(codes, scales, packed):
-            nc.vector.quantize_mx(out=codes.bitcast(FP8X4), scales=scales, in_=packed)
+            vector.quantize_mx(out=codes.bitcast(FP8X4), scales=scales, in_=packed)
+
+        def deal(i, eng, first, last):
+            copy(
+                eng,
+                dealt[i][:].rearrange("p s (c i) j -> p c j i s", i=2)[:, first:last],
+                w_raw[i][:].rearrange("p j (c i s) -> p c j i s", i=2, s=ROWS)[:, first:last],
+            )
+
+        def quant_w(i):
+            quantise(wide_codes[i][:], wide_scales[i][:], dealt[i][:].rearrange("p s q j -> p (s q j)"))
+
+        def regroup(eng, packed, wide):
+            copy(
+                eng,
+                packed.rearrange("p (u s m) -> p s m u", u=2, s=ROWS),
+                wide.rearrange("p (s m u) -> p s m u", s=ROWS, u=2),
+            )
+
+        def regroup_codes(i):
+            regroup(scalar, packed_codes[i][:, R : 5 * R].bitcast(U32), wide_codes[i][:].bitcast(U32))
+
+        def regroup_scales(i):
+            regroup(vector, packed_scales[i][:, R : 5 * R], wide_scales[i][:])
 
         def packed_walk(dst):
             return dst.rearrange("p (c i) j -> p c j i", i=RUN)
@@ -135,282 +127,235 @@ def tile_rows_pl_steps_tanh_kernel(tc, h, w1, x1, a1, w2, x2, out_0, out_1, out_
         def flat_walk(src):
             return src.rearrange("p j (c i) -> p c j i", i=RUN)
 
-        def packed_tiles(name):
-            return [sb.tile([P, QUARTER, PACK], BF16, name="%s%d" % (name, k), align_bytes=64) for k in range(4)]
-
-        h_packed, h1_packed, y_packed = packed_tiles("h_packed"), packed_tiles("h1_packed"), packed_tiles("y_packed")
+        packed = [
+            [sb.tile([P, QUARTER, PACK], BF16, name="packed%d_%d" % (i, k), align_bytes=64) for k in range(4)]
+            for i in range(3)
+        ]
         moving = {}
 
         def round_h(k, eng, first=0, last=QUARTER):
-            copy(eng, packed_walk(h_packed[k][:, first:last, :]), flat_walk(h_raw[k][:, :, first:last]))
+            src = h_raw[k // 2][:, :, quarter(k % 2)]
+            copy(eng, packed_walk(packed[0][k][:, first:last, :]), flat_walk(src[:, :, first:last]))
 
         def quant_moving(step, k):
             t = sb.tile([P, QUARTER + PLANE_WORDS], I32, name="moving%d_%d" % (step, k), align_bytes=64)
-            packed = (h_packed, h1_packed)[step][k]
-            quantise(t[:, 0:QUARTER], t[:, QUARTER:].bitcast(U8), packed[:].rearrange("p n j -> p (n j)"))
+            quantise(t[:, 0:QUARTER], t[:, QUARTER:].bitcast(U8), packed[step][k][:].rearrange("p n j -> p (n j)"))
             moving[step, k] = t
 
-        def one_pass(out, codes, scales, window, t, g):
-            nc.tensor.matmul_mx(
-                out=out,
-                lhsT=codes[rows[g], window].bitcast(FP8X4),
-                lhsT_scale=scales[rows[g], window],
-                rhs=t[rows[g], 0:QUARTER].bitcast(FP8X4),
-                rhs_scale=t[rows[g], QUARTER:].bitcast(U8),
-                start=True,
-                stop=True,
+        z, sums = {}, {}
+
+        def product(step, k, g):
+            groups = ROWS if k in WIDE else PACK
+            z[step, k, g] = ps.tile(
+                [P, groups, QUARTER], F32, name="z%d_%d_%d" % (step, k, g), tag="bank%d_%d" % (g, k)
+            )
+            t = moving[step, k]
+            for j in range(groups):
+                if k in WIDE:
+                    codes, scales, window = wide_codes, wide_scales, slice(j * P, (j + 1) * P)
+                else:
+                    codes, scales, window = packed_codes, packed_scales, slice((j + 1 - g) * R, (j + 3 - g) * R)
+                nc.tensor.matmul_mx(
+                    out=z[step, k, g][:, j, :],
+                    lhsT=codes[step][rows[g], window].bitcast(FP8X4),
+                    lhsT_scale=scales[step][rows[g], window],
+                    rhs=t[rows[g], 0:QUARTER].bitcast(FP8X4),
+                    rhs_scale=t[rows[g], QUARTER:].bitcast(U8),
+                    start=True,
+                    stop=True,
+                )
+
+        def add_wide(step, k, g):
+            sums[step, k, g] = sb.tile([P, ROWS, QUARTER], F32, name="sum%d_%d_%d" % (step, k, g))
+            vector.tensor_tensor(
+                out=sums[step, k, g][:], in0=z[step, k, g][:], in1=x[step, g][:, :, quarter(k)], op=ADD
             )
 
-        def bank(name, shape, k, g):
-            return ps.tile(shape, F32, name="%s_%d_%d" % (name, k, g), tag="bank%d_%d" % (g, k))
-
-        z1 = {}
-        sum1 = [sb.tile([P, PACK, QUARTER], F32, name="sum1_%d" % k) for k in range(4)]
-        tanh1 = [sb.tile([P, PACK, QUARTER], F32, name="tanh1_%d" % k) for k in range(4)]
-
-        def product1(k, g):
-            z1[k, g] = bank("z1", [P, PACK, QUARTER], k, g)
-            for x in range(PACK):
-                window = slice((x + 1 - g) * R, (x + 3 - g) * R)
-                one_pass(z1[k, g][:, x, :], w1_codes, w1_scales, window, moving[0, k], g)
-
-        def add1(k, g):
+        def add_packed(step, k, g, slots=slice(0, PACK)):
+            if (step, k) not in sums:
+                sums[step, k] = sb.tile([P, PACK, QUARTER], F32, name="sum%d_%d" % (step, k))
             part = read[g]
-            nc.vector.tensor_tensor(out=sum1[k][part], in0=z1[k, g][part], in1=x1_sb[k][part], op=ADD)
-
-        def act1(k):
-            nc.scalar.activation(out=tanh1[k][:], in_=sum1[k][:], func=TANH)
-
-        def scale1(k, eng, first=0, last=QUARTER):
-            eng.tensor_tensor(
-                out=packed_walk(h1_packed[k][:, first:last, :]),
-                in0=flat_walk(tanh1[k][:, :, first:last]),
-                in1=a_sb[:].unsqueeze(1).unsqueeze(3).to_broadcast([P, (last - first) // RUN, PACK, RUN]),
-                op=MULT,
-            )
-
-        def scale1_by_slot(k):
-            for j in range(PACK):
-                nc.scalar.mul(out=tanh1[k][:, j, :], in_=tanh1[k][:, j, :], mul=a_sb[:, j : j + 1])
-
-        def round_h1(k):
-            nc.vector.tensor_copy(out=packed_walk(h1_packed[k][:]), in_=flat_walk(tanh1[k][:]))
-
-        sum1w, tanh1w = {}, {}
-        moved1 = [sb.tile([P, 2, QUARTER], I32, name="moved1_%d" % k) for k in range(2)]
-
-        def product1w(k):
-            for g in heads:
-                z1[k, g] = bank("z1", [P, ROWS, QUARTER], k, g)
-                for s in range(ROWS):
-                    one_pass(z1[k, g][:, s, :], w1w_codes, w1w_scales, slice(s * P, (s + 1) * P), moving[0, k], g)
-
-        def add1w(k, g):
-            sum1w[k, g] = sb.tile([P, ROWS, QUARTER], F32, name="sum1w_%d_%d" % (k, g))
-            nc.vector.tensor_tensor(out=sum1w[k, g][:], in0=z1[k, g][:], in1=x1_wide[g][:, :, quarter(k)], op=ADD)
-
-        def act1w(k, g):
-            tanh1w[k, g] = sb.tile([P, ROWS, QUARTER], F32, name="tanh1w_%d_%d" % (k, g))
-            nc.scalar.activation(out=tanh1w[k, g][:], in_=sum1w[k, g][:], func=TANH)
-
-        pairs1 = {}
-
-        def scale1w(k, g, eng):
-            pairs = pairs1[k, g] = sb.tile([P, QUARTER, ROWS], BF16, name="pairs1_%d_%d" % (k, g))
-            eng.tensor_tensor(
-                out=packed_walk(pairs[:]),
-                in0=flat_walk(tanh1w[k, g][:]),
-                in1=a_wide[:, g, :].unsqueeze(1).unsqueeze(3).to_broadcast([P, QUARTER // RUN, ROWS, RUN]),
-                op=MULT,
-            )
-
-        def move1(k, g):
-            nc.sync.dma_start(out=moved1[k][rows[g]], in_=pairs1[k, g][:].rearrange("p n s -> p (n s)").bitcast(I32))
-
-        def join1(k, eng):
-            word = U32 if eng is nc.scalar else I32
-            copy(
-                eng,
-                h1_packed[k][:].rearrange("p n j -> p (n j)").bitcast(word).rearrange("p (n u) -> p n u", u=2),
-                moved1[k][:].bitcast(word).rearrange("p u n -> p n u"),
-            )
-
-        z2, sum2 = {}, {}
-        y = {g: sb.tile([P, ROWS, WIDE * QUARTER], F32, name="y%d" % g) for g in heads}
-        y_late = sb.tile([P, PACK, N - WIDE * QUARTER], F32, name="y_late")
-        sum_late = sb.tile([P, PACK, N - WIDE * QUARTER], F32, name="sum_late")
-        moved = [sb.tile([P, 2, QUARTER], I32, name="moved%d" % k) for k in range(WIDE)]
-        words = sb.tile([P, N], I32, name="words", align_bytes=64)
-        y_scales = sb.tile([P, N], U8, name="y_scales", align_bytes=64)
-        words_view = out_1[0].rearrange("p n j -> p (n j)").bitcast(I32)
-        scales_view = out_2[0].bitcast(I32)
-
-        def product2(k):
-            for g in heads:
-                z2[k, g] = bank("z2", [P, ROWS, QUARTER], k, g)
-                for s in range(ROWS):
-                    one_pass(z2[k, g][:, s, :], w2_codes, w2_scales, slice(s * P, (s + 1) * P), moving[1, k], g)
-
-        def add2(k, g):
-            sum2[k, g] = sb.tile([P, ROWS, QUARTER], F32, name="sum2_%d_%d" % (k, g))
-            nc.vector.tensor_tensor(out=sum2[k, g][:], in0=z2[k, g][:], in1=x2_sb[g][:, :, quarter(k)], op=ADD)
-
-        def act2(k, g):
-            nc.scalar.activation(out=y[g][:, :, quarter(k)], in_=sum2[k, g][:], func=TANH)
-
-        def send_pairs(k, g):
-            pairs = sb.tile([P, QUARTER, ROWS], BF16, name="pairs%d_%d" % (k, g))
-            nc.scalar.activation(out=packed_walk(pairs[:]), in_=flat_walk(sum2[k, g][:]), func=TANH)
-            nc.sync.dma_start(out=moved[k][rows[g]], in_=pairs[:].rearrange("p n s -> p (n s)").bitcast(I32))
-
-        def product2p(k, g):
-            z2[k, g] = bank("z2", [P, PACK, QUARTER], k, g)
-            for x in range(PACK):
-                window = slice((x + 1 - g) * R, (x + 3 - g) * R)
-                one_pass(z2[k, g][:, x, :], w2p_codes, w2p_scales, window, moving[1, k], g)
-
-        def add2p(k, g, s0=0, s1=PACK):
-            part = read[g]
-            nc.vector.tensor_tensor(
-                out=sum_late[part, s0:s1, quarter(k - WIDE)],
-                in0=z2[k, g][part, s0:s1, :],
-                in1=late["x2"][part, s0:s1, quarter(k - WIDE)],
+            vector.tensor_tensor(
+                out=sums[step, k][part, slots, :],
+                in0=z[step, k, g][part, slots, :],
+                in1=x[step][part, slots, quarter(k - 2)],
                 op=ADD,
             )
 
-        def act2p(k, s0=0, s1=PACK):
-            nc.scalar.activation(
-                out=y_late[:, s0:s1, quarter(k - WIDE)], in_=sum_late[:, s0:s1, quarter(k - WIDE)], func=TANH
-            )
+        pairs = {}
+        moved = {
+            (step, k): sb.tile([P, 2, QUARTER], I32, name="moved%d_%d" % (step, k)) for step in range(2) for k in WIDE
+        }
 
-        def round_y(k, eng=nc.vector, first=0, last=QUARTER):
-            o = (k - WIDE) * QUARTER
-            copy(eng, packed_walk(y_packed[k][:, first:last, :]), flat_walk(y_late[:, :, o + first : o + last]))
+        def new_pairs(step, k, g):
+            pairs[step, k, g] = sb.tile([P, QUARTER, ROWS], BF16, name="pairs%d_%d_%d" % (step, k, g))
+            return packed_walk(pairs[step, k, g][:])
 
-        def store_late(first, last, s0=0, s1=PACK):
+        def move(step, k, g):
             nc.sync.dma_start(
-                out=out_0.rearrange("(p j) n -> p j n", j=PACK)[:, s0:s1, first * QUARTER : last * QUARTER],
-                in_=y_late[:, s0:s1, (first - WIDE) * QUARTER : (last - WIDE) * QUARTER],
+                out=moved[step, k][rows[g]], in_=pairs[step, k, g][:].rearrange("p n s -> p (n s)").bitcast(I32)
             )
 
-        def join_pairs(k, eng=nc.vector):
-            word = U32 if eng is nc.scalar else I32
-            copy(
-                eng,
-                y_packed[k][:].rearrange("p n j -> p (n j)").bitcast(word).rearrange("p (n u) -> p n u", u=2),
-                moved[k][:].bitcast(word).rearrange("p u n -> p n u"),
+        def join(step, k):
+            vector.tensor_copy(
+                out=packed[step + 1][k][:].rearrange("p n j -> p (n j)").bitcast(I32).rearrange("p (n u) -> p n u", u=2),
+                in_=moved[step, k][:].rearrange("p u n -> p n u"),
             )
+
+        tanh1 = {}
+
+        def act1(*key):
+            src = sums[(0,) + key]
+            tanh1[key] = sb.tile(list(src.shape), F32, name="tanh1" + "_%d" * len(key) % key)
+            scalar.activation(out=tanh1[key][:], in_=src[:], func=TANH)
+
+        def scale(eng, out, src, a):
+            factor = a.unsqueeze(1).unsqueeze(3).to_broadcast([P, QUARTER // RUN, a.shape[1], RUN])
+            eng.tensor_tensor(out=out, in0=flat_walk(src), in1=factor, op=MULT)
+
+        def scale_wide(k, g, eng):
+            scale(eng, new_pairs(0, k, g), tanh1[k, g][:], a_wide[:, g, :])
+
+        def scale_packed(k):
+            scale(vector, packed_walk(packed[1][k][:]), tanh1[k,][:], a_packed[:])
+
+        def scale_by_slot(k):
+            for j in range(PACK):
+                scalar.mul(out=tanh1[k,][:, j, :], in_=tanh1[k,][:, j, :], mul=a_packed[:, j : j + 1])
+
+        def round_h1(k):
+            vector.tensor_copy(out=packed_walk(packed[1][k][:]), in_=flat_walk(tanh1[k,][:]))
+
+        y_wide = {g: sb.tile([P, ROWS, HALF], F32, name="y_wide%d" % g) for g in heads}
+        y_packed = sb.tile([P, PACK, HALF], F32, name="y_packed")
+        words = sb.tile([P, N], I32, name="words", align_bytes=64)
+        y_scales = sb.tile([P, N], U8, name="y_scales", align_bytes=64)
+        slot_pairs = (slice(0, 2), slice(2, 4))
+
+        def act2_wide(k, g):
+            scalar.activation(out=y_wide[g][:, :, quarter(k)], in_=sums[1, k, g][:], func=TANH)
+
+        def send_pairs(k, g):
+            scalar.activation(out=new_pairs(1, k, g), in_=flat_walk(sums[1, k, g][:]), func=TANH)
+            move(1, k, g)
+
+        def act2_packed(k, slots):
+            scalar.activation(out=y_packed[:, slots, quarter(k - 2)], in_=sums[1, k][:, slots, :], func=TANH)
+
+        def round_y(k):
+            vector.tensor_copy(out=packed_walk(packed[2][k][:]), in_=flat_walk(y_packed[:, :, quarter(k - 2)]))
 
         def quant_y(k):
-            quantise(words[:, quarter(k)], y_scales[:, quarter(k)], y_packed[k][:].rearrange("p n j -> p (n j)"))
+            quantise(words[:, quarter(k)], y_scales[:, quarter(k)], packed[2][k][:].rearrange("p n j -> p (n j)"))
 
-        def store_y(g, first, last):
-            cols = slice(first * QUARTER, last * QUARTER)
-            nc.sync.dma_start(out=by_row(out_0[g * D : (g + 1) * D, :])[:, :, cols], in_=y[g][:, :, cols])
+        def store_wide(g):
+            nc.sync.dma_start(out=by_row(out_0[g * D : (g + 1) * D, :])[:, :, half(0)], in_=y_wide[g][:])
 
-        def store_words(first, last):
-            cols = slice(first * QUARTER, last * QUARTER)
-            nc.scalar.dma_start(out=words_view[:, cols], in_=words[:, cols])
+        def store_packed(slots):
+            dst = out_0.rearrange("(p j) n -> p j n", j=PACK)
+            nc.sync.dma_start(out=dst[:, slots, half(1)], in_=y_packed[:, slots, :])
 
-        vector, scalar, gpsimd = nc.vector, nc.scalar, nc.gpsimd
 
-        deal(0, vector, 0, 40)
-        deal(0, scalar, 40, R)
+        deal(0, vector, 0, W1_ON_VECTOR)
+        deal(0, scalar, W1_ON_VECTOR, R)
         quant_w(0)
         round_h(0, vector, 0, H0_ON_VECTOR)
         round_h(0, scalar, H0_ON_VECTOR, QUARTER)
         round_h(1, scalar)
         quant_moving(0, 0)
-        product1w(0)
+        for g in heads:
+            product(0, 0, g)
         regroup_scales(0)
         regroup_codes(0)
         quant_moving(0, 1)
-        product1w(1)
+        for g in heads:
+            product(0, 1, g)
         round_h(2, vector)
         round_h(3, scalar)
-        quant_moving(0, 2)
-        add1w(0, upper)
-        quant_moving(0, 3)
-        add1w(1, upper)
-        for k in (2, 3):
-            product1(k, upper)
-        for k in (2, 3):
-            product1(k, lower)
-        add1w(0, lower)
-        add1w(1, lower)
+
+        for k in WIDE:
+            quant_moving(0, k + 2)
+            add_wide(0, k, upper)
         for g in heads:
-            for k in (0, 1):
-                act1w(k, g)
-        load_x2(upper)
-        scale1w(0, upper, vector)
-        scale1w(1, upper, vector)
-        scale1w(0, lower, vector)
-        scale1w(1, lower, gpsimd)
-        for k in (0, 1):
+            for k in PACKED:
+                product(0, k, g)
+        for k in WIDE:
+            add_wide(0, k, lower)
+        for g in heads:
+            for k in WIDE:
+                act1(k, g)
+        load_wide(1, upper)
+        for k, g, eng in ((0, upper, vector), (1, upper, vector), (0, lower, vector), (1, lower, gpsimd)):
+            scale_wide(k, g, eng)
+        for k in WIDE:
             for g in heads:
-                move1(k, g)
-        load_x2(lower)
-        load_x2_late()
+                move(0, k, g)
+        load_wide(1, lower)
+        load_packed(1)
+
         deal(1, scalar, 0, R)
-        for k in (2, 3):
-            add1(k, upper)
-        for k in (2, 3):
-            add1(k, lower)
+        for k in PACKED:
+            add_packed(0, k, upper)
+        for k in PACKED:
+            add_packed(0, k, lower)
             act1(k)
+
         quant_w(1)
-        join1(0, vector)
+        join(0, 0)
         regroup_codes(1)
-        scale1_by_slot(3)
+        scale_by_slot(3)
         regroup_scales(1)
         quant_moving(1, 0)
-        product2(0)
-        scale1(2, vector)
-        join1(1, vector)
+        for g in heads:
+            product(1, 0, g)
+        scale_packed(2)
+        join(0, 1)
         quant_moving(1, 2)
         quant_moving(1, 1)
-        product2(1)
-        product2p(2, upper)
-        add2(0, upper)
+        for g in heads:
+            product(1, 1, g)
+        product(1, 2, upper)
+        add_wide(1, 0, upper)
         round_h1(3)
-        add2(0, lower)
+        add_wide(1, 0, lower)
         quant_moving(1, 3)
-        product2p(3, upper)
-        product2p(2, lower)
-        product2p(3, lower)
-        add2(1, upper)
-        add2(1, lower)
-        for k in (2, 3):
-            add2p(k, upper)
-        add2p(2, lower, 0, 2)
-        add2p(2, lower, 2, 4)
-        add2p(3, lower, 0, 2)
-        add2p(3, lower, 2, 4)
+        product(1, 3, upper)
+        for k in PACKED:
+            product(1, k, lower)
+
+        for g in heads:
+            add_wide(1, 1, g)
+        for k in PACKED:
+            add_packed(1, k, upper)
+        for k in PACKED:
+            for slots in slot_pairs:
+                add_packed(1, k, lower, slots)
+
         send_pairs(0, upper)
-        act2(0, upper)
+        act2_wide(0, upper)
         send_pairs(0, lower)
-        send_pairs(1, upper)
-        send_pairs(1, lower)
-        act2(1, upper)
-        store_y(upper, 0, 2)
-        act2(0, lower)
-        act2(1, lower)
-        store_y(lower, 0, 2)
-        act2p(2, 0, 2)
-        act2p(2, 2, 4)
-        act2p(3, 0, 2)
-        store_late(2, 4, 0, 2)
-        act2p(3, 2, 4)
-        store_late(2, 4, 2, 4)
-        join_pairs(0)
+        for g in heads:
+            send_pairs(1, g)
+        act2_wide(1, upper)
+        store_wide(upper)
+        for k in WIDE:
+            act2_wide(k, lower)
+        store_wide(lower)
+        for k in PACKED:
+            for slots in slot_pairs:
+                act2_packed(k, slots)
+                if k == PACKED[-1]:
+                    store_packed(slots)
+
+        join(1, 0)
         round_y(2)
-        join_pairs(1)
+        join(1, 1)
         quant_y(0)
         round_y(3)
-        quant_y(1)
-        quant_y(2)
-        store_words(0, 3)
-        quant_y(3)
-        store_words(3, 4)
+        for k in (1, 2, 3):
+            quant_y(k)
+        scalar.dma_start(out=out_1[0].rearrange("p n j -> p (n j)").bitcast(I32), in_=words[:])
 
-        for q, queue in enumerate((nc.sync, nc.sync, nc.scalar, nc.sync)):
+        scales_view = out_2[0].bitcast(I32)
+        for q, queue in enumerate((nc.sync, nc.sync, scalar, nc.sync)):
             queue.dma_start(out=scales_view[4 * q : 4 * q + 4, :], in_=y_scales[32 * q : 32 * q + 4, :].bitcast(I32))

@@ -74,15 +74,13 @@ def tile_rows_pl_steps_tanh_kernel(tc, h, w1, x1, a1, w2, x2, out_0, out_1, out_
             x[step] = load("x%d_packed" % step, by_slot((x1, x2)[step])[:, :, half(1)])
 
         w_raw = [load("w1_raw", by_slot(w1))]
-        a_packed = sb.tile([P, PACK], F32, name="a_packed")
-        scalar.dma_start(out=a_packed[:], in_=a1.rearrange("g (p j) o -> (g p) (j o)", j=PACK))
-        a_wide = sb.tile([P, G, ROWS], F32, name="a_wide")
-        scalar.dma_start(out=a_wide[:], in_=a1.rearrange("g (q s) o -> q g (s o)", s=ROWS))
         h_raw = [load("h_raw%d" % hf, by_slot(h)[:, :, half(hf)]) for hf in range(2)]
         for g in heads:
             load_wide(0, g)
+        a_wide = load("a_wide", a1.rearrange("g (q s) o -> q g (s o)", s=ROWS))
         load_packed(0)
         w_raw.append(load("w2_raw", by_slot(w2)))
+        a_packed = load("a_packed", a1.rearrange("g (p j) o -> (g p) (j o)", j=PACK))
 
         dealt, wide_codes, wide_scales, packed_codes, packed_scales = [], [], [], [], []
         for i in range(2):

@@ -57,6 +57,8 @@ def tile_rows_pl_steps_tanh_kernel(tc, h, w1, x1, a1, w2, x2, out_0, out_1, out_
         def copy(eng, out, in_):
             if eng is scalar:
                 scalar.copy(out=out, in_=in_)
+            elif eng is gpsimd:
+                gpsimd.tensor_scalar(out=out, in0=in_, scalar1=1.0, scalar2=0.0, op0=MULT, op1=ADD)
             else:
                 vector.tensor_copy(out=out, in_=in_)
 
@@ -97,11 +99,18 @@ def tile_rows_pl_steps_tanh_kernel(tc, h, w1, x1, a1, w2, x2, out_0, out_1, out_
             vector.quantize_mx(out=codes.bitcast(FP8X4), scales=scales, in_=packed)
 
         def deal(i, eng, first, last):
-            copy(
-                eng,
-                dealt[i][:].rearrange("p s (c i) j -> p c j i s", i=2)[:, first:last],
-                w_raw[i][:].rearrange("p j (c i s) -> p c j i s", i=2, s=ROWS)[:, first:last],
-            )
+            if eng is gpsimd:
+                copy(
+                    eng,
+                    dealt[i][:].rearrange("p s q j -> p q j s")[:, 2 * first : 2 * last],
+                    w_raw[i][:].rearrange("p j (q s) -> p q j s", s=ROWS)[:, 2 * first : 2 * last],
+                )
+            else:
+                copy(
+                    eng,
+                    dealt[i][:].rearrange("p s (c i) j -> p c j i s", i=2)[:, first:last],
+                    w_raw[i][:].rearrange("p j (c i s) -> p c j i s", i=2, s=ROWS)[:, first:last],
+                )
 
         def quant_w(i):
             quantise(wide_codes[i][:], wide_scales[i][:], dealt[i][:].rearrange("p s q j -> p (s q j)"))
@@ -194,10 +203,12 @@ def tile_rows_pl_steps_tanh_kernel(tc, h, w1, x1, a1, w2, x2, out_0, out_1, out_
                 out=moved[step, k][rows[g]], in_=pairs[step, k, g][:].rearrange("p n s -> p (n s)").bitcast(I32)
             )
 
-        def join(step, k):
-            vector.tensor_copy(
-                out=packed[step + 1][k][:].rearrange("p n j -> p (n j)").bitcast(I32).rearrange("p (n u) -> p n u", u=2),
-                in_=moved[step, k][:].rearrange("p u n -> p n u"),
+        def join(step, k, eng=vector):
+            word = U32 if eng is scalar else I32
+            copy(
+                eng,
+                packed[step + 1][k][:].rearrange("p n j -> p (n j)").bitcast(word).rearrange("p (n u) -> p n u", u=2),
+                moved[step, k][:].bitcast(word).rearrange("p u n -> p n u"),
             )
 
         tanh1 = {}
@@ -240,8 +251,8 @@ def tile_rows_pl_steps_tanh_kernel(tc, h, w1, x1, a1, w2, x2, out_0, out_1, out_
         def act2_packed(k, slots):
             scalar.activation(out=y_packed[:, slots, quarter(k - 2)], in_=sums[1, k][:, slots, :], func=TANH)
 
-        def round_y(k):
-            vector.tensor_copy(out=packed_walk(packed[2][k][:]), in_=flat_walk(y_packed[:, :, quarter(k - 2)]))
+        def round_y(k, eng=vector):
+            copy(eng, packed_walk(packed[2][k][:]), flat_walk(y_packed[:, :, quarter(k - 2)]))
 
         def quant_y(k):
             quantise(words[:, quarter(k)], y_scales[:, quarter(k)], packed[2][k][:].rearrange("p n j -> p (n j)"))
@@ -252,6 +263,12 @@ def tile_rows_pl_steps_tanh_kernel(tc, h, w1, x1, a1, w2, x2, out_0, out_1, out_
         def store_packed(slots):
             dst = out_0.rearrange("(p j) n -> p j n", j=PACK)
             nc.sync.dma_start(out=dst[:, slots, half(1)], in_=y_packed[:, slots, :])
+
+        def store_planes():
+            scalar.dma_start(out=out_1[0].rearrange("p n j -> p (n j)").bitcast(I32), in_=words[:])
+            scales_view = out_2[0].bitcast(I32)
+            for q, queue in enumerate((nc.sync, nc.sync, scalar, nc.sync)):
+                queue.dma_start(out=scales_view[4 * q : 4 * q + 4, :], in_=y_scales[32 * q : 32 * q + 4, :].bitcast(I32))
 
 
         deal(0, vector, 0, W1_ON_VECTOR)
@@ -291,7 +308,8 @@ def tile_rows_pl_steps_tanh_kernel(tc, h, w1, x1, a1, w2, x2, out_0, out_1, out_
         load_wide(1, lower)
         load_packed(1)
 
-        deal(1, scalar, 0, R)
+        deal(1, scalar, 0, 36)
+        deal(1, gpsimd, 36, R)
         for k in PACKED:
             add_packed(0, k, upper)
         for k in PACKED:
@@ -352,8 +370,4 @@ def tile_rows_pl_steps_tanh_kernel(tc, h, w1, x1, a1, w2, x2, out_0, out_1, out_
         round_y(3)
         for k in (1, 2, 3):
             quant_y(k)
-        scalar.dma_start(out=out_1[0].rearrange("p n j -> p (n j)").bitcast(I32), in_=words[:])
-
-        scales_view = out_2[0].bitcast(I32)
-        for q, queue in enumerate((nc.sync, nc.sync, scalar, nc.sync)):
-            queue.dma_start(out=scales_view[4 * q : 4 * q + 4, :], in_=y_scales[32 * q : 32 * q + 4, :].bitcast(I32))
+        store_planes()

@@ -22,6 +22,7 @@ ROWS = 2
 QUARTER = 128
 HALF = 2 * QUARTER
 PLANE_WORDS = QUARTER // 4
+BURST = 256
 RUN = 4
 WIDE, PACKED = (0, 1), (2, 3)
 
@@ -63,7 +64,7 @@ def tile_rows_pl_steps_tanh_kernel(tc, h, w1, x1, a1, w2, x2, out_0, out_1, out_
                 vector.tensor_copy(out=out, in_=in_)
 
         def load(name, src):
-            raw = sb.tile(list(src.shape), F32, name=name)
+            raw = sb.tile(list(src.shape), F32, name=name, align_bytes=BURST)
             nc.sync.dma_start(out=raw[:], in_=src)
             return raw
 
@@ -191,11 +192,11 @@ def tile_rows_pl_steps_tanh_kernel(tc, h, w1, x1, a1, w2, x2, out_0, out_1, out_
 
         pairs = {}
         moved = {
-            (step, k): sb.tile([P, 2, QUARTER], I32, name="moved%d_%d" % (step, k)) for step in range(2) for k in WIDE
+            (step, k): sb.tile([P, 2, QUARTER], I32, name="moved%d_%d" % (step, k), align_bytes=BURST) for step in range(2) for k in WIDE
         }
 
         def new_pairs(step, k, g):
-            pairs[step, k, g] = sb.tile([P, QUARTER, ROWS], BF16, name="pairs%d_%d_%d" % (step, k, g))
+            pairs[step, k, g] = sb.tile([P, QUARTER, ROWS], BF16, name="pairs%d_%d_%d" % (step, k, g), align_bytes=BURST)
             return packed_walk(pairs[step, k, g][:])
 
         def move(step, k, g):
@@ -235,10 +236,10 @@ def tile_rows_pl_steps_tanh_kernel(tc, h, w1, x1, a1, w2, x2, out_0, out_1, out_
         def round_h1(k):
             vector.tensor_copy(out=packed_walk(packed[1][k][:]), in_=flat_walk(tanh1[k,][:]))
 
-        y_wide = {g: sb.tile([P, ROWS, HALF], F32, name="y_wide%d" % g) for g in heads}
-        y_packed = sb.tile([P, PACK, HALF], F32, name="y_packed")
-        words = sb.tile([P, N], I32, name="words", align_bytes=64)
-        y_scales = sb.tile([P, N], U8, name="y_scales", align_bytes=64)
+        y_wide = {g: sb.tile([P, ROWS, HALF], F32, name="y_wide%d" % g, align_bytes=BURST) for g in heads}
+        y_packed = sb.tile([P, PACK, HALF], F32, name="y_packed", align_bytes=BURST)
+        words = sb.tile([P, N], I32, name="words", align_bytes=BURST)
+        y_scales = sb.tile([P, N], U8, name="y_scales", align_bytes=BURST)
         slot_pairs = (slice(0, 2), slice(2, 4))
 
         def act2_wide(k, g):

@@ -28,6 +28,7 @@ WIDE, PACKED = (0, 1), (2, 3)
 
 W1_ON_VECTOR = 40
 H0_ON_VECTOR = 88
+W2_ON_SCALAR = 40
 
 
 def tile_rows_pl_steps_tanh_kernel(tc, h, w1, x1, a1, w2, x2, out_0, out_1, out_2):
@@ -76,14 +77,29 @@ def tile_rows_pl_steps_tanh_kernel(tc, h, w1, x1, a1, w2, x2, out_0, out_1, out_
         def load_packed(step):
             x[step] = load("x%d_packed" % step, by_slot((x1, x2)[step])[:, :, half(1)])
 
-        w_raw = [load("w1_raw", by_slot(w1))]
-        h_raw = [load("h_raw%d" % hf, by_slot(h)[:, :, half(hf)]) for hf in range(2)]
+        w_raw, h_raw, a = {}, {}, {}
+
+        def load_w(i):
+            w_raw[i] = load("w%d_raw" % (i + 1), by_slot((w1, w2)[i]))
+
+        def load_h(hf):
+            h_raw[hf] = load("h_raw%d" % hf, by_slot(h)[:, :, half(hf)])
+
+        def load_a_wide():
+            a["wide"] = load("a_wide", a1.rearrange("g (q s) o -> q g (s o)", s=ROWS))
+
+        def load_a_packed():
+            a["packed"] = load("a_packed", a1.rearrange("g (p j) o -> (g p) (j o)", j=PACK))
+
+        load_w(0)
+        for hf in range(2):
+            load_h(hf)
         for g in heads:
             load_wide(0, g)
-        a_wide = load("a_wide", a1.rearrange("g (q s) o -> q g (s o)", s=ROWS))
+        load_a_wide()
         load_packed(0)
-        w_raw.append(load("w2_raw", by_slot(w2)))
-        a_packed = load("a_packed", a1.rearrange("g (p j) o -> (g p) (j o)", j=PACK))
+        load_w(1)
+        load_a_packed()
 
         dealt, wide_codes, wide_scales, packed_codes, packed_scales = [], [], [], [], []
         for i in range(2):
@@ -190,6 +206,17 @@ def tile_rows_pl_steps_tanh_kernel(tc, h, w1, x1, a1, w2, x2, out_0, out_1, out_
                 op=ADD,
             )
 
+        emptied = {}
+
+        def empty(step, k, g):
+            if (step, k) not in emptied:
+                emptied[step, k] = sb.tile([P, PACK, QUARTER], F32, name="emptied%d_%d" % (step, k))
+            scalar.copy(out=emptied[step, k][rows[g]], in_=z[step, k, g][rows[g]])
+
+        def add_emptied(step, k, eng=vector):
+            sums[step, k] = sb.tile([P, PACK, QUARTER], F32, name="sum%d_%d" % (step, k))
+            eng.tensor_tensor(out=sums[step, k][:], in0=emptied[step, k][:], in1=x[step][:, :, quarter(k - 2)], op=ADD)
+
         pairs = {}
         moved = {
             (step, k): sb.tile([P, 2, QUARTER], I32, name="moved%d_%d" % (step, k), align_bytes=BURST) for step in range(2) for k in WIDE
@@ -219,19 +246,24 @@ def tile_rows_pl_steps_tanh_kernel(tc, h, w1, x1, a1, w2, x2, out_0, out_1, out_
             tanh1[key] = sb.tile(list(src.shape), F32, name="tanh1" + "_%d" * len(key) % key)
             scalar.activation(out=tanh1[key][:], in_=src[:], func=TANH)
 
-        def scale(eng, out, src, a):
-            factor = a.unsqueeze(1).unsqueeze(3).to_broadcast([P, QUARTER // RUN, a.shape[1], RUN])
+        def scale(eng, out, src, by):
+            factor = by.unsqueeze(1).unsqueeze(3).to_broadcast([P, QUARTER // RUN, by.shape[1], RUN])
             eng.tensor_tensor(out=out, in0=flat_walk(src), in1=factor, op=MULT)
 
         def scale_wide(k, g, eng):
-            scale(eng, new_pairs(0, k, g), tanh1[k, g][:], a_wide[:, g, :])
+            scale(eng, new_pairs(0, k, g), tanh1[k, g][:], a["wide"][:, g, :])
 
-        def scale_packed(k):
-            scale(vector, packed_walk(packed[1][k][:]), tanh1[k,][:], a_packed[:])
+        def scale_by_row(k, g):
+            new_pairs(0, k, g)
+            for s in range(ROWS):
+                scalar.mul(out=pairs[0, k, g][:, :, s], in_=tanh1[k, g][:, s, :], mul=a["wide"][:, g, s : s + 1])
+
+        def scale_packed(k, eng=vector):
+            scale(eng, packed_walk(packed[1][k][:]), tanh1[k,][:], a["packed"][:])
 
         def scale_by_slot(k):
             for j in range(PACK):
-                scalar.mul(out=tanh1[k,][:, j, :], in_=tanh1[k,][:, j, :], mul=a_packed[:, j : j + 1])
+                scalar.mul(out=tanh1[k,][:, j, :], in_=tanh1[k,][:, j, :], mul=a["packed"][:, j : j + 1])
 
         def round_h1(k):
             vector.tensor_copy(out=packed_walk(packed[1][k][:]), in_=flat_walk(tanh1[k,][:]))
@@ -265,12 +297,18 @@ def tile_rows_pl_steps_tanh_kernel(tc, h, w1, x1, a1, w2, x2, out_0, out_1, out_
             dst = out_0.rearrange("(p j) n -> p j n", j=PACK)
             nc.sync.dma_start(out=dst[:, slots, half(1)], in_=y_packed[:, slots, :])
 
-        def store_planes():
-            scalar.dma_start(out=out_1[0].rearrange("p n j -> p (n j)").bitcast(I32), in_=words[:])
+        def store_quarter(k, slots=slice(0, PACK)):
+            dst = out_0.rearrange("(p j) n -> p j n", j=PACK)
+            nc.sync.dma_start(out=dst[:, slots, quarter(k)], in_=y_packed[:, slots, quarter(k - 2)])
+
+        def store_words(queue, cols):
+            queue.dma_start(out=out_1[0].rearrange("p n j -> p (n j)").bitcast(I32)[:, cols], in_=words[:, cols])
+
+        def store_planes(cols=slice(0, N)):
+            store_words(scalar, cols)
             scales_view = out_2[0].bitcast(I32)
             for q, queue in enumerate((nc.sync, nc.sync, scalar, nc.sync)):
                 queue.dma_start(out=scales_view[4 * q : 4 * q + 4, :], in_=y_scales[32 * q : 32 * q + 4, :].bitcast(I32))
-
 
         deal(0, vector, 0, W1_ON_VECTOR)
         deal(0, scalar, W1_ON_VECTOR, R)
@@ -288,7 +326,6 @@ def tile_rows_pl_steps_tanh_kernel(tc, h, w1, x1, a1, w2, x2, out_0, out_1, out_
             product(0, 1, g)
         round_h(2, vector)
         round_h(3, scalar)
-
         for k in WIDE:
             quant_moving(0, k + 2)
             add_wide(0, k, upper)
@@ -300,46 +337,44 @@ def tile_rows_pl_steps_tanh_kernel(tc, h, w1, x1, a1, w2, x2, out_0, out_1, out_
         for g in heads:
             for k in WIDE:
                 act1(k, g)
-        load_wide(1, upper)
         for k, g, eng in ((0, upper, vector), (1, upper, vector), (0, lower, vector), (1, lower, gpsimd)):
             scale_wide(k, g, eng)
-        for k in WIDE:
-            for g in heads:
+        for g in heads:
+            for k in WIDE:
                 move(0, k, g)
+        load_wide(1, upper)
         load_wide(1, lower)
         load_packed(1)
 
-        deal(1, scalar, 0, 36)
-        deal(1, gpsimd, 36, R)
+        deal(1, scalar, 0, W2_ON_SCALAR)
+        deal(1, gpsimd, W2_ON_SCALAR, R)
         for k in PACKED:
             add_packed(0, k, upper)
         for k in PACKED:
             add_packed(0, k, lower)
             act1(k)
-
-        quant_w(1)
         join(0, 0)
-        regroup_codes(1)
+        quant_w(1)
+        join(0, 1, scalar)
         scale_by_slot(3)
-        regroup_scales(1)
+        regroup_codes(1)
         quant_moving(1, 0)
         for g in heads:
             product(1, 0, g)
         scale_packed(2)
-        join(0, 1)
-        quant_moving(1, 2)
+        regroup_scales(1)
         quant_moving(1, 1)
         for g in heads:
             product(1, 1, g)
-        product(1, 2, upper)
         add_wide(1, 0, upper)
+        quant_moving(1, 2)
+        product(1, 2, upper)
         round_h1(3)
         add_wide(1, 0, lower)
         quant_moving(1, 3)
         product(1, 3, upper)
         for k in PACKED:
             product(1, k, lower)
-
         for g in heads:
             add_wide(1, 1, g)
         for k in PACKED:
@@ -347,7 +382,6 @@ def tile_rows_pl_steps_tanh_kernel(tc, h, w1, x1, a1, w2, x2, out_0, out_1, out_
         for k in PACKED:
             for slots in slot_pairs:
                 add_packed(1, k, lower, slots)
-
         send_pairs(0, upper)
         act2_wide(0, upper)
         send_pairs(0, lower)
@@ -363,7 +397,6 @@ def tile_rows_pl_steps_tanh_kernel(tc, h, w1, x1, a1, w2, x2, out_0, out_1, out_
                 act2_packed(k, slots)
                 if k == PACKED[-1]:
                     store_packed(slots)
-
         join(1, 0)
         round_y(2)
         join(1, 1)

@@ -139,8 +139,9 @@ def tile_rows_pl_steps_tanh_kernel(tc, h, w1, x1, a1, w2, x2, out_0, out_1, out_
                 wide.rearrange("p (s m u) -> p s m u", s=ROWS, u=2),
             )
 
-        def regroup_codes(i):
-            regroup(scalar, packed_codes[i][:, R : 5 * R].bitcast(U32), wide_codes[i][:].bitcast(U32))
+        def regroup_codes(i, eng=scalar):
+            word = U32 if eng is scalar else I32
+            regroup(eng, packed_codes[i][:, R : 5 * R].bitcast(word), wide_codes[i][:].bitcast(word))
 
         def regroup_scales(i):
             regroup(vector, packed_scales[i][:, R : 5 * R], wide_scales[i][:])
@@ -190,10 +191,10 @@ def tile_rows_pl_steps_tanh_kernel(tc, h, w1, x1, a1, w2, x2, out_0, out_1, out_
                 )
 
         def add_wide(step, k, g):
-            sums[step, k, g] = sb.tile([P, ROWS, QUARTER], F32, name="sum%d_%d_%d" % (step, k, g))
-            vector.tensor_tensor(
-                out=sums[step, k, g][:], in0=z[step, k, g][:], in1=x[step, g][:, :, quarter(k)], op=ADD
-            )
+            if (step, "wide", g) not in sums:
+                sums[step, "wide", g] = sb.tile([P, ROWS, HALF], F32, name="sum%d_wide%d" % (step, g))
+            sums[step, k, g] = sums[step, "wide", g][:, :, quarter(k)]
+            vector.tensor_tensor(out=sums[step, k, g], in0=z[step, k, g][:], in1=x[step, g][:, :, quarter(k)], op=ADD)
 
         def add_packed(step, k, g, slots=slice(0, PACK)):
             if (step, k) not in sums:
@@ -277,11 +278,18 @@ def tile_rows_pl_steps_tanh_kernel(tc, h, w1, x1, a1, w2, x2, out_0, out_1, out_
         def act2_wide(k, g):
             scalar.activation(out=y_wide[g][:, :, quarter(k)], in_=sums[1, k, g][:], func=TANH)
 
+        def act2_head(g):
+            scalar.activation(out=y_wide[g][:], in_=sums[1, "wide", g][:], func=TANH)
+
+        def round_pairs(k, g):
+            copy(vector, new_pairs(1, k, g), flat_walk(y_wide[g][:, :, quarter(k)]))
+            move(1, k, g)
+
         def send_pairs(k, g):
             scalar.activation(out=new_pairs(1, k, g), in_=flat_walk(sums[1, k, g][:]), func=TANH)
             move(1, k, g)
 
-        def act2_packed(k, slots):
+        def act2_packed(k, slots=slice(0, PACK)):
             scalar.activation(out=y_packed[:, slots, quarter(k - 2)], in_=sums[1, k][:, slots, :], func=TANH)
 
         def round_y(k, eng=vector):
@@ -337,10 +345,11 @@ def tile_rows_pl_steps_tanh_kernel(tc, h, w1, x1, a1, w2, x2, out_0, out_1, out_
         for g in heads:
             for k in WIDE:
                 act1(k, g)
-        for k, g, eng in ((0, upper, vector), (1, upper, vector), (0, lower, vector), (1, lower, gpsimd)):
-            scale_wide(k, g, eng)
-        for g in heads:
-            for k in WIDE:
+        for k, g in ((0, upper), (1, upper), (0, lower)):
+            scale_wide(k, g, vector)
+        scale_by_row(1, lower)
+        for k in WIDE:
+            for g in heads:
                 move(0, k, g)
         load_wide(1, upper)
         load_wide(1, lower)
@@ -389,8 +398,7 @@ def tile_rows_pl_steps_tanh_kernel(tc, h, w1, x1, a1, w2, x2, out_0, out_1, out_
             send_pairs(1, g)
         act2_wide(1, upper)
         store_wide(upper)
-        for k in WIDE:
-            act2_wide(k, lower)
+        act2_head(lower)
         store_wide(lower)
         for k in PACKED:
             for slots in slot_pairs:

@@ -334,19 +334,21 @@ def tile_rows_pl_steps_tanh_kernel(tc, h, w1, x1, a1, w2, x2, out_0, out_1, out_
             product(0, 1, g)
         round_h(2, vector)
         round_h(3, scalar)
-        for k in WIDE:
-            quant_moving(0, k + 2)
-            add_wide(0, k, upper)
+        quant_moving(0, 2)
+        add_wide(0, 0, upper)
+        quant_moving(0, 3)
         for g in heads:
             for k in PACKED:
                 product(0, k, g)
-        for k in WIDE:
-            add_wide(0, k, lower)
+        add_wide(0, 0, lower)
         for g in heads:
-            for k in WIDE:
+            add_wide(0, 1, g)
+        for k in WIDE:
+            for g in heads:
                 act1(k, g)
-        for k, g in ((0, upper), (1, upper), (0, lower)):
-            scale_wide(k, g, vector)
+        for g in heads:
+            scale_wide(0, g, vector)
+        scale_wide(1, upper, gpsimd)
         scale_by_row(1, lower)
         for k in WIDE:
             for g in heads:
@@ -364,13 +366,13 @@ def tile_rows_pl_steps_tanh_kernel(tc, h, w1, x1, a1, w2, x2, out_0, out_1, out_
             act1(k)
         join(0, 0)
         quant_w(1)
-        join(0, 1, scalar)
         scale_by_slot(3)
         regroup_codes(1)
         quant_moving(1, 0)
         for g in heads:
             product(1, 0, g)
         scale_packed(2)
+        join(0, 1)
         regroup_scales(1)
         quant_moving(1, 1)
         for g in heads:
@@ -403,13 +405,14 @@ def tile_rows_pl_steps_tanh_kernel(tc, h, w1, x1, a1, w2, x2, out_0, out_1, out_
         for k in PACKED:
             for slots in slot_pairs:
                 act2_packed(k, slots)
-                if k == PACKED[-1]:
-                    store_packed(slots)
+            store_quarter(k)
         join(1, 0)
         round_y(2)
-        join(1, 1)
         quant_y(0)
+        join(1, 1)
         round_y(3)
-        for k in (1, 2, 3):
+        quant_y(1)
+        store_words(nc.sync, half(0))
+        for k in (2, 3):
             quant_y(k)
-        store_planes()
+        store_planes(half(1))

@@ -405,14 +405,13 @@ def tile_rows_pl_steps_tanh_kernel(tc, h, w1, x1, a1, w2, x2, out_0, out_1, out_
         for k in PACKED:
             for slots in slot_pairs:
                 act2_packed(k, slots)
-            store_quarter(k)
+                if k == PACKED[-1]:
+                    store_packed(slots)
         join(1, 0)
         round_y(2)
         quant_y(0)
         join(1, 1)
         round_y(3)
-        quant_y(1)
-        store_words(nc.sync, half(0))
-        for k in (2, 3):
+        for k in (2, 1, 3):
             quant_y(k)
-        store_planes(half(1))
+        store_planes()

from contextlib import ExitStack

import concourse.mybir as mybir

G, D, N = 2, 256, 512
FLOPS = 2 * 2 * G * D * D * N

F32 = mybir.dt.float32
BF16 = mybir.dt.bfloat16
I32 = mybir.dt.int32
U32 = mybir.dt.uint32
U8 = mybir.dt.uint8
FP8X4 = mybir.dt.float8_e4m3fn_x4
TANH = mybir.ActivationFunctionType.Tanh
ADD = mybir.AluOpType.add
MULT = mybir.AluOpType.mult

P = 128
R = 64
PACK = 4
ROWS = 2
QUARTER = 128
HALF = 2 * QUARTER
PLANE_WORDS = QUARTER // 4
BURST = 256
RUN = 4
WIDE, PACKED = (0, 1), (2, 3)

W1_ON_VECTOR = 40
H0_ON_VECTOR = 88
W2_ON_SCALAR = 40


def tile_rows_pl_steps_tanh_kernel(tc, h, w1, x1, a1, w2, x2, out_0, out_1, out_2):
    nc = tc.nc
    vector, scalar, gpsimd = nc.vector, nc.scalar, nc.gpsimd
    rows = [slice(0, R), slice(R, P)]
    read = [slice(0, R), slice(0, P)]
    upper, lower = 1, 0
    heads = (upper, lower)

    with ExitStack() as ctx:
        sb = ctx.enter_context(tc.tile_pool(name="sb", bufs=1))
        ps = ctx.enter_context(tc.psum_pool(name="ps", bufs=1))
        ctx.enter_context(tc.manual_schedule())

        def by_slot(src):
            return src.rearrange("g (p j) w -> (g p) j w", j=PACK)

        def by_row(src):
            return src.rearrange("(q s) n -> q s n", s=ROWS)

        def quarter(k):
            return slice(k * QUARTER, (k + 1) * QUARTER)

        def half(hf):
            return slice(hf * HALF, (hf + 1) * HALF)

        def copy(eng, out, in_):
            if eng is scalar:
                scalar.copy(out=out, in_=in_)
            elif eng is gpsimd:
                gpsimd.tensor_scalar(out=out, in0=in_, scalar1=1.0, scalar2=0.0, op0=MULT, op1=ADD)
            else:
                vector.tensor_copy(out=out, in_=in_)

        def load(name, src):
            raw = sb.tile(list(src.shape), F32, name=name, align_bytes=BURST)
            nc.sync.dma_start(out=raw[:], in_=src)
            return raw

        x = {}

        def load_wide(step, g):
            x[step, g] = load("x%d_wide%d" % (step, g), by_row((x1, x2)[step][g])[:, :, half(0)])

        def load_packed(step):
            x[step] = load("x%d_packed" % step, by_slot((x1, x2)[step])[:, :, half(1)])

        w_raw, h_raw, a = {}, {}, {}

        def load_w(i):
            w_raw[i] = load("w%d_raw" % (i + 1), by_slot((w1, w2)[i]))

        def load_h(hf):
            h_raw[hf] = load("h_raw%d" % hf, by_slot(h)[:, :, half(hf)])

        def load_a_wide():
            a["wide"] = load("a_wide", a1.rearrange("g (q s) o -> q g (s o)", s=ROWS))

        def load_a_packed():
            a["packed"] = load("a_packed", a1.rearrange("g (p j) o -> (g p) (j o)", j=PACK))

        load_w(0)
        for hf in range(2):
            load_h(hf)
        for g in heads:
            load_wide(0, g)
        load_a_wide()
        load_packed(0)
        load_w(1)
        load_a_packed()

        dealt, wide_codes, wide_scales, packed_codes, packed_scales = [], [], [], [], []
        for i in range(2):
            dealt.append(sb.tile([P, ROWS, P, PACK], BF16, name="dealt%d" % i, align_bytes=64))
            wide_codes.append(sb.tile([P, D], I32, name="wide_codes%d" % i, align_bytes=64))
            wide_scales.append(sb.tile([P, D], U8, name="wide_scales%d" % i, align_bytes=64))
            packed_codes.append(sb.tile([P, 6 * R], I32, name="packed_codes%d" % i, align_bytes=64))
            packed_scales.append(sb.tile([P, 6 * R], U8, name="packed_scales%d" % i, align_bytes=64))
            vector.memset(packed_codes[i][:].rearrange("p (b m) -> p b m", m=R)[:, 0:6:5, :], 0)
            vector.memset(packed_scales[i][:].bitcast(I32).rearrange("p (b m) -> p b m", b=6)[:, 0:6:5, :], 0)
            vector.memset(wide_scales[i][:].bitcast(I32), 0)

        def quantise(codes, scales, packed):
            vector.quantize_mx(out=codes.bitcast(FP8X4), scales=scales, in_=packed)

        def deal(i, eng, first, last):
            if eng is gpsimd:
                copy(
                    eng,
                    dealt[i][:].rearrange("p s q j -> p q j s")[:, 2 * first : 2 * last],
                    w_raw[i][:].rearrange("p j (q s) -> p q j s", s=ROWS)[:, 2 * first : 2 * last],
                )
            else:
                copy(
                    eng,
                    dealt[i][:].rearrange("p s (c i) j -> p c j i s", i=2)[:, first:last],
                    w_raw[i][:].rearrange("p j (c i s) -> p c j i s", i=2, s=ROWS)[:, first:last],
                )

        def quant_w(i):
            quantise(wide_codes[i][:], wide_scales[i][:], dealt[i][:].rearrange("p s q j -> p (s q j)"))

        def regroup(eng, packed, wide):
            copy(
                eng,
                packed.rearrange("p (u s m) -> p s m u", u=2, s=ROWS),
                wide.rearrange("p (s m u) -> p s m u", s=ROWS, u=2),
            )

        def regroup_codes(i, eng=scalar):
            word = U32 if eng is scalar else I32
            regroup(eng, packed_codes[i][:, R : 5 * R].bitcast(word), wide_codes[i][:].bitcast(word))

        def regroup_scales(i):
            regroup(vector, packed_scales[i][:, R : 5 * R], wide_scales[i][:])

        def packed_walk(dst):
            return dst.rearrange("p (c i) j -> p c j i", i=RUN)

        def flat_walk(src):
            return src.rearrange("p j (c i) -> p c j i", i=RUN)

        packed = [
            [sb.tile([P, QUARTER, PACK], BF16, name="packed%d_%d" % (i, k), align_bytes=64) for k in range(4)]
            for i in range(3)
        ]
        moving = {}

        def round_h(k, eng, first=0, last=QUARTER):
            src = h_raw[k // 2][:, :, quarter(k % 2)]
            copy(eng, packed_walk(packed[0][k][:, first:last, :]), flat_walk(src[:, :, first:last]))

        def quant_moving(step, k):
            t = sb.tile([P, QUARTER + PLANE_WORDS], I32, name="moving%d_%d" % (step, k), align_bytes=64)
            quantise(t[:, 0:QUARTER], t[:, QUARTER:].bitcast(U8), packed[step][k][:].rearrange("p n j -> p (n j)"))
            moving[step, k] = t

        z, sums = {}, {}

        def product(step, k, g):
            groups = ROWS if k in WIDE else PACK
            z[step, k, g] = ps.tile(
                [P, groups, QUARTER], F32, name="z%d_%d_%d" % (step, k, g), tag="bank%d_%d" % (g, k)
            )
            t = moving[step, k]
            for j in range(groups):
                if k in WIDE:
                    codes, scales, window = wide_codes, wide_scales, slice(j * P, (j + 1) * P)
                else:
                    codes, scales, window = packed_codes, packed_scales, slice((j + 1 - g) * R, (j + 3 - g) * R)
                nc.tensor.matmul_mx(
                    out=z[step, k, g][:, j, :],
                    lhsT=codes[step][rows[g], window].bitcast(FP8X4),
                    lhsT_scale=scales[step][rows[g], window],
                    rhs=t[rows[g], 0:QUARTER].bitcast(FP8X4),
                    rhs_scale=t[rows[g], QUARTER:].bitcast(U8),
                    start=True,
                    stop=True,
                )

        def add_wide(step, k, g):
            if (step, "wide", g) not in sums:
                sums[step, "wide", g] = sb.tile([P, ROWS, HALF], F32, name="sum%d_wide%d" % (step, g))
            sums[step, k, g] = sums[step, "wide", g][:, :, quarter(k)]
            vector.tensor_tensor(out=sums[step, k, g], in0=z[step, k, g][:], in1=x[step, g][:, :, quarter(k)], op=ADD)

        def add_packed(step, k, g, slots=slice(0, PACK)):
            if (step, k) not in sums:
                sums[step, k] = sb.tile([P, PACK, QUARTER], F32, name="sum%d_%d" % (step, k))
            part = read[g]
            vector.tensor_tensor(
                out=sums[step, k][part, slots, :],
                in0=z[step, k, g][part, slots, :],
                in1=x[step][part, slots, quarter(k - 2)],
                op=ADD,
            )

        emptied = {}

        def empty(step, k, g):
            if (step, k) not in emptied:
                emptied[step, k] = sb.tile([P, PACK, QUARTER], F32, name="emptied%d_%d" % (step, k))
            scalar.copy(out=emptied[step, k][rows[g]], in_=z[step, k, g][rows[g]])

        def add_emptied(step, k, eng=vector):
            sums[step, k] = sb.tile([P, PACK, QUARTER], F32, name="sum%d_%d" % (step, k))
            eng.tensor_tensor(out=sums[step, k][:], in0=emptied[step, k][:], in1=x[step][:, :, quarter(k - 2)], op=ADD)

        pairs = {}
        moved = {
            (step, k): sb.tile([P, 2, QUARTER], I32, name="moved%d_%d" % (step, k), align_bytes=BURST) for step in range(2) for k in WIDE
        }

        def new_pairs(step, k, g):
            pairs[step, k, g] = sb.tile([P, QUARTER, ROWS], BF16, name="pairs%d_%d_%d" % (step, k, g), align_bytes=BURST)
            return packed_walk(pairs[step, k, g][:])

        def move(step, k, g):
            nc.sync.dma_start(
                out=moved[step, k][rows[g]], in_=pairs[step, k, g][:].rearrange("p n s -> p (n s)").bitcast(I32)
            )

        def join(step, k, eng=vector):
            word = U32 if eng is scalar else I32
            copy(
                eng,
                packed[step + 1][k][:].rearrange("p n j -> p (n j)").bitcast(word).rearrange("p (n u) -> p n u", u=2),
                moved[step, k][:].bitcast(word).rearrange("p u n -> p n u"),
            )

        tanh1 = {}

        def act1(*key):
            src = sums[(0,) + key]
            tanh1[key] = sb.tile(list(src.shape), F32, name="tanh1" + "_%d" * len(key) % key)
            scalar.activation(out=tanh1[key][:], in_=src[:], func=TANH)

        def scale(eng, out, src, by):
            factor = by.unsqueeze(1).unsqueeze(3).to_broadcast([P, QUARTER // RUN, by.shape[1], RUN])
            eng.tensor_tensor(out=out, in0=flat_walk(src), in1=factor, op=MULT)

        def scale_wide(k, g, eng):
            scale(eng, new_pairs(0, k, g), tanh1[k, g][:], a["wide"][:, g, :])

        def scale_by_row(k, g):
            new_pairs(0, k, g)
            for s in range(ROWS):
                scalar.mul(out=pairs[0, k, g][:, :, s], in_=tanh1[k, g][:, s, :], mul=a["wide"][:, g, s : s + 1])

        def scale_packed(k, eng=vector):
            scale(eng, packed_walk(packed[1][k][:]), tanh1[k,][:], a["packed"][:])

        def scale_by_slot(k):
            for j in range(PACK):
                scalar.mul(out=tanh1[k,][:, j, :], in_=tanh1[k,][:, j, :], mul=a["packed"][:, j : j + 1])

        def round_h1(k):
            vector.tensor_copy(out=packed_walk(packed[1][k][:]), in_=flat_walk(tanh1[k,][:]))

        y_wide = {g: sb.tile([P, ROWS, HALF], F32, name="y_wide%d" % g, align_bytes=BURST) for g in heads}
        y_packed = sb.tile([P, PACK, HALF], F32, name="y_packed", align_bytes=BURST)
        words = sb.tile([P, N], I32, name="words", align_bytes=BURST)
        y_scales = sb.tile([P, N], U8, name="y_scales", align_bytes=BURST)
        slot_pairs = (slice(0, 2), slice(2, 4))

        def act2_wide(k, g):
            scalar.activation(out=y_wide[g][:, :, quarter(k)], in_=sums[1, k, g][:], func=TANH)

        def act2_head(g):
            scalar.activation(out=y_wide[g][:], in_=sums[1, "wide", g][:], func=TANH)

        def round_pairs(k, g):
            copy(vector, new_pairs(1, k, g), flat_walk(y_wide[g][:, :, quarter(k)]))
            move(1, k, g)

        def send_pairs(k, g):
            scalar.activation(out=new_pairs(1, k, g), in_=flat_walk(sums[1, k, g][:]), func=TANH)
            move(1, k, g)

        def act2_packed(k, slots=slice(0, PACK)):
            scalar.activation(out=y_packed[:, slots, quarter(k - 2)], in_=sums[1, k][:, slots, :], func=TANH)

        def round_y(k, eng=vector):
            copy(eng, packed_walk(packed[2][k][:]), flat_walk(y_packed[:, :, quarter(k - 2)]))

        def quant_y(k):
            quantise(words[:, quarter(k)], y_scales[:, quarter(k)], packed[2][k][:].rearrange("p n j -> p (n j)"))

        def store_wide(g):
            nc.sync.dma_start(out=by_row(out_0[g * D : (g + 1) * D, :])[:, :, half(0)], in_=y_wide[g][:])

        def store_packed(slots):
            dst = out_0.rearrange("(p j) n -> p j n", j=PACK)
            nc.sync.dma_start(out=dst[:, slots, half(1)], in_=y_packed[:, slots, :])

        def store_quarter(k, slots=slice(0, PACK)):
            dst = out_0.rearrange("(p j) n -> p j n", j=PACK)
            nc.sync.dma_start(out=dst[:, slots, quarter(k)], in_=y_packed[:, slots, quarter(k - 2)])

        def store_words(queue, cols):
            queue.dma_start(out=out_1[0].rearrange("p n j -> p (n j)").bitcast(I32)[:, cols], in_=words[:, cols])

        def store_planes(cols=slice(0, N)):
            store_words(scalar, cols)
            scales_view = out_2[0].bitcast(I32)
            for q, queue in enumerate((nc.sync, nc.sync, scalar, nc.sync)):
                queue.dma_start(out=scales_view[4 * q : 4 * q + 4, :], in_=y_scales[32 * q : 32 * q + 4, :].bitcast(I32))

        deal(0, vector, 0, W1_ON_VECTOR)
        deal(0, scalar, W1_ON_VECTOR, R)
        quant_w(0)
        round_h(0, vector, 0, H0_ON_VECTOR)
        round_h(0, scalar, H0_ON_VECTOR, QUARTER)
        round_h(1, scalar)
        quant_moving(0, 0)
        for g in heads:
            product(0, 0, g)
        regroup_scales(0)
        regroup_codes(0)
        quant_moving(0, 1)
        for g in heads:
            product(0, 1, g)
        round_h(2, vector)
        round_h(3, scalar)
        quant_moving(0, 2)
        add_wide(0, 0, upper)
        quant_moving(0, 3)
        for g in heads:
            for k in PACKED:
                product(0, k, g)
        add_wide(0, 0, lower)
        for g in heads:
            add_wide(0, 1, g)
        for k in WIDE:
            for g in heads:
                act1(k, g)
        for g in heads:
            scale_wide(0, g, vector)
        scale_wide(1, upper, gpsimd)
        scale_by_row(1, lower)
        for k in WIDE:
            for g in heads:
                move(0, k, g)
        load_wide(1, upper)
        load_wide(1, lower)
        load_packed(1)

        deal(1, scalar, 0, W2_ON_SCALAR)
        deal(1, gpsimd, W2_ON_SCALAR, R)
        for k in PACKED:
            add_packed(0, k, upper)
        for k in PACKED:
            add_packed(0, k, lower)
            act1(k)
        join(0, 0)
        quant_w(1)
        scale_by_slot(3)
        regroup_codes(1)
        quant_moving(1, 0)
        for g in heads:
            product(1, 0, g)
        scale_packed(2)
        join(0, 1)
        regroup_scales(1)
        quant_moving(1, 1)
        for g in heads:
            product(1, 1, g)
        add_wide(1, 0, upper)
        quant_moving(1, 2)
        product(1, 2, upper)
        round_h1(3)
        add_wide(1, 0, lower)
        quant_moving(1, 3)
        product(1, 3, upper)
        for k in PACKED:
            product(1, k, lower)
        for g in heads:
            add_wide(1, 1, g)
        for k in PACKED:
            add_packed(1, k, upper)
        for k in PACKED:
            for slots in slot_pairs:
                add_packed(1, k, lower, slots)
        send_pairs(0, upper)
        act2_wide(0, upper)
        send_pairs(0, lower)
        for g in heads:
            send_pairs(1, g)
        act2_wide(1, upper)
        store_wide(upper)
        act2_head(lower)
        store_wide(lower)
        for k in PACKED:
            for slots in slot_pairs:
                act2_packed(k, slots)
                if k == PACKED[-1]:
                    store_packed(slots)
        join(1, 0)
        round_y(2)
        quant_y(0)
        join(1, 1)
        round_y(3)
        for k in (2, 1, 3):
            quant_y(k)
        store_planes()
